import numpy as np
import ml_dtypes


def mxq(x, axis, fmt="e4m3"):
    dtype, down = {"e4m3": (ml_dtypes.float8_e4m3fn, 7), "e5m2": (ml_dtypes.float8_e5m2, 14)}[fmt]
    v = np.moveaxis(np.asarray(x, np.float32).astype(ml_dtypes.bfloat16).astype(np.float64), axis, -1)
    blocks = v.reshape(v.shape[:-1] + (-1, 32))
    amax = np.abs(blocks).max(-1, keepdims=True)
    byte = np.maximum(np.where(amax > 0, np.frexp(amax)[1] - 1 + 127, 0) - down, 1)
    scale = np.exp2(byte - 127.0)
    codes = (blocks / scale).astype(np.float32).astype(dtype).astype(np.float64)
    return np.moveaxis((codes * scale).reshape(v.shape), -1, axis)


WIDE = False


def mx_kscale(k):
    if not WIDE:
        return np.ones(k)
    levels = np.array([10, -10, 5, -5, 0])
    if k % 512:
        return np.exp2(np.random.permutation(np.resize(levels, k // 32))).repeat(32)
    a = np.empty((k // 512, 16))
    for p in range(k // 512):
        a[p, :8] = np.random.permutation(np.resize(levels, 8))
        for g in range(8):
            far = levels[np.abs(levels - a[p, g]) >= 10]
            a[p, g + 8] = far[np.random.randint(len(far))]
    return np.exp2(a.ravel()).repeat(32)


def f64(x):
    return np.asarray(x).astype(np.float64)


def striped(idx):
    return np.tile(idx.reshape(-1, 16).T, (8, 1)).astype(np.uint16)


def unstriped(offs):
    return offs[:16].T.reshape(-1).astype(np.int64)


E2M1 = np.array([0.0, 0.5, 1.0, 1.5, 2.0, 3.0, 4.0, 6.0, -0.0, -0.5, -1.0, -1.5, -2.0, -3.0, -4.0, -6.0])


def pack_weight(w, fmt):
    k, n = w.shape
    w = f64(np.asarray(w, np.float32).astype(ml_dtypes.bfloat16)).reshape(k // 32, 32, n)
    amax = np.abs(w).max(1)
    if fmt == "e4m3":
        byte = np.frexp(amax)[1] - 1 + 127 - 7
    else:
        mant, ex = np.frexp(amax / 6.0)
        byte = np.where(mant > 0.5, ex, ex - 1) + 127
    byte = np.clip(np.where(amax > 0, byte, 1), 1, 254)
    scaled = (w * np.exp2(127.0 - byte)[:, None, :]).reshape(k, n).astype(np.float32)
    by_word = np.ascontiguousarray(scaled.reshape(k // 512, 128, 4, n).transpose(0, 1, 3, 2))
    if fmt == "e4m3":
        words = by_word.astype(ml_dtypes.float8_e4m3fn).view(np.uint8)
    else:
        c = by_word.astype(ml_dtypes.float4_e2m1fn).view(np.uint8) & 0xF
        words = (c[..., 0::2] | (c[..., 1::2] << 4)).reshape(k // 512, 128, 2 * n)
    return np.ascontiguousarray(words), np.ascontiguousarray(byte.astype(np.uint8).reshape(k // 512, 16, n))


def unpack_weight(words, scales, fmt):
    g, _, n = scales.shape
    words = np.ascontiguousarray(words).reshape(g, 128, n, -1)
    if fmt == "e4m3":
        vals = words.view(ml_dtypes.float8_e4m3fn).astype(np.float64)
    else:
        nib = np.empty((g, 128, n, 4), np.uint8)
        nib[..., 0::2] = words & 0xF
        nib[..., 1::2] = words >> 4
        vals = E2M1[nib]
    vals = vals * np.repeat(np.exp2(scales.astype(np.float64) - 127.0), 8, axis=1)[..., None]
    return vals.transpose(0, 1, 3, 2).reshape(g * 512, n)


def gelu(v):
    return 0.5 * v * (1.0 + np.tanh(np.sqrt(2.0 / np.pi) * (v + 0.044715 * v**3)))


def often(T, S):
    return np.random.permutation(T)[(T * np.random.uniform(0, 1, S) ** 4).astype(np.int64)]


def bf(x):
    return np.asarray(x, np.float32).astype(ml_dtypes.bfloat16)


def planes(Y):
    n, m = Y.shape
    b = f64(bf(Y)).reshape(n // 32, 32, m)
    amax = np.abs(b).max(1)
    byte = np.clip(np.where(amax > 0, np.frexp(amax)[1] - 1 + 127 - 7, 1), 1, 254)
    codes = (b * np.exp2(127.0 - byte)[:, None, :]).reshape(n, m).astype(np.float32).astype(ml_dtypes.float8_e4m3fn).view(np.uint8)
    words = codes.reshape(n // 512, 128, 4, m).transpose(0, 1, 3, 2)
    return np.ascontiguousarray(words), np.ascontiguousarray(byte.astype(np.uint8).reshape(n // 512, 16, m))


K, H, N, T, S, T2, P = 512, 1536, 1024, 2048, 1024, 2048, 512

def setup_inputs():
    n = np.random.standard_normal
    s = mx_kscale(K)[:, None]
    u = mx_kscale(H)[:, None]
    tab_words, tab_scales = pack_weight(n((K, T)) * s, "e4m3")
    tab2_words, tab2_scales = pack_weight(n((K, T2)) * s, "e4m3")
    w1_words, w1_scales = pack_weight(n((K, H)) / np.sqrt(K) / s * u.T, "e2m1")
    wu_words, wu_scales = pack_weight(n((H, N)) / np.sqrt(H) / u, "e4m3")
    return {
        "tab_words": tab_words, "tab_scales": tab_scales,
        "offs": striped(np.random.permutation(T)[:S]),
        "pos1": striped(often(S, P)),
        "tab2_words": tab2_words, "tab2_scales": tab2_scales,
        "offs2": striped(np.random.permutation(T2)[:P]),
        "w1_words": w1_words, "w1_scales": w1_scales,
        "w2": (n((K, H)) / np.sqrt(K) / s * u.T).astype(np.float32),
        "wo": (n((H, N)) / np.sqrt(H) / u).astype(np.float32),
        "wu_words": wu_words, "wu_scales": wu_scales,
        "gain": np.exp(0.8 * n(N)).astype(np.float32),
    }

def reference(tab_words, tab_scales, offs, pos1, tab2_words, tab2_scales, offs2, w1_words, w1_scales, w2, wo, wu_words, wu_scales, gain):
    v = unpack_weight(tab_words, tab_scales, "e4m3")[:, unstriped(offs)]
    v2 = unpack_weight(tab2_words, tab2_scales, "e4m3")[:, unstriped(offs2)]
    w1 = unpack_weight(w1_words, w1_scales, "e2m1")
    wu = unpack_weight(wu_words, wu_scales, "e4m3")
    h = w1.T @ v
    a = h[:, unstriped(pos1)]
    b = mxq(f64(w2), 0, "e4m3").T @ v2
    above = np.maximum(b - a, 0.0)
    below = np.maximum(a - b, 0.0)
    over = mxq(f64(wo), 0, "e4m3").T @ mxq(above, 0, "e4m3")
    under = wu.T @ mxq(below, 0, "e4m3")
    y = f64(gain)[:, None] * (over - under)
    words, scales = planes(y)
    return y, words, scales

@@ -1,0 +1,293 @@
+from contextlib import ExitStack
+
+import concourse.mybir as mybir
+
+K, H, N, T, S, M = 512, 1536, 1024, 2048, 1024, 512
+FLOPS = 2 * K * H * S + 2 * K * H * M + 4 * H * N * M
+
+F32 = mybir.dt.float32
+BF16 = mybir.dt.bfloat16
+I32 = mybir.dt.int32
+U32 = mybir.dt.uint32
+U16 = mybir.dt.uint16
+U8 = mybir.dt.uint8
+FP8X4 = mybir.dt.float8_e4m3fn_x4
+FP4X4 = mybir.dt.float4_e2m1fn_x4
+COPY = mybir.ActivationFunctionType.Copy
+SUBTRACT = mybir.AluOpType.subtract
+
+P = 128
+PACK = 4
+PASS = P * PACK
+BANK = 512
+R_PASSES = H // PASS
+N_GROUPS = N // PASS
+HALF = M // 2
+CHUNK = BANK // PACK
+
+
+def tile_list_net_misstatement_scores_kernel(
+    tc, tab_words, tab_scales, offs, pos1, tab2_words, tab2_scales, offs2,
+    w1_words, w1_scales, w2, wo, wu_words, wu_scales, gain, out_0, out_1, out_2,
+):
+    nc = tc.nc
+    with ExitStack() as ctx:
+        keep = ctx.enter_context(tc.tile_pool(name="keep", bufs=1))
+        ring = ctx.enter_context(tc.tile_pool(name="ring", bufs=2))
+        psum = ctx.enter_context(tc.psum_pool(name="psum", bufs=1))
+
+        def kept(name, shape, dtype):
+            return keep.tile(shape, dtype, name=name, align_bytes=64)
+
+        landed = []
+
+        def landing(name, shape, dtype):
+            landed.append(name)
+            return ring.tile(shape, dtype, name=name, tag="landing%d" % (len(landed) % 5), bufs=1, align_bytes=64)
+
+        def load_words(tile, words):
+            nc.sync.dma_start(out=tile[:], in_=words.rearrange("p c i -> p (c i)").bitcast(I32))
+
+        def load_plane(queues, plane, rows):
+            for q in range(4):
+                queues[q].dma_start(
+                    out=plane[32 * q : 32 * q + 4, :].bitcast(I32),
+                    in_=rows[4 * q : 4 * q + 4, :].bitcast(I32),
+                )
+
+        idx = kept("idx", [P, S // 16], U16)
+        idx2 = kept("idx2", [P, M // 16], U16)
+        pick = kept("pick", [P, M // 16], U16)
+        w1_raw = landing("w1_raw", [P, 2 * H], U8)
+        w1_raw_plane = landing("w1_raw_plane", [P, H], U8)
+        tab = landing("tab", [P, T], I32)
+        tab_plane = landing("tab_plane", [P, T], U8)
+        tab2_plane = landing("tab2_plane", [P, T], U8)
+        gains = kept("gains", [P, N_GROUPS, PACK], F32)
+
+        nc.vector.memset(tab_plane[:].bitcast(I32), 0)
+        nc.vector.memset(w1_raw_plane[:].bitcast(I32), 0)
+        nc.vector.memset(tab2_plane[:].bitcast(I32), 0)
+
+        nc.sync.dma_start(idx[:], offs)
+        nc.sync.dma_start(idx2[:], offs2)
+        nc.sync.dma_start(pick[:], pos1)
+        nc.sync.dma_start(out=gains[:], in_=gain.rearrange("(g p t) -> p g t", p=P, t=PACK))
+        load_plane([nc.scalar] * 4, tab_plane, tab_scales[0])
+        nc.sync.dma_start(out=w1_raw[:].bitcast(I32), in_=w1_words[0].bitcast(I32))
+        load_words(tab, tab_words[0])
+        load_plane([nc.scalar] * 3 + [nc.gpsimd], w1_raw_plane, w1_scales[0])
+
+        def load_weight(w, g, cols):
+            raw = landing("raw", [P, PACK, PASS], F32)
+            nc.sync.dma_start(
+                out=raw[:], in_=w[g * PASS : (g + 1) * PASS, cols].rearrange("(p j) c -> p j c", j=PACK)
+            )
+            return raw
+
+        def quantise_weight(raw, name):
+            staged = ring.tile([P, PASS * PACK], BF16, name="staged", bufs=3, align_bytes=64)
+            nc.scalar.copy(
+                out=staged[:].rearrange("p (t m j) -> p m j t", t=PACK, j=PACK),
+                in_=raw[:].rearrange("p j (m t) -> p m j t", t=PACK),
+            )
+            codes = kept(name + "_codes", [P, PASS], U32)
+            plane = kept(name + "_plane", [P, PASS], U8)
+            nc.vector.quantize_mx(out=codes[:].bitcast(FP8X4), scales=plane[:], in_=staged[:])
+            return codes, plane
+
+        tab2 = landing("tab2", [P, T], I32)
+        load_words(tab2, tab2_words[0])
+        w2_raw = load_weight(w2, 0, slice(0, PASS))
+        load_plane([nc.scalar] * 4, tab2_plane, tab2_scales[0])
+
+        w1_codes = []
+        w1_planes = []
+        for g in range(R_PASSES):
+            codes = kept("w1_codes%d" % g, [P, 2 * PASS], U8)
+            nc.vector.tensor_copy(
+                out=codes[:].bitcast(U16).rearrange("p (t m) -> p t m", t=PACK),
+                in_=w1_raw[:, 2 * PASS * g : 2 * PASS * (g + 1)].bitcast(U16).rearrange("p (m t) -> p t m", t=PACK),
+            )
+            w1_codes.append(codes)
+        w1_plane = kept("w1_plane", [P, H], U8)
+
+        def gather_table(name, words, plane, offsets):
+            width = 16 * offsets.shape[1]
+            codes = kept(name + "_codes", [P, width], U32)
+            scales = kept(name + "_plane", [P, width], U8)
+            nc.vector.tensor_copy(out=scales[:], in_=plane[:].indirect(offsets))
+            nc.vector.tensor_copy(out=codes[:], in_=words[:].bitcast(U32).indirect(offsets))
+            return codes, scales
+
+        v = [gather_table("v0", tab, tab_plane, idx[:, 0 : BANK // 16])]
+        nc.vector.tensor_copy(
+            out=w1_plane[:].rearrange("p (g t m) -> p g t m", t=PACK, m=P),
+            in_=w1_raw_plane[:].rearrange("p (g m t) -> p g t m", t=PACK, m=P),
+        )
+        v.append(gather_table("v1", tab, tab_plane, idx[:, BANK // 16 : 2 * BANK // 16]))
+        v2_codes, v2_plane = gather_table("v2", tab2, tab2_plane, idx2[:])
+
+        def first_stage(g):
+            rows = [ring.tile([P, S], F32, name="h", bufs=8) for t in range(PACK)]
+            for s in range(S // BANK):
+                for t in range(PACK):
+                    bank = psum.tile([P, BANK], F32, name="h_bank", tag="bank%d" % (t % 2))
+                    nc.tensor.matmul_mx(
+                        out=bank[:],
+                        lhsT=w1_codes[g][:, 2 * P * t : 2 * P * (t + 1)].bitcast(FP4X4),
+                        lhsT_scale=w1_plane[:, g * PASS + P * t : g * PASS + P * (t + 1)],
+                        rhs=v[s][0][:].bitcast(FP8X4),
+                        rhs_scale=v[s][1][:],
+                        start=True,
+                        stop=True,
+                    )
+                    nc.scalar.copy(out=rows[t][:, s * BANK : (s + 1) * BANK], in_=bank[:])
+            return rows
+
+        def differences(g, first, width, h_rows, w2_q):
+            picked = ring.tile([P, PACK, width], F32, name="picked", bufs=2)
+            offsets = pick[:, first // 16 : (first + width) // 16]
+            for t in range(PACK):
+                nc.vector.tensor_copy(out=picked[:, t, :], in_=h_rows[t][:].indirect(offsets))
+            diff = ring.tile([P, width * PACK], BF16, name="diff", bufs=2, align_bytes=64)
+            for c in range(width // CHUNK):
+                cols = slice(first + c * CHUNK, first + (c + 1) * CHUNK)
+                bank = psum.tile([P, PACK, CHUNK], F32, name="b_bank", tag="bank%d" % (2 + c % 2))
+                for t in range(PACK):
+                    nc.tensor.matmul_mx(
+                        out=bank[:, t, :],
+                        lhsT=w2_q[0][:, P * t : P * (t + 1)].bitcast(FP8X4),
+                        lhsT_scale=w2_q[1][:, P * t : P * (t + 1)],
+                        rhs=v2_codes[:, cols].bitcast(FP8X4),
+                        rhs_scale=v2_plane[:, cols],
+                        start=True,
+                        stop=True,
+                    )
+                nc.vector.tensor_tensor(
+                    out=diff[:, c * BANK : (c + 1) * BANK].rearrange("p (c i t) -> p c t i", i=2, t=PACK),
+                    in0=bank[:].rearrange("p t (c i) -> p c t i", i=2),
+                    in1=picked[:, :, c * CHUNK : (c + 1) * CHUNK].rearrange("p t (c i) -> p c t i", i=2),
+                    op=SUBTRACT,
+                )
+            signed = ring.tile([P, 2 * width * PACK], BF16, name="signed", bufs=2, align_bytes=64)
+            nc.vector.tensor_scalar_max(out=signed[:, 0 : width * PACK], in0=diff[:], scalar1=0.0)
+            nc.vector.tensor_scalar_min(out=signed[:, width * PACK : 2 * width * PACK], in0=diff[:], scalar1=0.0)
+            codes = kept("d_codes%d_%d" % (g, first), [P, 2 * width], U32)
+            plane = kept("d_plane%d_%d" % (g, first), [P, 2 * width], U8)
+            nc.vector.quantize_mx(out=codes[:].bitcast(FP8X4), scales=plane[:], in_=signed[:])
+            return [
+                (codes, plane, slice(c, c + HALF), slice(width + c, width + c + HALF)) for c in range(0, width, HALF)
+            ]
+
+        def deal_wu(g):
+            raw = landing("wu_raw", [P, N], I32)
+            load_words(raw, wu_words[g])
+            codes = kept("wu_codes%d" % g, [P, N], I32)
+            nc.vector.tensor_copy(
+                out=codes[:].rearrange("p (n t m) -> p n m t", t=PACK, m=P),
+                in_=raw[:].rearrange("p (n m t) -> p n m t", t=PACK, m=P),
+            )
+            return codes
+
+        def second_stage(g, banks, d_q, wo_q, wu_codes, wu_planes, which):
+            for b in which:
+                n, pair = divmod(b, 2)
+                for u in range(2):
+                    t = 2 * pair + u
+                    nc.tensor.matmul_mx(
+                        out=banks[b][:, u, :],
+                        lhsT=wo_q[n][0][:, P * t : P * (t + 1)].bitcast(FP8X4),
+                        lhsT_scale=wo_q[n][1][:, P * t : P * (t + 1)],
+                        rhs=d_q[0][:, d_q[2]].bitcast(FP8X4),
+                        rhs_scale=d_q[1][:, d_q[2]],
+                        start=(g == 0 and u == 0),
+                        stop=False,
+                    )
+                    cols = slice(n * PASS + P * t, n * PASS + P * (t + 1))
+                    nc.tensor.matmul_mx(
+                        out=banks[b][:, u, :],
+                        lhsT=wu_codes[:, cols].bitcast(FP8X4),
+                        lhsT_scale=wu_planes[4 * g : P, cols],
+                        rhs=d_q[0][:, d_q[3]].bitcast(FP8X4),
+                        rhs_scale=d_q[1][:, d_q[3]],
+                        start=False,
+                        stop=(g == R_PASSES - 1 and u == 1),
+                    )
+
+        y_codes = kept("y_codes", [P, N_GROUPS, M], U32)
+        y_plane = kept("y_plane", [P, N_GROUPS, M], U8)
+
+        def finish(n, half, banks):
+            cols = slice(half * HALF, (half + 1) * HALF)
+            y = ring.tile([P, PACK, HALF], F32, name="y", bufs=4)
+            for t in range(PACK):
+                nc.scalar.activation(
+                    out=y[:, t, :], in_=banks[2 * n + t // 2][:, t % 2, :], func=COPY, scale=gains[:, n, t : t + 1]
+                )
+            nc.sync.dma_start(
+                out=out_0[n * PASS : (n + 1) * PASS, cols].rearrange("(p t) m -> p t m", t=PACK), in_=y[:]
+            )
+            rounded = ring.tile([P, HALF * PACK], BF16, name="rounded", bufs=2, align_bytes=64)
+            round_off = nc.scalar.copy if half == 0 else nc.vector.tensor_copy
+            round_off(
+                out=rounded[:].rearrange("p (c i t) -> p c t i", i=4, t=PACK),
+                in_=y[:].rearrange("p t (c i) -> p c t i", i=4),
+            )
+            nc.vector.quantize_mx(out=y_codes[:, n, cols].bitcast(FP8X4), scales=y_plane[:, n, cols], in_=rounded[:])
+            nc.sync.dma_start(
+                out=out_1[n].rearrange("p m t -> p (m t)").bitcast(I32)[:, cols],
+                in_=y_codes[:, n, cols].bitcast(I32),
+            )
+
+        h = [first_stage(0)]
+        w2_q = [quantise_weight(w2_raw, "w2_0")]
+        last = R_PASSES - 1
+        wo_q, wu_codes, d_q = [], [], []
+        wu_planes = kept("wu_planes", [P, N], U8)
+        banks0 = None
+        for g in range(R_PASSES):
+            if g + 1 < R_PASSES:
+                raw = load_weight(w2, 0, slice((g + 1) * PASS, (g + 2) * PASS))
+                w2_q.append(quantise_weight(raw, "w2_%d" % (g + 1)))
+                h.append(first_stage(g + 1))
+            d_q.append(differences(g, 0, HALF if g == last else M, h[g], w2_q[g]))
+            wo_q.append(
+                [
+                    quantise_weight(load_weight(wo, g, slice(n * PASS, (n + 1) * PASS)), "wo_%d%d" % (g, n))
+                    for n in range(N_GROUPS)
+                ]
+            )
+            if g == 0:
+                wu_raw_planes = landing("wu_raw_planes", [P, N], U8)
+                nc.vector.memset(wu_raw_planes[:].bitcast(I32), 0)
+                for q in range(4):
+                    nc.sync.dma_start(
+                        out=wu_raw_planes[32 * q : 32 * q + 4 * R_PASSES, :].bitcast(I32),
+                        in_=wu_scales[:, 4 * q : 4 * q + 4, :].bitcast(I32),
+                    )
+                nc.vector.tensor_copy(
+                    out=wu_planes[:].rearrange("p (n t m) -> p n t m", t=PACK, m=P),
+                    in_=wu_raw_planes[:].rearrange("p (n m t) -> p n t m", t=PACK, m=P),
+                )
+                banks0 = [psum.tile([P, 2, HALF], F32, name="y_bank", tag="bank%d" % (4 + b)) for b in range(4)]
+            wu_codes.append(deal_wu(g))
+            second_stage(g, banks0, d_q[g][0], wo_q[g], wu_codes[g], wu_planes, range(4))
+
+        d_q[last].extend(differences(last, HALF, HALF, h[last], w2_q[last]))
+        banks1 = [psum.tile([P, 2, HALF], F32, name="y_bank", tag="bank%d" % b) for b in (0, 1)]
+        for g in range(last):
+            second_stage(g, banks1, d_q[g][1], wo_q[g], wu_codes[g], wu_planes, range(2))
+        finish(0, 0, banks0)
+        banks1.extend(psum.tile([P, 2, HALF], F32, name="y_bank", tag="bank%d" % b) for b in (4, 5))
+        for g in range(last):
+            second_stage(g, banks1, d_q[g][1], wo_q[g], wu_codes[g], wu_planes, range(2, 4))
+        finish(1, 0, banks0)
+        second_stage(last, banks1, d_q[last][1], wo_q[last], wu_codes[last], wu_planes, range(4))
+        finish(0, 1, banks1)
+        finish(1, 1, banks1)
+        for q in range(4):
+            nc.sync.dma_start(
+                out=out_2[:, 4 * q : 4 * q + 4, :].rearrange("g r m -> r g m").bitcast(I32),
+                in_=y_plane[32 * q : 32 * q + 4, :, :].bitcast(I32),
+            )

@@ -39,11 +39,8 @@ def tile_list_net_misstatement_scores_kernel(
         def kept(name, shape, dtype):
             return keep.tile(shape, dtype, name=name, align_bytes=64)
 
-        landed = []
-
-        def landing(name, shape, dtype):
-            landed.append(name)
-            return ring.tile(shape, dtype, name=name, tag="landing%d" % (len(landed) % 5), bufs=1, align_bytes=64)
+        def landing(slot, name, shape, dtype):
+            return ring.tile(shape, dtype, name=name, tag="landing%d" % slot, bufs=1, align_bytes=64)
 
         def load_words(tile, words):
             nc.sync.dma_start(out=tile[:], in_=words.rearrange("p c i -> p (c i)").bitcast(I32))
@@ -58,12 +55,11 @@ def tile_list_net_misstatement_scores_kernel(
         idx = kept("idx", [P, S // 16], U16)
         idx2 = kept("idx2", [P, M // 16], U16)
         pick = kept("pick", [P, M // 16], U16)
-        w1_raw = landing("w1_raw", [P, 2 * H], U8)
-        w1_raw_plane = landing("w1_raw_plane", [P, H], U8)
-        tab = landing("tab", [P, T], I32)
-        tab_plane = landing("tab_plane", [P, T], U8)
-        tab2_plane = landing("tab2_plane", [P, T], U8)
-        gains = kept("gains", [P, N_GROUPS, PACK], F32)
+        w1_raw = landing(0, "w1_raw", [P, 2 * H], U8)
+        w1_raw_plane = landing(5, "w1_raw_plane", [P, H], U8)
+        tab = landing(1, "tab", [P, T], I32)
+        tab_plane = landing(2, "tab_plane", [P, T], U8)
+        tab2_plane = landing(3, "tab2_plane", [P, T], U8)
 
         nc.vector.memset(tab_plane[:].bitcast(I32), 0)
         nc.vector.memset(w1_raw_plane[:].bitcast(I32), 0)
@@ -72,14 +68,13 @@ def tile_list_net_misstatement_scores_kernel(
         nc.sync.dma_start(idx[:], offs)
         nc.sync.dma_start(idx2[:], offs2)
         nc.sync.dma_start(pick[:], pos1)
-        nc.sync.dma_start(out=gains[:], in_=gain.rearrange("(g p t) -> p g t", p=P, t=PACK))
         load_plane([nc.scalar] * 4, tab_plane, tab_scales[0])
         nc.sync.dma_start(out=w1_raw[:].bitcast(I32), in_=w1_words[0].bitcast(I32))
         load_words(tab, tab_words[0])
-        load_plane([nc.scalar] * 3 + [nc.gpsimd], w1_raw_plane, w1_scales[0])
+        load_plane([nc.scalar] * 4, w1_raw_plane, w1_scales[0])
 
-        def load_weight(w, g, cols):
-            raw = landing("raw", [P, PACK, PASS], F32)
+        def load_weight(slot, w, g, cols):
+            raw = landing(slot, "raw", [P, PACK, PASS], F32)
             nc.sync.dma_start(
                 out=raw[:], in_=w[g * PASS : (g + 1) * PASS, cols].rearrange("(p j) c -> p j c", j=PACK)
             )
@@ -96,43 +91,45 @@ def tile_list_net_misstatement_scores_kernel(
             nc.vector.quantize_mx(out=codes[:].bitcast(FP8X4), scales=plane[:], in_=staged[:])
             return codes, plane
 
-        tab2 = landing("tab2", [P, T], I32)
+        tab2 = landing(0, "tab2", [P, T], I32)
         load_words(tab2, tab2_words[0])
-        w2_raw = load_weight(w2, 0, slice(0, PASS))
+        w2_raw = load_weight(1, w2, 0, slice(0, PASS))
         load_plane([nc.scalar] * 4, tab2_plane, tab2_scales[0])
 
         w1_codes = []
         w1_planes = []
         for g in range(R_PASSES):
-            codes = kept("w1_codes%d" % g, [P, 2 * PASS], U8)
+            codes = landing((4, 6, 7)[g], "w1_codes%d" % g, [P, 2 * PASS], U8)
             nc.vector.tensor_copy(
                 out=codes[:].bitcast(U16).rearrange("p (t m) -> p t m", t=PACK),
                 in_=w1_raw[:, 2 * PASS * g : 2 * PASS * (g + 1)].bitcast(U16).rearrange("p (m t) -> p t m", t=PACK),
             )
             w1_codes.append(codes)
         w1_plane = kept("w1_plane", [P, H], U8)
+        gains = landing(7, "gains", [P, N_GROUPS, PACK], F32)
+        nc.sync.dma_start(out=gains[:], in_=gain.rearrange("(g p t) -> p g t", p=P, t=PACK))
 
-        def gather_table(name, words, plane, offsets):
+        def gather_table(name, words, plane, offsets, slot):
             width = 16 * offsets.shape[1]
             codes = kept(name + "_codes", [P, width], U32)
-            scales = kept(name + "_plane", [P, width], U8)
+            scales = landing(slot, name + "_plane", [P, width], U8)
             nc.vector.tensor_copy(out=scales[:], in_=plane[:].indirect(offsets))
             nc.vector.tensor_copy(out=codes[:], in_=words[:].bitcast(U32).indirect(offsets))
             return codes, scales
 
-        v = [gather_table("v0", tab, tab_plane, idx[:, 0 : BANK // 16])]
+        v = [gather_table("v0", tab, tab_plane, idx[:, 0 : BANK // 16], 8)]
         nc.vector.tensor_copy(
             out=w1_plane[:].rearrange("p (g t m) -> p g t m", t=PACK, m=P),
             in_=w1_raw_plane[:].rearrange("p (g m t) -> p g t m", t=PACK, m=P),
         )
-        v.append(gather_table("v1", tab, tab_plane, idx[:, BANK // 16 : 2 * BANK // 16]))
-        v2_codes, v2_plane = gather_table("v2", tab2, tab2_plane, idx2[:])
+        v.append(gather_table("v1", tab, tab_plane, idx[:, BANK // 16 : 2 * BANK // 16], 5))
+        v2_codes, v2_plane = gather_table("v2", tab2, tab2_plane, idx2[:], 9)
 
-        def first_stage(g):
+        def first_stage(g, n_banks):
             rows = [ring.tile([P, S], F32, name="h", bufs=8) for t in range(PACK)]
             for s in range(S // BANK):
                 for t in range(PACK):
-                    bank = psum.tile([P, BANK], F32, name="h_bank", tag="bank%d" % (t % 2))
+                    bank = psum.tile([P, BANK], F32, name="h_bank", tag="bank%d" % (t % n_banks))
                     nc.tensor.matmul_mx(
                         out=bank[:],
                         lhsT=w1_codes[g][:, 2 * P * t : 2 * P * (t + 1)].bitcast(FP4X4),
@@ -145,15 +142,19 @@ def tile_list_net_misstatement_scores_kernel(
                     nc.scalar.copy(out=rows[t][:, s * BANK : (s + 1) * BANK], in_=bank[:])
             return rows
 
-        def differences(g, first, width, h_rows, w2_q):
-            picked = ring.tile([P, PACK, width], F32, name="picked", bufs=2)
-            offsets = pick[:, first // 16 : (first + width) // 16]
-            for t in range(PACK):
+        def pick_rows(h_rows, half, ts, picked=None):
+            if picked is None:
+                picked = ring.tile([P, PACK, HALF], F32, name="picked", bufs=4)
+            offsets = pick[:, half * HALF // 16 : (half + 1) * HALF // 16]
+            for t in ts:
                 nc.vector.tensor_copy(out=picked[:, t, :], in_=h_rows[t][:].indirect(offsets))
-            diff = ring.tile([P, width * PACK], BF16, name="diff", bufs=2, align_bytes=64)
-            for c in range(width // CHUNK):
-                cols = slice(first + c * CHUNK, first + (c + 1) * CHUNK)
-                bank = psum.tile([P, PACK, CHUNK], F32, name="b_bank", tag="bank%d" % (2 + c % 2))
+            return picked
+
+        def ledger_features(w2_q, half, tags):
+            banks = []
+            for c in range(HALF // CHUNK):
+                cols = slice(half * HALF + c * CHUNK, half * HALF + (c + 1) * CHUNK)
+                bank = psum.tile([P, PACK, CHUNK], F32, name="b_bank", tag="bank%d" % tags[c])
                 for t in range(PACK):
                     nc.tensor.matmul_mx(
                         out=bank[:, t, :],
@@ -164,24 +165,34 @@ def tile_list_net_misstatement_scores_kernel(
                         start=True,
                         stop=True,
                     )
+                banks.append(bank)
+            return banks
+
+        def subtract(banks, picked):
+            diff = ring.tile([P, HALF * PACK], BF16, name="diff", bufs=3, align_bytes=64)
+            for c, bank in enumerate(banks):
                 nc.vector.tensor_tensor(
                     out=diff[:, c * BANK : (c + 1) * BANK].rearrange("p (c i t) -> p c t i", i=2, t=PACK),
                     in0=bank[:].rearrange("p t (c i) -> p c t i", i=2),
                     in1=picked[:, :, c * CHUNK : (c + 1) * CHUNK].rearrange("p t (c i) -> p c t i", i=2),
                     op=SUBTRACT,
                 )
-            signed = ring.tile([P, 2 * width * PACK], BF16, name="signed", bufs=2, align_bytes=64)
-            nc.vector.tensor_scalar_max(out=signed[:, 0 : width * PACK], in0=diff[:], scalar1=0.0)
-            nc.vector.tensor_scalar_min(out=signed[:, width * PACK : 2 * width * PACK], in0=diff[:], scalar1=0.0)
-            codes = kept("d_codes%d_%d" % (g, first), [P, 2 * width], U32)
-            plane = kept("d_plane%d_%d" % (g, first), [P, 2 * width], U8)
+            return diff
+
+        def split_signs(diff):
+            signed = ring.tile([P, 2 * HALF * PACK], BF16, name="signed", bufs=3, align_bytes=64)
+            nc.vector.tensor_scalar_max(out=signed[:, 0 : HALF * PACK], in0=diff[:], scalar1=0.0)
+            nc.vector.tensor_scalar_min(out=signed[:, HALF * PACK : 2 * HALF * PACK], in0=diff[:], scalar1=0.0)
+            return signed
+
+        def quantise_signed(g, half, signed):
+            codes = kept("d_codes%d%d" % (g, half), [P, 2 * HALF], U32)
+            plane = kept("d_plane%d%d" % (g, half), [P, 2 * HALF], U8)
             nc.vector.quantize_mx(out=codes[:].bitcast(FP8X4), scales=plane[:], in_=signed[:])
-            return [
-                (codes, plane, slice(c, c + HALF), slice(width + c, width + c + HALF)) for c in range(0, width, HALF)
-            ]
+            return codes, plane
 
         def deal_wu(g):
-            raw = landing("wu_raw", [P, N], I32)
+            raw = landing(2, "wu_raw", [P, N], I32)
             load_words(raw, wu_words[g])
             codes = kept("wu_codes%d" % g, [P, N], I32)
             nc.vector.tensor_copy(
@@ -199,8 +210,8 @@ def tile_list_net_misstatement_scores_kernel(
                         out=banks[b][:, u, :],
                         lhsT=wo_q[n][0][:, P * t : P * (t + 1)].bitcast(FP8X4),
                         lhsT_scale=wo_q[n][1][:, P * t : P * (t + 1)],
-                        rhs=d_q[0][:, d_q[2]].bitcast(FP8X4),
-                        rhs_scale=d_q[1][:, d_q[2]],
+                        rhs=d_q[0][:, 0:HALF].bitcast(FP8X4),
+                        rhs_scale=d_q[1][:, 0:HALF],
                         start=(g == 0 and u == 0),
                         stop=False,
                     )
@@ -209,8 +220,8 @@ def tile_list_net_misstatement_scores_kernel(
                         out=banks[b][:, u, :],
                         lhsT=wu_codes[:, cols].bitcast(FP8X4),
                         lhsT_scale=wu_planes[4 * g : P, cols],
-                        rhs=d_q[0][:, d_q[3]].bitcast(FP8X4),
-                        rhs_scale=d_q[1][:, d_q[3]],
+                        rhs=d_q[0][:, HALF : 2 * HALF].bitcast(FP8X4),
+                        rhs_scale=d_q[1][:, HALF : 2 * HALF],
                         start=False,
                         stop=(g == R_PASSES - 1 and u == 1),
                     )
@@ -240,26 +251,44 @@ def tile_list_net_misstatement_scores_kernel(
                 in_=y_codes[:, n, cols].bitcast(I32),
             )
 
-        h = [first_stage(0)]
+        h = [first_stage(0, 4)]
         w2_q = [quantise_weight(w2_raw, "w2_0")]
         last = R_PASSES - 1
         wo_q, wu_codes, d_q = [], [], []
         wu_planes = kept("wu_planes", [P, N], U8)
-        banks0 = None
-        for g in range(R_PASSES):
-            if g + 1 < R_PASSES:
-                raw = load_weight(w2, 0, slice((g + 1) * PASS, (g + 2) * PASS))
-                w2_q.append(quantise_weight(raw, "w2_%d" % (g + 1)))
-                h.append(first_stage(g + 1))
-            d_q.append(differences(g, 0, HALF if g == last else M, h[g], w2_q[g]))
+        b_tags = [[(4, 5), (6, 7)], [(2, 3), (4, 5)], [(2, 3), (6, 7)]]
+        w2_slots = [1, 2, 1]
+        wo_slots = [(3, 0), (4, 3), (1, 0)]
+
+        def y_banks(tags):
+            return [psum.tile([P, 2, HALF], F32, name="y_bank", tag="bank%d" % b) for b in tags]
+
+        def second_weights(g):
             wo_q.append(
                 [
-                    quantise_weight(load_weight(wo, g, slice(n * PASS, (n + 1) * PASS)), "wo_%d%d" % (g, n))
+                    quantise_weight(
+                        load_weight(wo_slots[g][n], wo, g, slice(n * PASS, (n + 1) * PASS)), "wo_%d%d" % (g, n)
+                    )
                     for n in range(N_GROUPS)
                 ]
             )
+            wu_codes.append(deal_wu(g))
+
+        def passes(g, half, banks, which):
+            second_stage(g, banks, d_q[g][half], wo_q[g], wu_codes[g], wu_planes, which)
+
+        for g in range(last):
+            b = [ledger_features(w2_q[g], half, b_tags[g][half]) for half in range(2)]
+            raw = load_weight(w2_slots[g + 1], w2, 0, slice((g + 1) * PASS, (g + 2) * PASS))
+            w2_q.append(quantise_weight(raw, "w2_%d" % (g + 1)))
+            h.append(first_stage(g + 1, 2))
+            picked = [pick_rows(h[g], half, range(PACK)) for half in range(2)]
+            diff = [subtract(b[half], picked[half]) for half in range(2)]
+            signed = [split_signs(diff[half]) for half in range(2)]
+            d_q.append([quantise_signed(g, half, signed[half]) for half in range(2)])
+            second_weights(g)
             if g == 0:
-                wu_raw_planes = landing("wu_raw_planes", [P, N], U8)
+                wu_raw_planes = landing(6, "wu_raw_planes", [P, N], U8)
                 nc.vector.memset(wu_raw_planes[:].bitcast(I32), 0)
                 for q in range(4):
                     nc.sync.dma_start(
@@ -270,24 +299,36 @@ def tile_list_net_misstatement_scores_kernel(
                     out=wu_planes[:].rearrange("p (n t m) -> p n t m", t=PACK, m=P),
                     in_=wu_raw_planes[:].rearrange("p (n m t) -> p n t m", t=PACK, m=P),
                 )
-                banks0 = [psum.tile([P, 2, HALF], F32, name="y_bank", tag="bank%d" % (4 + b)) for b in range(4)]
-            wu_codes.append(deal_wu(g))
-            second_stage(g, banks0, d_q[g][0], wo_q[g], wu_codes[g], wu_planes, range(4))
 
-        d_q[last].extend(differences(last, HALF, HALF, h[last], w2_q[last]))
-        banks1 = [psum.tile([P, 2, HALF], F32, name="y_bank", tag="bank%d" % b) for b in (0, 1)]
+        b = [ledger_features(w2_q[last], half, b_tags[last][half]) for half in range(2)]
+        banks0 = y_banks((0, 1, 4, 5))
         for g in range(last):
-            second_stage(g, banks1, d_q[g][1], wo_q[g], wu_codes[g], wu_planes, range(2))
+            passes(g, 0, banks0, range(4))
+        second_weights(last)
+        picked0 = pick_rows(h[last], 0, range(PACK))
+        picked1 = pick_rows(h[last], 1, range(0, 1))
+        diff0 = subtract(b[0], picked0)
+        pick_rows(h[last], 1, range(1, 2), picked1)
+        signed0 = split_signs(diff0)
+        pick_rows(h[last], 1, range(2, 3), picked1)
+        d_q.append([quantise_signed(last, 0, signed0)])
+        pick_rows(h[last], 1, range(3, 4), picked1)
+        banks1 = y_banks((2, 3))
+        for g in range(last):
+            passes(g, 1, banks1, range(2))
+        passes(last, 0, banks0, range(4))
+        d_q[last].append(quantise_signed(last, 1, split_signs(subtract(b[1], picked1))))
         finish(0, 0, banks0)
-        banks1.extend(psum.tile([P, 2, HALF], F32, name="y_bank", tag="bank%d" % b) for b in (4, 5))
+        banks1.extend(y_banks((0, 1)))
         for g in range(last):
-            second_stage(g, banks1, d_q[g][1], wo_q[g], wu_codes[g], wu_planes, range(2, 4))
+            passes(g, 1, banks1, range(2, 4))
         finish(1, 0, banks0)
-        second_stage(last, banks1, d_q[last][1], wo_q[last], wu_codes[last], wu_planes, range(4))
+        passes(last, 1, banks1, range(4))
         finish(0, 1, banks1)
         finish(1, 1, banks1)
         for q in range(4):
-            nc.sync.dma_start(
+            queue = nc.scalar if q % 2 else nc.sync
+            queue.dma_start(
                 out=out_2[:, 4 * q : 4 * q + 4, :].rearrange("g r m -> r g m").bitcast(I32),
                 in_=y_plane[32 * q : 32 * q + 4, :, :].bitcast(I32),
             )

@@ -20,10 +20,17 @@ P = 128
 PACK = 4
 PASS = P * PACK
 BANK = 512
+LIST = 16
+QUADRANTS = 4
 R_PASSES = H // PASS
+LAST = R_PASSES - 1
 N_GROUPS = N // PASS
 HALF = M // 2
 CHUNK = BANK // PACK
+MX_ALIGN = 64
+
+W2_BERTHS = ("a", "c", "a")
+WO_BERTHS = (("d", "e"), ("b", "c"), ("d", "e"))
 
 
 def tile_list_net_misstatement_scores_kernel(
@@ -33,55 +40,41 @@ def tile_list_net_misstatement_scores_kernel(
     nc = tc.nc
     with ExitStack() as ctx:
         keep = ctx.enter_context(tc.tile_pool(name="keep", bufs=1))
-        ring = ctx.enter_context(tc.tile_pool(name="ring", bufs=2))
+        ring = ctx.enter_context(tc.tile_pool(name="ring", bufs=1))
         psum = ctx.enter_context(tc.psum_pool(name="psum", bufs=1))
 
         def kept(name, shape, dtype):
-            return keep.tile(shape, dtype, name=name, align_bytes=64)
+            return keep.tile(shape, dtype, name=name, align_bytes=MX_ALIGN)
 
-        def landing(slot, name, shape, dtype):
-            return ring.tile(shape, dtype, name=name, tag="landing%d" % slot, bufs=1, align_bytes=64)
+        def berth(place, name, shape, dtype):
+            return ring.tile(shape, dtype, name=name, tag="berth_" + place, align_bytes=MX_ALIGN)
 
-        def load_words(tile, words):
-            nc.sync.dma_start(out=tile[:], in_=words.rearrange("p c i -> p (c i)").bitcast(I32))
+        def bank(number, name, shape):
+            return psum.tile(shape, F32, name=name, tag="bank%d" % number)
 
-        def load_plane(queues, plane, rows):
-            for q in range(4):
-                queues[q].dma_start(
-                    out=plane[32 * q : 32 * q + 4, :].bitcast(I32),
-                    in_=rows[4 * q : 4 * q + 4, :].bitcast(I32),
+        def load_words(words, source):
+            nc.sync.dma_start(out=words[:], in_=source.rearrange("p c i -> p (c i)").bitcast(I32))
+
+        def load_plane(plane, rows):
+            for q in range(QUADRANTS):
+                nc.scalar.dma_start(
+                    out=plane[32 * q : 32 * q + 4, :].bitcast(I32), in_=rows[4 * q : 4 * q + 4, :].bitcast(I32)
                 )
 
-        idx = kept("idx", [P, S // 16], U16)
-        idx2 = kept("idx2", [P, M // 16], U16)
-        pick = kept("pick", [P, M // 16], U16)
-        w1_raw = landing(0, "w1_raw", [P, 2 * H], U8)
-        w1_raw_plane = landing(5, "w1_raw_plane", [P, H], U8)
-        tab = landing(1, "tab", [P, T], I32)
-        tab_plane = landing(2, "tab_plane", [P, T], U8)
-        tab2_plane = landing(3, "tab2_plane", [P, T], U8)
-
-        nc.vector.memset(tab_plane[:].bitcast(I32), 0)
-        nc.vector.memset(w1_raw_plane[:].bitcast(I32), 0)
-        nc.vector.memset(tab2_plane[:].bitcast(I32), 0)
-
-        nc.sync.dma_start(idx[:], offs)
-        nc.sync.dma_start(idx2[:], offs2)
-        nc.sync.dma_start(pick[:], pos1)
-        load_plane([nc.scalar] * 4, tab_plane, tab_scales[0])
-        nc.sync.dma_start(out=w1_raw[:].bitcast(I32), in_=w1_words[0].bitcast(I32))
-        load_words(tab, tab_words[0])
-        load_plane([nc.scalar] * 4, w1_raw_plane, w1_scales[0])
-
-        def load_weight(slot, w, g, cols):
-            raw = landing(slot, "raw", [P, PACK, PASS], F32)
-            nc.sync.dma_start(
-                out=raw[:], in_=w[g * PASS : (g + 1) * PASS, cols].rearrange("(p j) c -> p j c", j=PACK)
+        def deal_plane(dealt, plane):
+            nc.vector.tensor_copy(
+                out=dealt[:].rearrange("p (g t m) -> p g t m", t=PACK, m=P),
+                in_=plane[:].rearrange("p (g m t) -> p g t m", t=PACK, m=P),
             )
+
+        def load_weight(place, w, g, group):
+            raw = berth(place, "raw", [P, PACK, PASS], F32)
+            rows = w[g * PASS : (g + 1) * PASS, group * PASS : (group + 1) * PASS]
+            nc.sync.dma_start(out=raw[:], in_=rows.rearrange("(p j) c -> p j c", j=PACK))
             return raw
 
-        def quantise_weight(raw, name):
-            staged = ring.tile([P, PASS * PACK], BF16, name="staged", bufs=3, align_bytes=64)
+        def quantise_weight(name, raw):
+            staged = ring.tile([P, PASS * PACK], BF16, name="staged", bufs=4, align_bytes=MX_ALIGN)
             nc.scalar.copy(
                 out=staged[:].rearrange("p (t m j) -> p m j t", t=PACK, j=PACK),
                 in_=raw[:].rearrange("p j (m t) -> p m j t", t=PACK),
@@ -91,242 +84,283 @@ def tile_list_net_misstatement_scores_kernel(
             nc.vector.quantize_mx(out=codes[:].bitcast(FP8X4), scales=plane[:], in_=staged[:])
             return codes, plane
 
-        tab2 = landing(0, "tab2", [P, T], I32)
-        load_words(tab2, tab2_words[0])
-        w2_raw = load_weight(1, w2, 0, slice(0, PASS))
-        load_plane([nc.scalar] * 4, tab2_plane, tab2_scales[0])
+        idx = kept("idx", [P, S // LIST], U16)
+        idx2 = kept("idx2", [P, M // LIST], U16)
+        pick = kept("pick", [P, M // LIST], U16)
+        w1_first = berth("a", "w1_first", [P, 2 * PASS], U8)
+        w1_rest = berth("b", "w1_rest", [P, 2 * (H - PASS)], U8)
+        w1_raw_plane = berth("f", "w1_raw_plane", [P, H], U8)
+        tab = berth("c", "tab", [P, T], I32)
+        tab_plane = berth("d", "tab_plane", [P, T], U8)
+        tab2_plane = berth("e", "tab2_plane", [P, T], U8)
 
+        for plane in (tab_plane, w1_raw_plane, tab2_plane):
+            nc.vector.memset(plane[:].bitcast(I32), 0)
+
+        nc.sync.dma_start(idx[:], offs)
+        nc.sync.dma_start(idx2[:], offs2)
+        nc.sync.dma_start(pick[:], pos1)
+        load_plane(tab_plane, tab_scales[0])
+        nc.sync.dma_start(out=w1_first[:].bitcast(I32), in_=w1_words[0][:, 0 : 2 * PASS].bitcast(I32))
+        nc.sync.dma_start(out=w1_rest[:].bitcast(I32), in_=w1_words[0][:, 2 * PASS : 2 * H].bitcast(I32))
+        load_words(tab, tab_words[0])
+        load_plane(w1_raw_plane, w1_scales[0])
+        w2_first = load_weight(W2_BERTHS[0], w2, 0, 0)
+        tab2 = berth("b", "tab2", [P, T], I32)
+        load_words(tab2, tab2_words[0])
+        load_plane(tab2_plane, tab2_scales[0])
+
+        w1_groups = [w1_first[:]] + [w1_rest[:, 2 * PASS * g : 2 * PASS * (g + 1)] for g in range(LAST)]
         w1_codes = []
-        w1_planes = []
         for g in range(R_PASSES):
-            codes = landing((4, 6, 7)[g], "w1_codes%d" % g, [P, 2 * PASS], U8)
+            codes = berth("pass%d" % g, "w1_codes", [P, 2 * PASS], U8)
             nc.vector.tensor_copy(
                 out=codes[:].bitcast(U16).rearrange("p (t m) -> p t m", t=PACK),
-                in_=w1_raw[:, 2 * PASS * g : 2 * PASS * (g + 1)].bitcast(U16).rearrange("p (m t) -> p t m", t=PACK),
+                in_=w1_groups[g].bitcast(U16).rearrange("p (m t) -> p t m", t=PACK),
             )
             w1_codes.append(codes)
-        w1_plane = kept("w1_plane", [P, H], U8)
-        gains = landing(7, "gains", [P, N_GROUPS, PACK], F32)
-        nc.sync.dma_start(out=gains[:], in_=gain.rearrange("(g p t) -> p g t", p=P, t=PACK))
 
-        def gather_table(name, words, plane, offsets, slot):
-            width = 16 * offsets.shape[1]
-            codes = kept(name + "_codes", [P, width], U32)
-            scales = landing(slot, name + "_plane", [P, width], U8)
+        def gather_table(name, words, plane, offsets, place):
+            codes = kept(name + "_codes", [P, BANK], U32)
+            scales = berth(place, name + "_plane", [P, BANK], U8)
             nc.vector.tensor_copy(out=scales[:], in_=plane[:].indirect(offsets))
             nc.vector.tensor_copy(out=codes[:], in_=words[:].bitcast(U32).indirect(offsets))
             return codes, scales
 
-        v = [gather_table("v0", tab, tab_plane, idx[:, 0 : BANK // 16], 8)]
-        nc.vector.tensor_copy(
-            out=w1_plane[:].rearrange("p (g t m) -> p g t m", t=PACK, m=P),
-            in_=w1_raw_plane[:].rearrange("p (g m t) -> p g t m", t=PACK, m=P),
-        )
-        v.append(gather_table("v1", tab, tab_plane, idx[:, BANK // 16 : 2 * BANK // 16], 5))
-        v2_codes, v2_plane = gather_table("v2", tab2, tab2_plane, idx2[:], 9)
+        w1_plane = kept("w1_plane", [P, H], U8)
+        v = [gather_table("v0", tab, tab_plane, idx[:, 0 : BANK // LIST], "g")]
+        deal_plane(w1_plane, w1_raw_plane)
+        v.append(gather_table("v1", tab, tab_plane, idx[:, BANK // LIST : 2 * BANK // LIST], "f"))
+        gains = berth("f", "gains", [P, N_GROUPS, PACK], F32)
+        nc.sync.dma_start(out=gains[:], in_=gain.rearrange("(g p t) -> p g t", p=P, t=PACK))
+        v2_codes, v2_plane = gather_table("v2", tab2, tab2_plane, idx2[:], "h")
 
-        def first_stage(g, n_banks):
-            rows = [ring.tile([P, S], F32, name="h", bufs=8) for t in range(PACK)]
-            for s in range(S // BANK):
-                for t in range(PACK):
-                    bank = psum.tile([P, BANK], F32, name="h_bank", tag="bank%d" % (t % n_banks))
-                    nc.tensor.matmul_mx(
-                        out=bank[:],
-                        lhsT=w1_codes[g][:, 2 * P * t : 2 * P * (t + 1)].bitcast(FP4X4),
-                        lhsT_scale=w1_plane[:, g * PASS + P * t : g * PASS + P * (t + 1)],
-                        rhs=v[s][0][:].bitcast(FP8X4),
-                        rhs_scale=v[s][1][:],
-                        start=True,
-                        stop=True,
-                    )
-                    nc.scalar.copy(out=rows[t][:, s * BANK : (s + 1) * BANK], in_=bank[:])
+        def summary_rows(count):
+            return [ring.tile([P, S], F32, name="h_slice", bufs=8)[:] for t in range(count)]
+
+        def summary_features(g, rows, first_bank):
+            steps = [(t, s) for pair in (0, 2) for s in range(S // BANK) for t in (pair, pair + 1)]
+            for i, (t, s) in enumerate(steps):
+                acc = bank(first_bank + i % 4, "h_acc", [P, BANK])
+                nc.tensor.matmul_mx(
+                    out=acc[:],
+                    lhsT=w1_codes[g][:, 2 * P * t : 2 * P * (t + 1)].bitcast(FP4X4),
+                    lhsT_scale=w1_plane[:, g * PASS + P * t : g * PASS + P * (t + 1)],
+                    rhs=v[s][0][:].bitcast(FP8X4),
+                    rhs_scale=v[s][1][:],
+                    start=True,
+                    stop=True,
+                )
+                nc.scalar.copy(out=rows[t][:, s * BANK : (s + 1) * BANK], in_=acc[:])
             return rows
 
-        def pick_rows(h_rows, half, ts, picked=None):
-            if picked is None:
-                picked = ring.tile([P, PACK, HALF], F32, name="picked", bufs=4)
-            offsets = pick[:, half * HALF // 16 : (half + 1) * HALF // 16]
-            for t in ts:
-                nc.vector.tensor_copy(out=picked[:, t, :], in_=h_rows[t][:].indirect(offsets))
-            return picked
-
-        def ledger_features(w2_q, half, tags):
+        def ledger_features(g, half, first_bank):
+            codes, plane = w2_q[g]
             banks = []
             for c in range(HALF // CHUNK):
                 cols = slice(half * HALF + c * CHUNK, half * HALF + (c + 1) * CHUNK)
-                bank = psum.tile([P, PACK, CHUNK], F32, name="b_bank", tag="bank%d" % tags[c])
+                acc = bank(first_bank + c, "b_acc", [P, PACK, CHUNK])
                 for t in range(PACK):
                     nc.tensor.matmul_mx(
-                        out=bank[:, t, :],
-                        lhsT=w2_q[0][:, P * t : P * (t + 1)].bitcast(FP8X4),
-                        lhsT_scale=w2_q[1][:, P * t : P * (t + 1)],
+                        out=acc[:, t, :],
+                        lhsT=codes[:, P * t : P * (t + 1)].bitcast(FP8X4),
+                        lhsT_scale=plane[:, P * t : P * (t + 1)],
                         rhs=v2_codes[:, cols].bitcast(FP8X4),
                         rhs_scale=v2_plane[:, cols],
                         start=True,
                         stop=True,
                     )
-                banks.append(bank)
+                banks.append(acc)
             return banks
 
+        def pick_columns(g, first, slices, picked):
+            offsets = pick[:, first // LIST : (first + picked.shape[2]) // LIST]
+            for t in slices:
+                nc.vector.tensor_copy(out=picked[:, t, :], in_=h[g][t].indirect(offsets))
+            return picked
+
         def subtract(banks, picked):
-            diff = ring.tile([P, HALF * PACK], BF16, name="diff", bufs=3, align_bytes=64)
-            for c, bank in enumerate(banks):
+            diff = ring.tile([P, len(banks) * BANK], BF16, name="diff", bufs=3, align_bytes=MX_ALIGN)
+            for c, acc in enumerate(banks):
                 nc.vector.tensor_tensor(
                     out=diff[:, c * BANK : (c + 1) * BANK].rearrange("p (c i t) -> p c t i", i=2, t=PACK),
-                    in0=bank[:].rearrange("p t (c i) -> p c t i", i=2),
+                    in0=acc[:].rearrange("p t (c i) -> p c t i", i=2),
                     in1=picked[:, :, c * CHUNK : (c + 1) * CHUNK].rearrange("p t (c i) -> p c t i", i=2),
                     op=SUBTRACT,
                 )
             return diff
 
-        def split_signs(diff):
-            signed = ring.tile([P, 2 * HALF * PACK], BF16, name="signed", bufs=3, align_bytes=64)
-            nc.vector.tensor_scalar_max(out=signed[:, 0 : HALF * PACK], in0=diff[:], scalar1=0.0)
-            nc.vector.tensor_scalar_min(out=signed[:, HALF * PACK : 2 * HALF * PACK], in0=diff[:], scalar1=0.0)
+        def split_signs(diff, signed):
+            width = diff.shape[1]
+            nc.vector.tensor_scalar_max(out=signed[:, 0:width], in0=diff[:], scalar1=0.0)
+            nc.vector.tensor_scalar_min(out=signed[:, width : 2 * width], in0=diff[:], scalar1=0.0)
             return signed
 
-        def quantise_signed(g, half, signed):
-            codes = kept("d_codes%d%d" % (g, half), [P, 2 * HALF], U32)
-            plane = kept("d_plane%d%d" % (g, half), [P, 2 * HALF], U8)
-            nc.vector.quantize_mx(out=codes[:].bitcast(FP8X4), scales=plane[:], in_=signed[:])
+        def signed_tile(columns):
+            return ring.tile([P, 2 * columns * PACK], BF16, name="signed", bufs=3, align_bytes=MX_ALIGN)
+
+        def quantise_signed(name, signed, calls):
+            words = signed.shape[1] // PACK
+            codes = kept(name + "_codes", [P, words], U32)
+            plane = kept(name + "_plane", [P, words], U8)
+            step = words // calls
+            for c in range(0, words, step):
+                nc.vector.quantize_mx(
+                    out=codes[:, c : c + step].bitcast(FP8X4),
+                    scales=plane[:, c : c + step],
+                    in_=signed[:, PACK * c : PACK * (c + step)],
+                )
             return codes, plane
 
-        def deal_wu(g):
-            raw = landing(2, "wu_raw", [P, N], I32)
+        def both_halves(g, b):
+            picked = [
+                pick_columns(g, half * HALF, range(PACK), ring.tile([P, PACK, HALF], F32, name="picked", bufs=4))
+                for half in range(2)
+            ]
+            diff = [subtract(b[half], picked[half]) for half in range(2)]
+            signed = [split_signs(diff[half], signed_tile(HALF)) for half in range(2)]
+            return [quantise_signed("d%d%d" % (g, half), signed[half], 1) for half in range(2)]
+
+        def score_weights(g):
+            wo_q.append(
+                [
+                    quantise_weight("wo%d%d" % (g, n), load_weight(WO_BERTHS[g][n], wo, g, n))
+                    for n in range(N_GROUPS)
+                ]
+            )
+            raw = berth("pass%d" % g, "wu_raw", [P, N], I32)
             load_words(raw, wu_words[g])
             codes = kept("wu_codes%d" % g, [P, N], I32)
             nc.vector.tensor_copy(
                 out=codes[:].rearrange("p (n t m) -> p n m t", t=PACK, m=P),
                 in_=raw[:].rearrange("p (n m t) -> p n m t", t=PACK, m=P),
             )
-            return codes
+            wu_codes.append(codes)
 
-        def second_stage(g, banks, d_q, wo_q, wu_codes, wu_planes, which):
-            for b in which:
-                n, pair = divmod(b, 2)
+        def score_banks(first_bank, count):
+            return [bank(first_bank + i, "y_acc", [P, 2, HALF]) for i in range(count)]
+
+        def add_pass(g, d_q, banks, which, first, closes):
+            d_codes, d_plane = d_q
+            width = d_codes.shape[1] // 2
+            for i in which:
+                n, pair = divmod(i, 2)
                 for u in range(2):
                     t = 2 * pair + u
                     nc.tensor.matmul_mx(
-                        out=banks[b][:, u, :],
-                        lhsT=wo_q[n][0][:, P * t : P * (t + 1)].bitcast(FP8X4),
-                        lhsT_scale=wo_q[n][1][:, P * t : P * (t + 1)],
-                        rhs=d_q[0][:, 0:HALF].bitcast(FP8X4),
-                        rhs_scale=d_q[1][:, 0:HALF],
+                        out=banks[i][:, u, first : first + width],
+                        lhsT=wo_q[g][n][0][:, P * t : P * (t + 1)].bitcast(FP8X4),
+                        lhsT_scale=wo_q[g][n][1][:, P * t : P * (t + 1)],
+                        rhs=d_codes[:, 0:width].bitcast(FP8X4),
+                        rhs_scale=d_plane[:, 0:width],
                         start=(g == 0 and u == 0),
                         stop=False,
                     )
                     cols = slice(n * PASS + P * t, n * PASS + P * (t + 1))
                     nc.tensor.matmul_mx(
-                        out=banks[b][:, u, :],
-                        lhsT=wu_codes[:, cols].bitcast(FP8X4),
+                        out=banks[i][:, u, first : first + width],
+                        lhsT=wu_codes[g][:, cols].bitcast(FP8X4),
                         lhsT_scale=wu_planes[4 * g : P, cols],
-                        rhs=d_q[0][:, HALF : 2 * HALF].bitcast(FP8X4),
-                        rhs_scale=d_q[1][:, HALF : 2 * HALF],
+                        rhs=d_codes[:, width : 2 * width].bitcast(FP8X4),
+                        rhs_scale=d_plane[:, width : 2 * width],
                         start=False,
-                        stop=(g == R_PASSES - 1 and u == 1),
+                        stop=(closes and u == 1),
                     )
 
-        y_codes = kept("y_codes", [P, N_GROUPS, M], U32)
-        y_plane = kept("y_plane", [P, N_GROUPS, M], U8)
-
-        def finish(n, half, banks):
-            cols = slice(half * HALF, (half + 1) * HALF)
-            y = ring.tile([P, PACK, HALF], F32, name="y", bufs=4)
+        def scores(n, half, banks, on_vector):
+            y = ring.tile([P, PACK, HALF], F32, name="y", bufs=2 * N_GROUPS)
             for t in range(PACK):
-                nc.scalar.activation(
-                    out=y[:, t, :], in_=banks[2 * n + t // 2][:, t % 2, :], func=COPY, scale=gains[:, n, t : t + 1]
-                )
-            nc.sync.dma_start(
-                out=out_0[n * PASS : (n + 1) * PASS, cols].rearrange("(p t) m -> p t m", t=PACK), in_=y[:]
-            )
-            rounded = ring.tile([P, HALF * PACK], BF16, name="rounded", bufs=2, align_bytes=64)
-            round_off = nc.scalar.copy if half == 0 else nc.vector.tensor_copy
-            round_off(
+                acc = banks[2 * n + t // 2][:, t % 2, :]
+                if on_vector:
+                    nc.vector.tensor_scalar_mul(out=y[:, t, :], in0=acc, scalar1=gains[:, n, t : t + 1])
+                else:
+                    nc.scalar.activation(out=y[:, t, :], in_=acc, func=COPY, scale=gains[:, n, t : t + 1])
+            rows = out_0[n * PASS : (n + 1) * PASS, half * HALF : (half + 1) * HALF]
+            nc.sync.dma_start(out=rows.rearrange("(p t) m -> p t m", t=PACK), in_=y[:])
+            return y
+
+        def round_scores(y, on_vector):
+            rounded = ring.tile([P, HALF * PACK], BF16, name="rounded", bufs=2 * N_GROUPS, align_bytes=MX_ALIGN)
+            copy = nc.vector.tensor_copy if on_vector else nc.scalar.copy
+            copy(
                 out=rounded[:].rearrange("p (c i t) -> p c t i", i=4, t=PACK),
                 in_=y[:].rearrange("p t (c i) -> p c t i", i=4),
             )
+            return rounded
+
+        def score_planes(n, half, rounded, queue):
+            cols = slice(half * HALF, (half + 1) * HALF)
             nc.vector.quantize_mx(out=y_codes[:, n, cols].bitcast(FP8X4), scales=y_plane[:, n, cols], in_=rounded[:])
-            nc.sync.dma_start(
+            queue.dma_start(
                 out=out_1[n].rearrange("p m t -> p (m t)").bitcast(I32)[:, cols],
                 in_=y_codes[:, n, cols].bitcast(I32),
             )
 
-        h = [first_stage(0, 4)]
-        w2_q = [quantise_weight(w2_raw, "w2_0")]
-        last = R_PASSES - 1
-        wo_q, wu_codes, d_q = [], [], []
-        wu_planes = kept("wu_planes", [P, N], U8)
-        b_tags = [[(4, 5), (6, 7)], [(2, 3), (4, 5)], [(2, 3), (6, 7)]]
-        w2_slots = [1, 2, 1]
-        wo_slots = [(3, 0), (4, 3), (1, 0)]
+        w2_q = [quantise_weight("w2_0", w2_first)]
+        h_pair = berth(W2_BERTHS[0], "h_pair", [P, 2, S], F32)
+        h = [summary_features(0, [h_pair[:, 0, :], h_pair[:, 1, :]] + summary_rows(2), 0)]
+        b = [ledger_features(0, 0, 0), ledger_features(0, 1, 2)]
+        w2_q.append(quantise_weight("w2_1", load_weight(W2_BERTHS[1], w2, 0, 1)))
+        h.append(summary_features(1, summary_rows(PACK), 4))
+        h.append(summary_features(2, summary_rows(PACK), 4))
+        d_q = [both_halves(0, b)]
+        w2_q.append(quantise_weight("w2_2", load_weight(W2_BERTHS[2], w2, 0, 2)))
+        b = [ledger_features(1, 0, 4), ledger_features(1, 1, 6)]
+        b_last = ledger_features(LAST, 0, 0)
+        d_q.append(both_halves(1, b))
 
-        def y_banks(tags):
-            return [psum.tile([P, 2, HALF], F32, name="y_bank", tag="bank%d" % b) for b in tags]
-
-        def second_weights(g):
-            wo_q.append(
-                [
-                    quantise_weight(
-                        load_weight(wo_slots[g][n], wo, g, slice(n * PASS, (n + 1) * PASS)), "wo_%d%d" % (g, n)
-                    )
-                    for n in range(N_GROUPS)
-                ]
+        wu_raw_planes = berth("g", "wu_raw_planes", [P, N], U8)
+        nc.vector.memset(wu_raw_planes[:].bitcast(I32), 0)
+        for q in range(QUADRANTS):
+            nc.sync.dma_start(
+                out=wu_raw_planes[32 * q : 32 * q + 4 * R_PASSES, :].bitcast(I32),
+                in_=wu_scales[:, 4 * q : 4 * q + 4, :].bitcast(I32),
             )
-            wu_codes.append(deal_wu(g))
+        wu_planes = kept("wu_planes", [P, N], U8)
+        deal_plane(wu_planes, wu_raw_planes)
 
-        def passes(g, half, banks, which):
-            second_stage(g, banks, d_q[g][half], wo_q[g], wu_codes[g], wu_planes, which)
+        wo_q, wu_codes = [], []
+        banks0 = score_banks(2, 4)
+        for g in range(LAST):
+            score_weights(g)
+            add_pass(g, d_q[g][0], banks0, range(4), 0, False)
+        score_weights(LAST)
+        picked = berth(WO_BERTHS[1][0], "picked", [P, PACK, HALF], F32)
+        diff = subtract(b_last, pick_columns(LAST, 0, range(PACK), picked))
+        b_last = ledger_features(LAST, 1, 0)
+        d_last = quantise_signed("d20", split_signs(diff, signed_tile(HALF)), 1)
+        banks1 = score_banks(6, 2)
+        for g in range(LAST):
+            add_pass(g, d_q[g][1], banks1, range(2), 0, False)
+        add_pass(LAST, d_last, banks0, range(4), 0, True)
+        y = [scores(n, 0, banks0, False) for n in range(N_GROUPS)]
+        rounded = [round_scores(y[n], False) for n in range(N_GROUPS)]
 
-        for g in range(last):
-            b = [ledger_features(w2_q[g], half, b_tags[g][half]) for half in range(2)]
-            raw = load_weight(w2_slots[g + 1], w2, 0, slice((g + 1) * PASS, (g + 2) * PASS))
-            w2_q.append(quantise_weight(raw, "w2_%d" % (g + 1)))
-            h.append(first_stage(g + 1, 2))
-            picked = [pick_rows(h[g], half, range(PACK)) for half in range(2)]
-            diff = [subtract(b[half], picked[half]) for half in range(2)]
-            signed = [split_signs(diff[half]) for half in range(2)]
-            d_q.append([quantise_signed(g, half, signed[half]) for half in range(2)])
-            second_weights(g)
-            if g == 0:
-                wu_raw_planes = landing(6, "wu_raw_planes", [P, N], U8)
-                nc.vector.memset(wu_raw_planes[:].bitcast(I32), 0)
-                for q in range(4):
-                    nc.sync.dma_start(
-                        out=wu_raw_planes[32 * q : 32 * q + 4 * R_PASSES, :].bitcast(I32),
-                        in_=wu_scales[:, 4 * q : 4 * q + 4, :].bitcast(I32),
-                    )
-                nc.vector.tensor_copy(
-                    out=wu_planes[:].rearrange("p (n t m) -> p n t m", t=PACK, m=P),
-                    in_=wu_raw_planes[:].rearrange("p (n m t) -> p n t m", t=PACK, m=P),
-                )
+        banks1.extend(score_banks(2, 2))
+        for i in range(2, 4):
+            for g in range(LAST):
+                add_pass(g, d_q[g][1], banks1, [i], 0, False)
 
-        b = [ledger_features(w2_q[last], half, b_tags[last][half]) for half in range(2)]
-        banks0 = y_banks((0, 1, 4, 5))
-        for g in range(last):
-            passes(g, 0, banks0, range(4))
-        second_weights(last)
-        picked0 = pick_rows(h[last], 0, range(PACK))
-        picked1 = pick_rows(h[last], 1, range(0, 1))
-        diff0 = subtract(b[0], picked0)
-        pick_rows(h[last], 1, range(1, 2), picked1)
-        signed0 = split_signs(diff0)
-        pick_rows(h[last], 1, range(2, 3), picked1)
-        d_q.append([quantise_signed(last, 0, signed0)])
-        pick_rows(h[last], 1, range(3, 4), picked1)
-        banks1 = y_banks((2, 3))
-        for g in range(last):
-            passes(g, 1, banks1, range(2))
-        passes(last, 0, banks0, range(4))
-        d_q[last].append(quantise_signed(last, 1, split_signs(subtract(b[1], picked1))))
-        finish(0, 0, banks0)
-        banks1.extend(y_banks((0, 1)))
-        for g in range(last):
-            passes(g, 1, banks1, range(2, 4))
-        finish(1, 0, banks0)
-        passes(last, 1, banks1, range(4))
-        finish(0, 1, banks1)
-        finish(1, 1, banks1)
-        for q in range(4):
+        picked = berth(WO_BERTHS[LAST][1], "picked", [P, 2, PACK, CHUNK], F32)
+        pick_columns(LAST, HALF, range(PACK), picked[:, 0])
+        pick_columns(LAST, HALF + CHUNK, range(1), picked[:, 1])
+        diff = subtract(b_last[0:1], picked[:, 0])
+        pick_columns(LAST, HALF + CHUNK, range(1, PACK), picked[:, 1])
+        signed = split_signs(diff, signed_tile(CHUNK))
+        diff = subtract(b_last[1:2], picked[:, 1])
+        add_pass(LAST, quantise_signed("d21a", signed, 1), banks1, range(4), 0, False)
+        signed = split_signs(diff, berth("i", "signed", [P, 2 * CHUNK * PACK], BF16))
+        add_pass(LAST, quantise_signed("d21b", signed, 2), banks1, range(4), CHUNK, True)
+
+        y_codes = berth("i", "y_codes", [P, N_GROUPS, M], U32)
+        y_plane = kept("y_plane", [P, N_GROUPS, M], U8)
+        for n in range(N_GROUPS):
+            score_planes(n, 0, rounded[n], nc.sync)
+        y = [scores(n, 1, banks1, n == 1) for n in range(N_GROUPS)]
+        rounded = [round_scores(y[n], n == 1) for n in range(N_GROUPS)]
+        for n in range(N_GROUPS):
+            score_planes(n, 1, rounded[n], nc.scalar)
+        for q in range(QUADRANTS):
             queue = nc.scalar if q % 2 else nc.sync
             queue.dma_start(
                 out=out_2[:, 4 * q : 4 * q + 4, :].rearrange("g r m -> r g m").bitcast(I32),

@@ -237,71 +237,70 @@ def tile_list_net_misstatement_scores_kernel(
             )
             wu_codes.append(codes)
 
-        def score_banks(first_bank, count):
-            return [bank(first_bank + i, "y_acc", [P, 2, HALF]) for i in range(count)]
+        def score_bank(number, slices):
+            return bank(number, "y_acc", [P, slices, BANK // slices])
 
-        def add_pass(g, d_q, banks, which, first, closes):
+        def add_pass(g, d_q, first, acc, n, first_slice, closes):
             d_codes, d_plane = d_q
-            width = d_codes.shape[1] // 2
-            for i in which:
-                n, pair = divmod(i, 2)
-                for u in range(2):
-                    t = 2 * pair + u
-                    nc.tensor.matmul_mx(
-                        out=banks[i][:, u, first : first + width],
-                        lhsT=wo_q[g][n][0][:, P * t : P * (t + 1)].bitcast(FP8X4),
-                        lhsT_scale=wo_q[g][n][1][:, P * t : P * (t + 1)],
-                        rhs=d_codes[:, 0:width].bitcast(FP8X4),
-                        rhs_scale=d_plane[:, 0:width],
-                        start=(g == 0 and u == 0),
-                        stop=False,
-                    )
-                    cols = slice(n * PASS + P * t, n * PASS + P * (t + 1))
-                    nc.tensor.matmul_mx(
-                        out=banks[i][:, u, first : first + width],
-                        lhsT=wu_codes[g][:, cols].bitcast(FP8X4),
-                        lhsT_scale=wu_planes[4 * g : P, cols],
-                        rhs=d_codes[:, width : 2 * width].bitcast(FP8X4),
-                        rhs_scale=d_plane[:, width : 2 * width],
-                        start=False,
-                        stop=(closes and u == 1),
-                    )
+            slices, width = acc.shape[1], acc.shape[2]
+            above = slice(first, first + width)
+            below = slice(d_codes.shape[1] // 2 + first, d_codes.shape[1] // 2 + first + width)
+            for u in range(slices):
+                t = first_slice + u
+                nc.tensor.matmul_mx(
+                    out=acc[:, u, :],
+                    lhsT=wo_q[g][n][0][:, P * t : P * (t + 1)].bitcast(FP8X4),
+                    lhsT_scale=wo_q[g][n][1][:, P * t : P * (t + 1)],
+                    rhs=d_codes[:, above].bitcast(FP8X4),
+                    rhs_scale=d_plane[:, above],
+                    start=(g == 0 and u == 0),
+                    stop=False,
+                )
+                cols = slice(n * PASS + P * t, n * PASS + P * (t + 1))
+                nc.tensor.matmul_mx(
+                    out=acc[:, u, :],
+                    lhsT=wu_codes[g][:, cols].bitcast(FP8X4),
+                    lhsT_scale=wu_planes[4 * g : P, cols],
+                    rhs=d_codes[:, below].bitcast(FP8X4),
+                    rhs_scale=d_plane[:, below],
+                    start=False,
+                    stop=(closes and u == slices - 1),
+                )
 
-        def scores(n, half, banks, on_vector):
-            y = ring.tile([P, PACK, HALF], F32, name="y", bufs=2 * N_GROUPS)
+        def scores(n, first, sums):
+            width = sums[0].shape[1]
+            count = N_GROUPS * HALF // width
+            y = ring.tile([P, PACK, width], F32, name="y%d" % width, bufs=count)
             for t in range(PACK):
-                acc = banks[2 * n + t // 2][:, t % 2, :]
-                if on_vector:
-                    nc.vector.tensor_scalar_mul(out=y[:, t, :], in0=acc, scalar1=gains[:, n, t : t + 1])
-                else:
-                    nc.scalar.activation(out=y[:, t, :], in_=acc, func=COPY, scale=gains[:, n, t : t + 1])
-            rows = out_0[n * PASS : (n + 1) * PASS, half * HALF : (half + 1) * HALF]
+                nc.scalar.activation(out=y[:, t, :], in_=sums[t], func=COPY, scale=gains[:, n, t : t + 1])
+            rows = out_0[n * PASS : (n + 1) * PASS, first : first + width]
             nc.sync.dma_start(out=rows.rearrange("(p t) m -> p t m", t=PACK), in_=y[:])
             return y
 
-        def round_scores(y, on_vector):
-            rounded = ring.tile([P, HALF * PACK], BF16, name="rounded", bufs=2 * N_GROUPS, align_bytes=MX_ALIGN)
-            copy = nc.vector.tensor_copy if on_vector else nc.scalar.copy
+        def round_scores(y, copy):
+            width = y.shape[2]
+            rounded = ring.tile(
+                [P, width * PACK], BF16, name="rounded%d" % width, bufs=N_GROUPS * HALF // width, align_bytes=MX_ALIGN
+            )
             copy(
                 out=rounded[:].rearrange("p (c i t) -> p c t i", i=4, t=PACK),
                 in_=y[:].rearrange("p t (c i) -> p c t i", i=4),
             )
             return rounded
 
-        def score_planes(n, half, rounded, queue):
-            cols = slice(half * HALF, (half + 1) * HALF)
+        def quantise_scores(n, first, rounded):
+            cols = slice(first, first + rounded.shape[1] // PACK)
             nc.vector.quantize_mx(out=y_codes[:, n, cols].bitcast(FP8X4), scales=y_plane[:, n, cols], in_=rounded[:])
-            queue.dma_start(
-                out=out_1[n].rearrange("p m t -> p (m t)").bitcast(I32)[:, cols],
-                in_=y_codes[:, n, cols].bitcast(I32),
-            )
+
+        def paired_rows(place):
+            pair = berth(place, "h_pair", [P, 2, S], F32)
+            return [pair[:, 0, :], pair[:, 1, :]] + summary_rows(2)
 
         w2_q = [quantise_weight("w2_0", w2_first)]
-        h_pair = berth(W2_BERTHS[0], "h_pair", [P, 2, S], F32)
-        h = [summary_features(0, [h_pair[:, 0, :], h_pair[:, 1, :]] + summary_rows(2), 0)]
+        h = [summary_features(0, paired_rows(W2_BERTHS[0]), 0)]
         b = [ledger_features(0, 0, 0), ledger_features(0, 1, 2)]
         w2_q.append(quantise_weight("w2_1", load_weight(W2_BERTHS[1], w2, 0, 1)))
-        h.append(summary_features(1, summary_rows(PACK), 4))
+        h.append(summary_features(1, paired_rows(W2_BERTHS[1]), 4))
         h.append(summary_features(2, summary_rows(PACK), 4))
         d_q = [both_halves(0, b)]
         w2_q.append(quantise_weight("w2_2", load_weight(W2_BERTHS[2], w2, 0, 2)))
@@ -320,26 +319,32 @@ def tile_list_net_misstatement_scores_kernel(
         deal_plane(wu_planes, wu_raw_planes)
 
         wo_q, wu_codes = [], []
-        banks0 = score_banks(2, 4)
+        banks0 = [score_bank(2 + i, 2) for i in range(2 * N_GROUPS)]
+
+        def add_half_pass(g, d_half):
+            for i, acc in enumerate(banks0):
+                add_pass(g, d_half, 0, acc, i // 2, 2 * (i % 2), g == LAST)
+
         for g in range(LAST):
             score_weights(g)
-            add_pass(g, d_q[g][0], banks0, range(4), 0, False)
+            add_half_pass(g, d_q[g][0])
         score_weights(LAST)
         picked = berth(WO_BERTHS[1][0], "picked", [P, PACK, HALF], F32)
         diff = subtract(b_last, pick_columns(LAST, 0, range(PACK), picked))
         b_last = ledger_features(LAST, 1, 0)
         d_last = quantise_signed("d20", split_signs(diff, signed_tile(HALF)), 1)
-        banks1 = score_banks(6, 2)
-        for g in range(LAST):
-            add_pass(g, d_q[g][1], banks1, range(2), 0, False)
-        add_pass(LAST, d_last, banks0, range(4), 0, True)
-        y = [scores(n, 0, banks0, False) for n in range(N_GROUPS)]
-        rounded = [round_scores(y[n], False) for n in range(N_GROUPS)]
 
-        banks1.extend(score_banks(2, 2))
-        for i in range(2, 4):
+        banks1 = [[score_bank(6 + n, PACK) for n in range(N_GROUPS)]]
+        for g in range(LAST):
+            for n in range(N_GROUPS):
+                add_pass(g, d_q[g][1], 0, banks1[0][n], n, 0, False)
+        add_half_pass(LAST, d_last)
+        y = [scores(n, 0, [banks0[2 * n + t // 2][:, t % 2, :] for t in range(PACK)]) for n in range(N_GROUPS)]
+        rounded = [round_scores(y[n], nc.scalar.copy) for n in range(N_GROUPS)]
+        banks1.append([score_bank(2 + n, PACK) for n in range(N_GROUPS)])
+        for n in range(N_GROUPS):
             for g in range(LAST):
-                add_pass(g, d_q[g][1], banks1, [i], 0, False)
+                add_pass(g, d_q[g][1], CHUNK, banks1[1][n], n, 0, False)
 
         picked = berth(WO_BERTHS[LAST][1], "picked", [P, 2, PACK, CHUNK], F32)
         pick_columns(LAST, HALF, range(PACK), picked[:, 0])
@@ -348,18 +353,29 @@ def tile_list_net_misstatement_scores_kernel(
         pick_columns(LAST, HALF + CHUNK, range(1, PACK), picked[:, 1])
         signed = split_signs(diff, signed_tile(CHUNK))
         diff = subtract(b_last[1:2], picked[:, 1])
-        add_pass(LAST, quantise_signed("d21a", signed, 1), banks1, range(4), 0, False)
+        d_last = quantise_signed("d21a", signed, 1)
+        for n in range(N_GROUPS):
+            add_pass(LAST, d_last, 0, banks1[0][n], n, 0, True)
         signed = split_signs(diff, berth("i", "signed", [P, 2 * CHUNK * PACK], BF16))
-        add_pass(LAST, quantise_signed("d21b", signed, 2), banks1, range(4), CHUNK, True)
+        d_last = quantise_signed("d21b", signed, 2)
+        for n in range(N_GROUPS):
+            add_pass(LAST, d_last, 0, banks1[1][n], n, 0, True)
 
         y_codes = berth("i", "y_codes", [P, N_GROUPS, M], U32)
         y_plane = kept("y_plane", [P, N_GROUPS, M], U8)
+        out_words = out_1.rearrange("g p m t -> p g (m t)").bitcast(I32)
         for n in range(N_GROUPS):
-            score_planes(n, 0, rounded[n], nc.sync)
-        y = [scores(n, 1, banks1, n == 1) for n in range(N_GROUPS)]
-        rounded = [round_scores(y[n], n == 1) for n in range(N_GROUPS)]
-        for n in range(N_GROUPS):
-            score_planes(n, 1, rounded[n], nc.scalar)
+            quantise_scores(n, 0, rounded[n])
+            nc.sync.dma_start(out=out_words[:, n, 0:HALF], in_=y_codes[:, n, 0:HALF].bitcast(I32))
+        for c in range(HALF // CHUNK):
+            first = HALF + c * CHUNK
+            rounded = [
+                round_scores(scores(n, first, [banks1[c][n][:, t, :] for t in range(PACK)]), nc.vector.tensor_copy)
+                for n in range(N_GROUPS)
+            ]
+            for n in range(N_GROUPS):
+                quantise_scores(n, first, rounded[n])
+        nc.scalar.dma_start(out=out_words[:, :, HALF:M], in_=y_codes[:, :, HALF:M].bitcast(I32))
         for q in range(QUADRANTS):
             queue = nc.scalar if q % 2 else nc.sync
             queue.dma_start(

@@ -73,8 +73,9 @@ def tile_list_net_misstatement_scores_kernel(
             nc.sync.dma_start(out=raw[:], in_=rows.rearrange("(p j) c -> p j c", j=PACK))
             return raw
 
-        def quantise_weight(name, raw):
-            staged = ring.tile([P, PASS * PACK], BF16, name="staged", bufs=4, align_bytes=MX_ALIGN)
+        def quantise_weight(name, raw, staged=None):
+            if staged is None:
+                staged = ring.tile([P, PASS * PACK], BF16, name="staged", bufs=4, align_bytes=MX_ALIGN)
             nc.scalar.copy(
                 out=staged[:].rearrange("p (t m j) -> p m j t", t=PACK, j=PACK),
                 in_=raw[:].rearrange("p j (m t) -> p m j t", t=PACK),
@@ -212,28 +213,32 @@ def tile_list_net_misstatement_scores_kernel(
                 )
             return codes, plane
 
-        def both_halves(g, b):
+        def both_halves(g, b, last_signed):
             picked = [
                 pick_columns(g, half * HALF, range(PACK), ring.tile([P, PACK, HALF], F32, name="picked", bufs=4))
                 for half in range(2)
             ]
             diff = [subtract(b[half], picked[half]) for half in range(2)]
-            signed = [split_signs(diff[half], signed_tile(HALF)) for half in range(2)]
+            signed = [split_signs(diff[0], signed_tile(HALF)), split_signs(diff[1], last_signed)]
             return [quantise_signed("d%d%d" % (g, half), signed[half], 1) for half in range(2)]
 
         def score_weights(g):
             wo_q.append(
                 [
-                    quantise_weight("wo%d%d" % (g, n), load_weight(WO_BERTHS[g][n], wo, g, n))
+                    quantise_weight(
+                        "wo%d%d" % (g, n),
+                        load_weight(WO_BERTHS[g][n], wo, g, n),
+                        berth("wu2", "staged", [P, PASS * PACK], BF16) if (g, n) == (1, 0) else None,
+                    )
                     for n in range(N_GROUPS)
                 ]
             )
             raw = berth("pass%d" % g, "wu_raw", [P, N], I32)
             load_words(raw, wu_words[g])
-            codes = kept("wu_codes%d" % g, [P, N], I32)
-            nc.vector.tensor_copy(
-                out=codes[:].rearrange("p (n t m) -> p n m t", t=PACK, m=P),
-                in_=raw[:].rearrange("p (n m t) -> p n m t", t=PACK, m=P),
+            codes = berth("wu%d" % g, "wu_codes", [P, N], I32)
+            nc.gpsimd.tensor_copy(
+                out=codes[:].rearrange("p (n t m) -> p n t m", t=PACK, m=P),
+                in_=raw[:].rearrange("p (n m t) -> p n t m", t=PACK, m=P),
             )
             wu_codes.append(codes)
 
@@ -302,11 +307,11 @@ def tile_list_net_misstatement_scores_kernel(
         w2_q.append(quantise_weight("w2_1", load_weight(W2_BERTHS[1], w2, 0, 1)))
         h.append(summary_features(1, paired_rows(W2_BERTHS[1]), 4))
         h.append(summary_features(2, summary_rows(PACK), 4))
-        d_q = [both_halves(0, b)]
+        d_q = [both_halves(0, b, berth("wu0", "signed", [P, 2 * HALF * PACK], BF16))]
         w2_q.append(quantise_weight("w2_2", load_weight(W2_BERTHS[2], w2, 0, 2)))
         b = [ledger_features(1, 0, 4), ledger_features(1, 1, 6)]
         b_last = ledger_features(LAST, 0, 0)
-        d_q.append(both_halves(1, b))
+        d_q.append(both_halves(1, b, signed_tile(HALF)))
 
         wu_raw_planes = berth("g", "wu_raw_planes", [P, N], U8)
         nc.vector.memset(wu_raw_planes[:].bitcast(I32), 0)

@@ -14,6 +14,8 @@ U8 = mybir.dt.uint8
 FP8X4 = mybir.dt.float8_e4m3fn_x4
 FP4X4 = mybir.dt.float4_e2m1fn_x4
 COPY = mybir.ActivationFunctionType.Copy
+ADD = mybir.AluOpType.add
+MULT = mybir.AluOpType.mult
 SUBTRACT = mybir.AluOpType.subtract
 
 P = 128
@@ -23,14 +25,24 @@ BANK = 512
 LIST = 16
 QUADRANTS = 4
 R_PASSES = H // PASS
-LAST = R_PASSES - 1
 N_GROUPS = N // PASS
 HALF = M // 2
 CHUNK = BANK // PACK
-MX_ALIGN = 64
+KB = 1024
 
-W2_BERTHS = ("a", "c", "a")
-WO_BERTHS = (("d", "e"), ("b", "c"), ("d", "e"))
+H_ROWS = 0
+LAND = 48
+WU_RAW = 96
+W1_RAW, W1_RAW_PLANE, W1_CODES, W1_PLANE = 108, 111, 113, 116
+TAB_PLANE, TAB2_PLANE, WU_RAW_PLANES = 118, 120, 122
+V_CODES, V_PLANE, V2_CODES, V2_PLANE = 123, 127, 128, 130
+W_CODES = 131
+D_CODES = 149
+DIFF = 164
+STAGE = 176
+TURN = 192
+LAST = 213
+W2_PLANE = 221
 
 
 def tile_list_net_misstatement_scores_kernel(
@@ -40,14 +52,11 @@ def tile_list_net_misstatement_scores_kernel(
     nc = tc.nc
     with ExitStack() as ctx:
         keep = ctx.enter_context(tc.tile_pool(name="keep", bufs=1))
-        ring = ctx.enter_context(tc.tile_pool(name="ring", bufs=1))
+        sbuf = ctx.enter_context(tc.tile_pool(name="sbuf", bufs=1))
         psum = ctx.enter_context(tc.psum_pool(name="psum", bufs=1))
 
-        def kept(name, shape, dtype):
-            return keep.tile(shape, dtype, name=name, align_bytes=MX_ALIGN)
-
-        def berth(place, name, shape, dtype):
-            return ring.tile(shape, dtype, name=name, tag="berth_" + place, align_bytes=MX_ALIGN)
+        def at(kb, name, shape, dtype):
+            return sbuf.tile(shape, dtype, name=name, offset=int(kb * KB), align_bytes=64)
 
         def bank(number, name, shape):
             return psum.tile(shape, F32, name=name, tag="bank%d" % number)
@@ -55,133 +64,143 @@ def tile_list_net_misstatement_scores_kernel(
         def load_words(words, source):
             nc.sync.dma_start(out=words[:], in_=source.rearrange("p c i -> p (c i)").bitcast(I32))
 
-        def load_plane(plane, rows):
+        def load_plane(queue, plane, rows):
             for q in range(QUADRANTS):
-                nc.scalar.dma_start(
+                queue.dma_start(
                     out=plane[32 * q : 32 * q + 4, :].bitcast(I32), in_=rows[4 * q : 4 * q + 4, :].bitcast(I32)
                 )
 
-        def deal_plane(dealt, plane):
-            nc.vector.tensor_copy(
-                out=dealt[:].rearrange("p (g t m) -> p g t m", t=PACK, m=P),
-                in_=plane[:].rearrange("p (g m t) -> p g t m", t=PACK, m=P),
+        def deal(engine, dealt, natural):
+            engine.tensor_copy(
+                out=dealt.rearrange("p (g t m) -> p g t m", t=PACK, m=P),
+                in_=natural.rearrange("p (g m t) -> p g t m", t=PACK, m=P),
             )
 
-        def load_weight(place, w, g, group):
-            raw = berth(place, "raw", [P, PACK, PASS], F32)
+        def load_weight(place, name, w, g, group):
+            raw = at(LAND + 8 * place, name + "_raw", [P, PACK, PASS], F32)
             rows = w[g * PASS : (g + 1) * PASS, group * PASS : (group + 1) * PASS]
             nc.sync.dma_start(out=raw[:], in_=rows.rearrange("(p j) c -> p j c", j=PACK))
             return raw
 
-        def quantise_weight(name, raw, staged=None):
-            if staged is None:
-                staged = ring.tile([P, PASS * PACK], BF16, name="staged", bufs=4, align_bytes=MX_ALIGN)
-            nc.scalar.copy(
-                out=staged[:].rearrange("p (t m j) -> p m j t", t=PACK, j=PACK),
-                in_=raw[:].rearrange("p j (m t) -> p m j t", t=PACK),
-            )
-            codes = kept(name + "_codes", [P, PASS], U32)
-            plane = kept(name + "_plane", [P, PASS], U8)
+        def round_weight(name, raw, kb, on_gpsimd):
+            staged = at(kb, name + "_staged", [P, PASS * PACK], BF16)
+            if on_gpsimd:
+                nc.gpsimd.tensor_scalar(
+                    out=staged[:].rearrange("p (t m j) -> p m t j", t=PACK, j=PACK),
+                    in0=raw[:].rearrange("p j (m t) -> p m t j", t=PACK),
+                    scalar1=1.0, scalar2=0.0, op0=MULT, op1=ADD,
+                )
+            else:
+                nc.scalar.copy(
+                    out=staged[:].rearrange("p (t m j) -> p m j t", t=PACK, j=PACK),
+                    in_=raw[:].rearrange("p j (m t) -> p m j t", t=PACK),
+                )
+            return staged
+
+        def quantise_weight(name, number, staged, plane_kb):
+            codes = at(W_CODES + 2 * number, name + "_codes", [P, PASS], U32)
+            plane = at(plane_kb, name + "_plane", [P, PASS], U8)
             nc.vector.quantize_mx(out=codes[:].bitcast(FP8X4), scales=plane[:], in_=staged[:])
             return codes, plane
 
-        idx = kept("idx", [P, S // LIST], U16)
-        idx2 = kept("idx2", [P, M // LIST], U16)
-        pick = kept("pick", [P, M // LIST], U16)
-        w1_first = berth("a", "w1_first", [P, 2 * PASS], U8)
-        w1_rest = berth("b", "w1_rest", [P, 2 * (H - PASS)], U8)
-        w1_raw_plane = berth("f", "w1_raw_plane", [P, H], U8)
-        tab = berth("c", "tab", [P, T], I32)
-        tab_plane = berth("d", "tab_plane", [P, T], U8)
-        tab2_plane = berth("e", "tab2_plane", [P, T], U8)
-
-        for plane in (tab_plane, w1_raw_plane, tab2_plane):
-            nc.vector.memset(plane[:].bitcast(I32), 0)
+        idx = keep.tile([P, S // LIST], U16, name="idx")
+        idx2 = keep.tile([P, M // LIST], U16, name="idx2")
+        pick = keep.tile([P, M // LIST], U16, name="pick")
+        gains = keep.tile([P, N_GROUPS, PACK], F32, name="gains")
+        tab_plane = at(TAB_PLANE, "tab_plane", [P, T], U8)
+        w1_raw_plane = at(W1_RAW_PLANE, "w1_raw_plane", [P, H], U8)
+        tab2_plane = at(TAB2_PLANE, "tab2_plane", [P, T], U8)
+        wu_raw_planes = at(WU_RAW_PLANES, "wu_raw_planes", [P, N], U8)
+        nc.vector.memset(tab_plane[:].bitcast(I32), 0)
+        nc.vector.memset(w1_raw_plane[:].bitcast(I32), 0)
+        nc.vector.memset(tab2_plane[:].bitcast(I32), 0)
+        nc.vector.memset(wu_raw_planes[:].bitcast(I32), 0)
 
         nc.sync.dma_start(idx[:], offs)
+        w1_raw = at(W1_RAW, "w1_raw", [P, 2 * H], U8)
+        nc.sync.dma_start(out=w1_raw[:].bitcast(I32), in_=w1_words[0].bitcast(I32))
+        load_plane(nc.sync, tab_plane, tab_scales[0])
         nc.sync.dma_start(idx2[:], offs2)
-        nc.sync.dma_start(pick[:], pos1)
-        load_plane(tab_plane, tab_scales[0])
-        nc.sync.dma_start(out=w1_first[:].bitcast(I32), in_=w1_words[0][:, 0 : 2 * PASS].bitcast(I32))
-        nc.sync.dma_start(out=w1_rest[:].bitcast(I32), in_=w1_words[0][:, 2 * PASS : 2 * H].bitcast(I32))
+        w2_raw = [load_weight(2, "w2_0", w2, 0, 0)]
+        load_plane(nc.scalar, w1_raw_plane, w1_scales[0])
+        tab = at(LAND, "tab", [P, T], I32)
         load_words(tab, tab_words[0])
-        load_plane(w1_raw_plane, w1_scales[0])
-        w2_first = load_weight(W2_BERTHS[0], w2, 0, 0)
-        tab2 = berth("b", "tab2", [P, T], I32)
+        load_plane(nc.sync, tab2_plane, tab2_scales[0])
+        tab2 = at(LAND + 8, "tab2", [P, T], I32)
         load_words(tab2, tab2_words[0])
-        load_plane(tab2_plane, tab2_scales[0])
-
-        w1_groups = [w1_first[:]] + [w1_rest[:, 2 * PASS * g : 2 * PASS * (g + 1)] for g in range(LAST)]
-        w1_codes = []
-        for g in range(R_PASSES):
-            codes = berth("pass%d" % g, "w1_codes", [P, 2 * PASS], U8)
-            nc.vector.tensor_copy(
-                out=codes[:].bitcast(U16).rearrange("p (t m) -> p t m", t=PACK),
-                in_=w1_groups[g].bitcast(U16).rearrange("p (m t) -> p t m", t=PACK),
+        nc.sync.dma_start(pick[:], pos1)
+        w2_raw.append(load_weight(3, "w2_1", w2, 0, 1))
+        w2_raw.append(load_weight(4, "w2_2", w2, 0, 2))
+        wo_raw = [load_weight(5, "wo00", wo, 0, 0)]
+        for q in range(QUADRANTS):
+            nc.sync.dma_start(
+                out=wu_raw_planes[32 * q : 32 * q + 4 * R_PASSES, :].bitcast(I32),
+                in_=wu_scales[:, 4 * q : 4 * q + 4, :].bitcast(I32),
             )
-            w1_codes.append(codes)
-
-        def gather_table(name, words, plane, offsets, place):
-            codes = kept(name + "_codes", [P, BANK], U32)
-            scales = berth(place, name + "_plane", [P, BANK], U8)
-            nc.vector.tensor_copy(out=scales[:], in_=plane[:].indirect(offsets))
-            nc.vector.tensor_copy(out=codes[:], in_=words[:].bitcast(U32).indirect(offsets))
-            return codes, scales
-
-        w1_plane = kept("w1_plane", [P, H], U8)
-        v = [gather_table("v0", tab, tab_plane, idx[:, 0 : BANK // LIST], "g")]
-        deal_plane(w1_plane, w1_raw_plane)
-        v.append(gather_table("v1", tab, tab_plane, idx[:, BANK // LIST : 2 * BANK // LIST], "f"))
-        gains = berth("f", "gains", [P, N_GROUPS, PACK], F32)
         nc.sync.dma_start(out=gains[:], in_=gain.rearrange("(g p t) -> p g t", p=P, t=PACK))
-        v2_codes, v2_plane = gather_table("v2", tab2, tab2_plane, idx2[:], "h")
+        wu_raw = at(WU_RAW, "wu_raw", [P, R_PASSES, N], I32)
+        nc.sync.dma_start(out=wu_raw[:], in_=wu_words.rearrange("a p c i -> p a (c i)").bitcast(I32))
 
-        def summary_rows(count):
-            return [ring.tile([P, S], F32, name="h_slice", bufs=8)[:] for t in range(count)]
+        v_plane = at(V_PLANE, "v_plane", [P, S], U8)
+        nc.vector.tensor_copy(out=v_plane[:], in_=tab_plane[:].indirect(idx[:]))
+        w1_codes = at(W1_CODES, "w1_codes", [P, 2 * H], U8)
+        deal(nc.vector, w1_codes[:].bitcast(U16), w1_raw[:].bitcast(U16))
+        w1_plane = at(W1_PLANE, "w1_plane", [P, H], U8)
+        deal(nc.vector, w1_plane[:], w1_raw_plane[:])
+        v_codes = []
+        for s in range(S // BANK):
+            codes = at(V_CODES + 2 * s, "v_codes%d" % s, [P, BANK], U32)
+            offsets = idx[:, s * BANK // LIST : (s + 1) * BANK // LIST]
+            nc.vector.tensor_copy(out=codes[:], in_=tab[:].bitcast(U32).indirect(offsets))
+            v_codes.append(codes)
+        v2_plane = at(V2_PLANE, "v2_plane", [P, M], U8)
+        nc.vector.tensor_copy(out=v2_plane[:], in_=tab2_plane[:].indirect(idx2[:]))
+        w2_q = [quantise_weight("w2_0", 0, round_weight("w2_0", w2_raw[0], STAGE, False), W2_PLANE)]
+        v2_codes = at(V2_CODES, "v2_codes", [P, M], U32)
+        nc.vector.tensor_copy(out=v2_codes[:], in_=tab2[:].bitcast(U32).indirect(idx2[:]))
+        wo_raw.append(load_weight(2, "wo01", wo, 0, 1))
+        wo_raw.append(load_weight(0, "wo10", wo, 1, 0))
 
-        def summary_features(g, rows, first_bank):
-            steps = [(t, s) for pair in (0, 2) for s in range(S // BANK) for t in (pair, pair + 1)]
-            for i, (t, s) in enumerate(steps):
-                acc = bank(first_bank + i % 4, "h_acc", [P, BANK])
-                nc.tensor.matmul_mx(
-                    out=acc[:],
-                    lhsT=w1_codes[g][:, 2 * P * t : 2 * P * (t + 1)].bitcast(FP4X4),
-                    lhsT_scale=w1_plane[:, g * PASS + P * t : g * PASS + P * (t + 1)],
-                    rhs=v[s][0][:].bitcast(FP8X4),
-                    rhs_scale=v[s][1][:],
-                    start=True,
-                    stop=True,
-                )
-                nc.scalar.copy(out=rows[t][:, s * BANK : (s + 1) * BANK], in_=acc[:])
-            return rows
-
-        def ledger_features(g, half, first_bank):
-            codes, plane = w2_q[g]
-            banks = []
-            for c in range(HALF // CHUNK):
-                cols = slice(half * HALF + c * CHUNK, half * HALF + (c + 1) * CHUNK)
-                acc = bank(first_bank + c, "b_acc", [P, PACK, CHUNK])
-                for t in range(PACK):
+        def summary_features(g):
+            rows = [at(H_ROWS + 4 * (PACK * g + t), "h%d%d" % (g, t), [P, S], F32) for t in range(PACK)]
+            for t in range(PACK):
+                for s in range(S // BANK):
+                    acc = bank((2 * t + s) % 4, "h_acc", [P, BANK])
+                    cols = slice(g * PASS + P * t, g * PASS + P * (t + 1))
                     nc.tensor.matmul_mx(
-                        out=acc[:, t, :],
-                        lhsT=codes[:, P * t : P * (t + 1)].bitcast(FP8X4),
-                        lhsT_scale=plane[:, P * t : P * (t + 1)],
-                        rhs=v2_codes[:, cols].bitcast(FP8X4),
-                        rhs_scale=v2_plane[:, cols],
+                        out=acc[:],
+                        lhsT=w1_codes[:, 2 * cols.start : 2 * cols.stop].bitcast(FP4X4),
+                        lhsT_scale=w1_plane[:, cols],
+                        rhs=v_codes[s][:].bitcast(FP8X4),
+                        rhs_scale=v_plane[:, s * BANK : (s + 1) * BANK],
                         start=True,
                         stop=True,
                     )
-                banks.append(acc)
-            return banks
+                    nc.scalar.copy(out=rows[t][:, s * BANK : (s + 1) * BANK], in_=acc[:])
+            return rows
+
+        def ledger_features(g, c, number):
+            codes, plane = w2_q[g]
+            cols = slice(c * CHUNK, (c + 1) * CHUNK)
+            acc = bank(number, "b_acc%d%d" % (g, c), [P, PACK, CHUNK])
+            for t in range(PACK):
+                nc.tensor.matmul_mx(
+                    out=acc[:, t, :],
+                    lhsT=codes[:, P * t : P * (t + 1)].bitcast(FP8X4),
+                    lhsT_scale=plane[:, P * t : P * (t + 1)],
+                    rhs=v2_codes[:, cols].bitcast(FP8X4),
+                    rhs_scale=v2_plane[:, cols],
+                    start=True,
+                    stop=True,
+                )
+            return acc
 
         def pick_columns(g, first, slices, picked):
             offsets = pick[:, first // LIST : (first + picked.shape[2]) // LIST]
             for t in slices:
-                nc.vector.tensor_copy(out=picked[:, t, :], in_=h[g][t].indirect(offsets))
-            return picked
+                nc.vector.tensor_copy(out=picked[:, t, :], in_=h[g][t][:].indirect(offsets))
 
-        def subtract(banks, picked):
-            diff = ring.tile([P, len(banks) * BANK], BF16, name="diff", bufs=3, align_bytes=MX_ALIGN)
+        def subtract(banks, picked, diff):
             for c, acc in enumerate(banks):
                 nc.vector.tensor_tensor(
                     out=diff[:, c * BANK : (c + 1) * BANK].rearrange("p (c i t) -> p c t i", i=2, t=PACK),
@@ -189,197 +208,173 @@ def tile_list_net_misstatement_scores_kernel(
                     in1=picked[:, :, c * CHUNK : (c + 1) * CHUNK].rearrange("p t (c i) -> p c t i", i=2),
                     op=SUBTRACT,
                 )
-            return diff
 
-        def split_signs(diff, signed):
+        def split_signs(name, diff, kb):
             width = diff.shape[1]
-            nc.vector.tensor_scalar_max(out=signed[:, 0:width], in0=diff[:], scalar1=0.0)
-            nc.vector.tensor_scalar_min(out=signed[:, width : 2 * width], in0=diff[:], scalar1=0.0)
-            return signed
+            above = at(kb, name + "_above", [P, width], BF16)
+            below = at(kb + 2 * width / KB, name + "_below", [P, width], BF16)
+            nc.vector.tensor_scalar_max(out=above[:], in0=diff, scalar1=0.0)
+            nc.vector.tensor_scalar_min(out=below[:], in0=diff, scalar1=0.0)
+            return above, below
 
-        def signed_tile(columns):
-            return ring.tile([P, 2 * columns * PACK], BF16, name="signed", bufs=3, align_bytes=MX_ALIGN)
+        def quantise_signed(g, first, signed):
+            for side in range(2):
+                words = signed[side].shape[1] // PACK
+                cols = slice(side * M + first, side * M + first + words)
+                nc.vector.quantize_mx(out=d_q[g][0][:, cols].bitcast(FP8X4), scales=d_q[g][1][:, cols], in_=signed[side][:])
 
-        def quantise_signed(name, signed, calls):
-            words = signed.shape[1] // PACK
-            codes = kept(name + "_codes", [P, words], U32)
-            plane = kept(name + "_plane", [P, words], U8)
-            step = words // calls
-            for c in range(0, words, step):
-                nc.vector.quantize_mx(
-                    out=codes[:, c : c + step].bitcast(FP8X4),
-                    scales=plane[:, c : c + step],
-                    in_=signed[:, PACK * c : PACK * (c + step)],
-                )
-            return codes, plane
+        d_q = [
+            (at(D_CODES + 5 * g, "d%d_codes" % g, [P, 2 * M], U32), at(D_CODES + 5 * g + 4, "d%d_plane" % g, [P, 2 * M], U8))
+            for g in range(R_PASSES)
+        ]
 
-        def both_halves(g, b, last_signed):
-            picked = [
-                pick_columns(g, half * HALF, range(PACK), ring.tile([P, PACK, HALF], F32, name="picked", bufs=4))
-                for half in range(2)
-            ]
-            diff = [subtract(b[half], picked[half]) for half in range(2)]
-            signed = [split_signs(diff[0], signed_tile(HALF)), split_signs(diff[1], last_signed)]
-            return [quantise_signed("d%d%d" % (g, half), signed[half], 1) for half in range(2)]
+        h = [summary_features(0)]
+        b = [ledger_features(0, c, 4 + c) for c in range(4)]
+        h.append(summary_features(1))
+        h.append(summary_features(2))
+        staged = [round_weight("w2_%d" % g, w2_raw[g], TURN + 4 * (g - 1), True) for g in (1, 2)]
+        wo_raw.append(load_weight(3, "wo11", wo, 1, 1))
+        picked = at(LAND + 8, "picked0", [P, PACK, M], F32)
+        pick_columns(0, 0, range(PACK), picked)
+        diff = at(DIFF, "diff0", [P, M * PACK], BF16)
+        subtract(b, picked, diff)
+        wo_raw.append(load_weight(1, "wo20", wo, 2, 0))
+        wo_raw.append(load_weight(4, "wo21", wo, 2, 1))
+        signed = split_signs("d0", diff[:], TURN + 8)
+        w2_q.append(quantise_weight("w2_1", 1, staged[0], DIFF))
+        quantise_signed(0, 0, signed)
+        w2_q.append(quantise_weight("w2_2", 2, staged[1], DIFF + 1))
 
-        def score_weights(g):
-            wo_q.append(
-                [
-                    quantise_weight(
-                        "wo%d%d" % (g, n),
-                        load_weight(WO_BERTHS[g][n], wo, g, n),
-                        berth("wu2", "staged", [P, PASS * PACK], BF16) if (g, n) == (1, 0) else None,
-                    )
-                    for n in range(N_GROUPS)
-                ]
-            )
-            raw = berth("pass%d" % g, "wu_raw", [P, N], I32)
-            load_words(raw, wu_words[g])
-            codes = berth("wu%d" % g, "wu_codes", [P, N], I32)
-            nc.gpsimd.tensor_copy(
-                out=codes[:].rearrange("p (n t m) -> p n t m", t=PACK, m=P),
-                in_=raw[:].rearrange("p (n m t) -> p n t m", t=PACK, m=P),
-            )
-            wu_codes.append(codes)
+        b = [ledger_features(1, c, 4 + c) for c in range(4)]
+        wu_planes = at(TURN + 12, "wu_planes", [P, N], U8)
+        deal(nc.gpsimd, wu_planes[:], wu_raw_planes[:])
+        wu_codes = at(TURN, "wu_codes", [P, R_PASSES, N], I32)
+        for g in range(R_PASSES):
+            deal(nc.gpsimd, wu_codes[:, g, :], wu_raw[:, g, :])
+        picked = at(TURN + 13, "picked1", [P, PACK, M], F32)
+        pick_columns(1, 0, range(PACK), picked)
+        diff = at(DIFF + 4, "diff1", [P, M * PACK], BF16)
+        subtract(b, picked, diff)
+        staged = [round_weight("wo%d" % i, wo_raw[i], STAGE + 4 * (i % 4), False) for i in range(4)]
+        signed = split_signs("d1", diff[:], TURN + 13)
+        wo_q = [quantise_weight("wo0", 3, staged[0], DIFF + 4)]
+        quantise_signed(1, 0, signed)
+        for i in range(1, 4):
+            wo_q.append(quantise_weight("wo%d" % i, 3 + i, staged[i], DIFF + 4 + i))
+        staged_last = [round_weight("wo%d" % i, wo_raw[i], STAGE + 4 * (i % 4), False) for i in (4, 5)]
 
-        def score_bank(number, slices):
-            return bank(number, "y_acc", [P, slices, BANK // slices])
-
-        def add_pass(g, d_q, first, acc, n, first_slice, closes):
-            d_codes, d_plane = d_q
+        def add_pass(g, first, acc, n, first_slice, sides, closes):
             slices, width = acc.shape[1], acc.shape[2]
-            above = slice(first, first + width)
-            below = slice(d_codes.shape[1] // 2 + first, d_codes.shape[1] // 2 + first + width)
-            for u in range(slices):
-                t = first_slice + u
-                nc.tensor.matmul_mx(
-                    out=acc[:, u, :],
-                    lhsT=wo_q[g][n][0][:, P * t : P * (t + 1)].bitcast(FP8X4),
-                    lhsT_scale=wo_q[g][n][1][:, P * t : P * (t + 1)],
-                    rhs=d_codes[:, above].bitcast(FP8X4),
-                    rhs_scale=d_plane[:, above],
-                    start=(g == 0 and u == 0),
-                    stop=False,
-                )
-                cols = slice(n * PASS + P * t, n * PASS + P * (t + 1))
-                nc.tensor.matmul_mx(
-                    out=acc[:, u, :],
-                    lhsT=wu_codes[g][:, cols].bitcast(FP8X4),
-                    lhsT_scale=wu_planes[4 * g : P, cols],
-                    rhs=d_codes[:, below].bitcast(FP8X4),
-                    rhs_scale=d_plane[:, below],
-                    start=False,
-                    stop=(closes and u == slices - 1),
-                )
+            for side in sides:
+                cols = slice(side * M + first, side * M + first + width)
+                for u in range(slices):
+                    t = first_slice + u
+                    if side == 0:
+                        codes = wo_q[2 * g + n][0][:, P * t : P * (t + 1)]
+                        plane = wo_q[2 * g + n][1][:, P * t : P * (t + 1)]
+                    else:
+                        codes = wu_codes[:, g, n * PASS + P * t : n * PASS + P * (t + 1)]
+                        plane = wu_planes[4 * g : P, n * PASS + P * t : n * PASS + P * (t + 1)]
+                    nc.tensor.matmul_mx(
+                        out=acc[:, u, :],
+                        lhsT=codes.bitcast(FP8X4),
+                        lhsT_scale=plane,
+                        rhs=d_q[g][0][:, cols].bitcast(FP8X4),
+                        rhs_scale=d_q[g][1][:, cols],
+                        start=(g == 0 and side == 0 and u == 0),
+                        stop=(closes and side == 1 and u == slices - 1),
+                    )
 
-        def scores(n, first, sums):
-            width = sums[0].shape[1]
-            count = N_GROUPS * HALF // width
-            y = ring.tile([P, PACK, width], F32, name="y%d" % width, bufs=count)
+        def scale_scores(n, first, sums, y):
             for t in range(PACK):
                 nc.scalar.activation(out=y[:, t, :], in_=sums[t], func=COPY, scale=gains[:, n, t : t + 1])
-            rows = out_0[n * PASS : (n + 1) * PASS, first : first + width]
-            nc.sync.dma_start(out=rows.rearrange("(p t) m -> p t m", t=PACK), in_=y[:])
-            return y
 
-        def round_scores(y, copy):
-            width = y.shape[2]
-            rounded = ring.tile(
-                [P, width * PACK], BF16, name="rounded%d" % width, bufs=N_GROUPS * HALF // width, align_bytes=MX_ALIGN
-            )
+        def store_scores(queue, n, first, y):
+            rows = out_0[n * PASS : (n + 1) * PASS, first : first + y.shape[2]]
+            queue.dma_start(out=rows.rearrange("(p t) m -> p t m", t=PACK), in_=y[:])
+
+        def round_scores(copy, rounded, y):
             copy(
-                out=rounded[:].rearrange("p (c i t) -> p c t i", i=4, t=PACK),
+                out=rounded.rearrange("p (c i t) -> p c t i", i=4, t=PACK),
                 in_=y[:].rearrange("p t (c i) -> p c t i", i=4),
             )
             return rounded
 
         def quantise_scores(n, first, rounded):
             cols = slice(first, first + rounded.shape[1] // PACK)
-            nc.vector.quantize_mx(out=y_codes[:, n, cols].bitcast(FP8X4), scales=y_plane[:, n, cols], in_=rounded[:])
+            nc.vector.quantize_mx(out=y_codes[:, n, cols].bitcast(FP8X4), scales=y_plane[:, n, cols], in_=rounded)
 
-        def paired_rows(place):
-            pair = berth(place, "h_pair", [P, 2, S], F32)
-            return [pair[:, 0, :], pair[:, 1, :]] + summary_rows(2)
-
-        w2_q = [quantise_weight("w2_0", w2_first)]
-        h = [summary_features(0, paired_rows(W2_BERTHS[0]), 0)]
-        b = [ledger_features(0, 0, 0), ledger_features(0, 1, 2)]
-        w2_q.append(quantise_weight("w2_1", load_weight(W2_BERTHS[1], w2, 0, 1)))
-        h.append(summary_features(1, paired_rows(W2_BERTHS[1]), 4))
-        h.append(summary_features(2, summary_rows(PACK), 4))
-        d_q = [both_halves(0, b, berth("wu0", "signed", [P, 2 * HALF * PACK], BF16))]
-        w2_q.append(quantise_weight("w2_2", load_weight(W2_BERTHS[2], w2, 0, 2)))
-        b = [ledger_features(1, 0, 4), ledger_features(1, 1, 6)]
-        b_last = ledger_features(LAST, 0, 0)
-        d_q.append(both_halves(1, b, signed_tile(HALF)))
-
-        wu_raw_planes = berth("g", "wu_raw_planes", [P, N], U8)
-        nc.vector.memset(wu_raw_planes[:].bitcast(I32), 0)
-        for q in range(QUADRANTS):
-            nc.sync.dma_start(
-                out=wu_raw_planes[32 * q : 32 * q + 4 * R_PASSES, :].bitcast(I32),
-                in_=wu_scales[:, 4 * q : 4 * q + 4, :].bitcast(I32),
-            )
-        wu_planes = kept("wu_planes", [P, N], U8)
-        deal_plane(wu_planes, wu_raw_planes)
-
-        wo_q, wu_codes = [], []
-        banks0 = [score_bank(2 + i, 2) for i in range(2 * N_GROUPS)]
-
-        def add_half_pass(g, d_half):
+        b = [ledger_features(2, c, 4 + c) for c in range(2)]
+        banks0 = [bank(i, "y0_acc%d" % i, [P, 2, HALF]) for i in range(4)]
+        banks2 = [bank(6 + n, "y2_acc%d" % n, [P, PACK, CHUNK]) for n in range(N_GROUPS)]
+        for g in range(2):
             for i, acc in enumerate(banks0):
-                add_pass(g, d_half, 0, acc, i // 2, 2 * (i % 2), g == LAST)
-
-        for g in range(LAST):
-            score_weights(g)
-            add_half_pass(g, d_q[g][0])
-        score_weights(LAST)
-        picked = berth(WO_BERTHS[1][0], "picked", [P, PACK, HALF], F32)
-        diff = subtract(b_last, pick_columns(LAST, 0, range(PACK), picked))
-        b_last = ledger_features(LAST, 1, 0)
-        d_last = quantise_signed("d20", split_signs(diff, signed_tile(HALF)), 1)
-
-        banks1 = [[score_bank(6 + n, PACK) for n in range(N_GROUPS)]]
-        for g in range(LAST):
+                add_pass(g, 0, acc, i // 2, 2 * (i % 2), (0, 1), False)
             for n in range(N_GROUPS):
-                add_pass(g, d_q[g][1], 0, banks1[0][n], n, 0, False)
-        add_half_pass(LAST, d_last)
-        y = [scores(n, 0, [banks0[2 * n + t // 2][:, t % 2, :] for t in range(PACK)]) for n in range(N_GROUPS)]
-        rounded = [round_scores(y[n], nc.scalar.copy) for n in range(N_GROUPS)]
-        banks1.append([score_bank(2 + n, PACK) for n in range(N_GROUPS)])
+                add_pass(g, HALF, banks2[n], n, 0, (0, 1), False)
+        picked = at(STAGE + 12, "picked2", [P, PACK, HALF], F32)
+        pick_columns(2, 0, range(PACK), picked)
+        diff = at(DIFF + 8, "diff2", [P, M * PACK], BF16)
+        subtract(b, picked, diff)
+        b = [ledger_features(2, 2 + c, 4 + c) for c in range(2)]
+        wo_q.append(quantise_weight("wo4", 7, staged_last[0], W2_PLANE + 0.5))
+        signed = split_signs("d20", diff[:, 0 : 2 * BANK], LAST)
+        wo_q.append(quantise_weight("wo5", 8, staged_last[1], W2_PLANE + 1))
+        quantise_signed(2, 0, signed)
+        for i, acc in enumerate(banks0):
+            add_pass(2, 0, acc, i // 2, 2 * (i % 2), (0, 1), True)
+        y0 = [at(H_ROWS + 4 * n, "y0%d" % n, [P, PACK, HALF], F32) for n in range(N_GROUPS)]
         for n in range(N_GROUPS):
-            for g in range(LAST):
-                add_pass(g, d_q[g][1], CHUNK, banks1[1][n], n, 0, False)
+            scale_scores(n, 0, [banks0[2 * n + t // 2][:, t % 2, :] for t in range(PACK)], y0[n])
+            store_scores(nc.sync, n, 0, y0[n])
 
-        picked = berth(WO_BERTHS[LAST][1], "picked", [P, 2, PACK, CHUNK], F32)
-        pick_columns(LAST, HALF, range(PACK), picked[:, 0])
-        pick_columns(LAST, HALF + CHUNK, range(1), picked[:, 1])
-        diff = subtract(b_last[0:1], picked[:, 0])
-        pick_columns(LAST, HALF + CHUNK, range(1, PACK), picked[:, 1])
-        signed = split_signs(diff, signed_tile(CHUNK))
-        diff = subtract(b_last[1:2], picked[:, 1])
-        d_last = quantise_signed("d21a", signed, 1)
+        picked = at(STAGE + 4, "picked3", [P, 2, PACK, CHUNK], F32)
+        pick_columns(2, HALF, range(PACK), picked[:, 0])
+        pick_columns(2, HALF + CHUNK, range(1), picked[:, 1])
+        subtract(b[0:1], picked[:, 0], diff[:, 2 * BANK : 3 * BANK])
+        pick_columns(2, HALF + CHUNK, range(1, PACK), picked[:, 1])
+        signed = split_signs("d22", diff[:, 2 * BANK : 3 * BANK], LAST + 4)
+        subtract(b[1:2], picked[:, 1], diff[:, 3 * BANK : 4 * BANK])
+        quantise_signed(2, HALF, signed)
+        banks3 = [bank(4 + n, "y3_acc%d" % n, [P, PACK, CHUNK]) for n in range(N_GROUPS)]
+        for g in range(2):
+            add_pass(g, HALF + CHUNK, banks3[0], 0, 0, (0, 1), False)
         for n in range(N_GROUPS):
-            add_pass(LAST, d_last, 0, banks1[0][n], n, 0, True)
-        signed = split_signs(diff, berth("i", "signed", [P, 2 * CHUNK * PACK], BF16))
-        d_last = quantise_signed("d21b", signed, 2)
-        for n in range(N_GROUPS):
-            add_pass(LAST, d_last, 0, banks1[1][n], n, 0, True)
+            add_pass(2, HALF, banks2[n], n, 0, (0, 1), True)
+        for g in range(2):
+            add_pass(g, HALF + CHUNK, banks3[1], 1, 0, (0, 1), False)
+        signed = split_signs("d23", diff[:, 3 * BANK : 4 * BANK], LAST + 6)
+        quantise_signed(2, HALF + CHUNK, signed)
+        for side in range(2):
+            for n in range(N_GROUPS):
+                add_pass(2, HALF + CHUNK, banks3[n], n, 0, (side,), True)
 
-        y_codes = berth("i", "y_codes", [P, N_GROUPS, M], U32)
-        y_plane = kept("y_plane", [P, N_GROUPS, M], U8)
+        y2 = [at(H_ROWS + 8 + 2 * n, "y2%d" % n, [P, PACK, CHUNK], F32) for n in range(N_GROUPS)]
+        y3 = [at(H_ROWS + 12 + 2 * n, "y3%d" % n, [P, PACK, CHUNK], F32) for n in range(N_GROUPS)]
+        for n in range(N_GROUPS):
+            scale_scores(n, HALF, [banks2[n][:, t, :] for t in range(PACK)], y2[n])
+            store_scores(nc.sync, n, HALF, y2[n])
+        scale_scores(0, HALF + CHUNK, [banks3[0][:, t, :] for t in range(PACK)], y3[0])
+        store_scores(nc.scalar, 0, HALF + CHUNK, y3[0])
+
+        y_codes = at(H_ROWS + 24, "y_codes", [P, N_GROUPS, M], U32)
+        y_plane = at(H_ROWS + 28, "y_plane", [P, N_GROUPS, M], U8)
         out_words = out_1.rearrange("g p m t -> p g (m t)").bitcast(I32)
+        both = at(LAST + 4, "r0", [P, N_GROUPS, HALF * PACK], BF16)
+        rounded = [round_scores(nc.vector.tensor_copy, both[:, n, :], y0[n]) for n in range(N_GROUPS)]
         for n in range(N_GROUPS):
             quantise_scores(n, 0, rounded[n])
-            nc.sync.dma_start(out=out_words[:, n, 0:HALF], in_=y_codes[:, n, 0:HALF].bitcast(I32))
-        for c in range(HALF // CHUNK):
-            first = HALF + c * CHUNK
-            rounded = [
-                round_scores(scores(n, first, [banks1[c][n][:, t, :] for t in range(PACK)]), nc.vector.tensor_copy)
-                for n in range(N_GROUPS)
-            ]
-            for n in range(N_GROUPS):
-                quantise_scores(n, first, rounded[n])
+        nc.sync.dma_start(out=out_words[:, :, 0:HALF], in_=y_codes[:, :, 0:HALF].bitcast(I32))
+        nc.vector.tensor_tensor(
+            out=y3[1][:], in0=banks3[1][:], in1=gains[:, 1, :].unsqueeze(2).to_broadcast([P, PACK, CHUNK]), op=MULT
+        )
+        store_scores(nc.sync, 1, HALF + CHUNK, y3[1])
+        rounded = [
+            round_scores(nc.vector.tensor_copy, at(H_ROWS + 20 + i, "r%d" % (i + 2), [P, BANK], BF16)[:], y)
+            for i, y in enumerate(y2 + y3)
+        ]
+        for i in range(4):
+            quantise_scores(i % 2, HALF + CHUNK * (i // 2), rounded[i])
         nc.scalar.dma_start(out=out_words[:, :, HALF:M], in_=y_codes[:, :, HALF:M].bitcast(I32))
         for q in range(QUADRANTS):
             queue = nc.scalar if q % 2 else nc.sync

@@ -40,9 +40,10 @@ W_CODES = 131
 D_CODES = 149
 DIFF = 164
 STAGE = 176
-TURN = 192
-LAST = 213
-W2_PLANE = 221
+ABOVE = 197
+BELOW = 207
+LAST = 215
+W2_PLANE = 227
 
 
 def tile_list_net_misstatement_scores_kernel(
@@ -82,17 +83,19 @@ def tile_list_net_misstatement_scores_kernel(
             nc.sync.dma_start(out=raw[:], in_=rows.rearrange("(p j) c -> p j c", j=PACK))
             return raw
 
-        def round_weight(name, raw, kb, on_gpsimd):
-            staged = at(kb, name + "_staged", [P, PASS * PACK], BF16)
+        def stage(name, kb):
+            return at(kb, name + "_staged", [P, PASS * PACK], BF16)[:]
+
+        def round_weight(raw, staged, on_gpsimd):
             if on_gpsimd:
                 nc.gpsimd.tensor_scalar(
-                    out=staged[:].rearrange("p (t m j) -> p m t j", t=PACK, j=PACK),
+                    out=staged.rearrange("p (t m j) -> p m t j", t=PACK, j=PACK),
                     in0=raw[:].rearrange("p j (m t) -> p m t j", t=PACK),
                     scalar1=1.0, scalar2=0.0, op0=MULT, op1=ADD,
                 )
             else:
                 nc.scalar.copy(
-                    out=staged[:].rearrange("p (t m j) -> p m j t", t=PACK, j=PACK),
+                    out=staged.rearrange("p (t m j) -> p m j t", t=PACK, j=PACK),
                     in_=raw[:].rearrange("p j (m t) -> p m j t", t=PACK),
                 )
             return staged
@@ -100,7 +103,7 @@ def tile_list_net_misstatement_scores_kernel(
         def quantise_weight(name, number, staged, plane_kb):
             codes = at(W_CODES + 2 * number, name + "_codes", [P, PASS], U32)
             plane = at(plane_kb, name + "_plane", [P, PASS], U8)
-            nc.vector.quantize_mx(out=codes[:].bitcast(FP8X4), scales=plane[:], in_=staged[:])
+            nc.vector.quantize_mx(out=codes[:].bitcast(FP8X4), scales=plane[:], in_=staged)
             return codes, plane
 
         idx = keep.tile([P, S // LIST], U16, name="idx")
@@ -111,24 +114,24 @@ def tile_list_net_misstatement_scores_kernel(
         w1_raw_plane = at(W1_RAW_PLANE, "w1_raw_plane", [P, H], U8)
         tab2_plane = at(TAB2_PLANE, "tab2_plane", [P, T], U8)
         wu_raw_planes = at(WU_RAW_PLANES, "wu_raw_planes", [P, N], U8)
-        nc.vector.memset(tab_plane[:].bitcast(I32), 0)
-        nc.vector.memset(w1_raw_plane[:].bitcast(I32), 0)
-        nc.vector.memset(tab2_plane[:].bitcast(I32), 0)
-        nc.vector.memset(wu_raw_planes[:].bitcast(I32), 0)
+        for engine, plane in (
+            (nc.gpsimd, tab_plane), (nc.vector, w1_raw_plane), (nc.vector, tab2_plane), (nc.gpsimd, wu_raw_planes)
+        ):
+            engine.memset(plane[:].bitcast(I32), 0)
 
         nc.sync.dma_start(idx[:], offs)
         w1_raw = at(W1_RAW, "w1_raw", [P, 2 * H], U8)
         nc.sync.dma_start(out=w1_raw[:].bitcast(I32), in_=w1_words[0].bitcast(I32))
         load_plane(nc.sync, tab_plane, tab_scales[0])
-        nc.sync.dma_start(idx2[:], offs2)
-        w2_raw = [load_weight(2, "w2_0", w2, 0, 0)]
-        load_plane(nc.scalar, w1_raw_plane, w1_scales[0])
         tab = at(LAND, "tab", [P, T], I32)
         load_words(tab, tab_words[0])
-        load_plane(nc.sync, tab2_plane, tab2_scales[0])
+        nc.sync.dma_start(idx2[:], offs2)
+        load_plane(nc.sync, w1_raw_plane, w1_scales[0])
         tab2 = at(LAND + 8, "tab2", [P, T], I32)
         load_words(tab2, tab2_words[0])
+        load_plane(nc.sync, tab2_plane, tab2_scales[0])
         nc.sync.dma_start(pick[:], pos1)
+        w2_raw = [load_weight(2, "w2_0", w2, 0, 0)]
         w2_raw.append(load_weight(3, "w2_1", w2, 0, 1))
         w2_raw.append(load_weight(4, "w2_2", w2, 0, 2))
         wo_raw = [load_weight(5, "wo00", wo, 0, 0)]
@@ -141,36 +144,43 @@ def tile_list_net_misstatement_scores_kernel(
         wu_raw = at(WU_RAW, "wu_raw", [P, R_PASSES, N], I32)
         nc.sync.dma_start(out=wu_raw[:], in_=wu_words.rearrange("a p c i -> p a (c i)").bitcast(I32))
 
+        w1_codes = [at(W1_CODES + g, "w1_codes%d" % g, [P, 2 * PASS], U8) for g in range(R_PASSES)]
+        w1_plane = [at(W1_PLANE + g / 2, "w1_plane%d" % g, [P, PASS], U8) for g in range(R_PASSES)]
+        deal(nc.vector, w1_codes[0][:].bitcast(U16), w1_raw[:, 0 : 2 * PASS].bitcast(U16))
+        for g in range(R_PASSES):
+            deal(nc.gpsimd, w1_plane[g][:], w1_raw_plane[:, g * PASS : (g + 1) * PASS])
+        for g in range(1, R_PASSES):
+            nc.gpsimd.tensor_copy(
+                out=w1_codes[g][:].rearrange("p (t m b) -> p t m b", t=PACK, b=2),
+                in_=w1_raw[:, 2 * PASS * g : 2 * PASS * (g + 1)].rearrange("p (m t b) -> p t m b", t=PACK, b=2),
+            )
         v_plane = at(V_PLANE, "v_plane", [P, S], U8)
         nc.vector.tensor_copy(out=v_plane[:], in_=tab_plane[:].indirect(idx[:]))
-        w1_codes = at(W1_CODES, "w1_codes", [P, 2 * H], U8)
-        deal(nc.vector, w1_codes[:].bitcast(U16), w1_raw[:].bitcast(U16))
-        w1_plane = at(W1_PLANE, "w1_plane", [P, H], U8)
-        deal(nc.vector, w1_plane[:], w1_raw_plane[:])
         v_codes = []
         for s in range(S // BANK):
             codes = at(V_CODES + 2 * s, "v_codes%d" % s, [P, BANK], U32)
             offsets = idx[:, s * BANK // LIST : (s + 1) * BANK // LIST]
             nc.vector.tensor_copy(out=codes[:], in_=tab[:].bitcast(U32).indirect(offsets))
             v_codes.append(codes)
-        v2_plane = at(V2_PLANE, "v2_plane", [P, M], U8)
-        nc.vector.tensor_copy(out=v2_plane[:], in_=tab2_plane[:].indirect(idx2[:]))
-        w2_q = [quantise_weight("w2_0", 0, round_weight("w2_0", w2_raw[0], STAGE, False), W2_PLANE)]
         v2_codes = at(V2_CODES, "v2_codes", [P, M], U32)
         nc.vector.tensor_copy(out=v2_codes[:], in_=tab2[:].bitcast(U32).indirect(idx2[:]))
-        wo_raw.append(load_weight(2, "wo01", wo, 0, 1))
-        wo_raw.append(load_weight(0, "wo10", wo, 1, 0))
+        v2_plane = at(V2_PLANE, "v2_plane", [P, M], U8)
+        nc.vector.tensor_copy(out=v2_plane[:], in_=tab2_plane[:].indirect(idx2[:]))
+        first = at(LAST, "first", [P, 6 * M], F32)
+        staged = round_weight(w2_raw[0], first[:, 3 * M : 5 * M].bitcast(BF16), True)
+        w2_q = [quantise_weight("w2_0", 0, staged, W2_PLANE)]
+        wo_raw.append(load_weight(0, "wo01", wo, 0, 1))
+        wo_raw.append(load_weight(1, "wo10", wo, 1, 0))
 
         def summary_features(g):
             rows = [at(H_ROWS + 4 * (PACK * g + t), "h%d%d" % (g, t), [P, S], F32) for t in range(PACK)]
             for t in range(PACK):
                 for s in range(S // BANK):
-                    acc = bank((2 * t + s) % 4, "h_acc", [P, BANK])
-                    cols = slice(g * PASS + P * t, g * PASS + P * (t + 1))
+                    acc = bank((2 * t + s) % 4 + (4 if g > 0 and t < 2 else 0), "h_acc", [P, BANK])
                     nc.tensor.matmul_mx(
                         out=acc[:],
-                        lhsT=w1_codes[:, 2 * cols.start : 2 * cols.stop].bitcast(FP4X4),
-                        lhsT_scale=w1_plane[:, cols],
+                        lhsT=w1_codes[g][:, 2 * P * t : 2 * P * (t + 1)].bitcast(FP4X4),
+                        lhsT_scale=w1_plane[g][:, P * t : P * (t + 1)],
                         rhs=v_codes[s][:].bitcast(FP8X4),
                         rhs_scale=v_plane[:, s * BANK : (s + 1) * BANK],
                         start=True,
@@ -200,6 +210,12 @@ def tile_list_net_misstatement_scores_kernel(
             for t in slices:
                 nc.vector.tensor_copy(out=picked[:, t, :], in_=h[g][t][:].indirect(offsets))
 
+        def pick_all(g, first, picked):
+            half = picked.shape[2] // 2
+            pick_columns(g, first, range(PACK - 1), picked)
+            for part in range(2):
+                pick_columns(g, first + part * half, [PACK - 1], picked[:, :, part * half : (part + 1) * half])
+
         def subtract(banks, picked, diff):
             for c, acc in enumerate(banks):
                 nc.vector.tensor_tensor(
@@ -209,16 +225,18 @@ def tile_list_net_misstatement_scores_kernel(
                     op=SUBTRACT,
                 )
 
-        def split_signs(name, diff, kb):
+        def split_signs(name, diff, kb, below_kb, parts):
             width = diff.shape[1]
             above = at(kb, name + "_above", [P, width], BF16)
-            below = at(kb + 2 * width / KB, name + "_below", [P, width], BF16)
-            nc.vector.tensor_scalar_max(out=above[:], in0=diff, scalar1=0.0)
-            nc.vector.tensor_scalar_min(out=below[:], in0=diff, scalar1=0.0)
+            below = at(below_kb, name + "_below", [P, width], BF16)
+            for c in range(0, width, width // parts):
+                cols = slice(c, c + width // parts)
+                nc.vector.tensor_scalar_min(out=below[:, cols], in0=diff[:, cols], scalar1=0.0)
+                nc.vector.tensor_scalar_max(out=above[:, cols], in0=diff[:, cols], scalar1=0.0)
             return above, below
 
         def quantise_signed(g, first, signed):
-            for side in range(2):
+            for side in (1, 0):
                 words = signed[side].shape[1] // PACK
                 cols = slice(side * M + first, side * M + first + words)
                 nc.vector.quantize_mx(out=d_q[g][0][:, cols].bitcast(FP8X4), scales=d_q[g][1][:, cols], in_=signed[side][:])
@@ -229,39 +247,44 @@ def tile_list_net_misstatement_scores_kernel(
         ]
 
         h = [summary_features(0)]
-        b = [ledger_features(0, c, 4 + c) for c in range(4)]
         h.append(summary_features(1))
+        b = [ledger_features(0, c, c) for c in range(4)]
         h.append(summary_features(2))
-        staged = [round_weight("w2_%d" % g, w2_raw[g], TURN + 4 * (g - 1), True) for g in (1, 2)]
-        wo_raw.append(load_weight(3, "wo11", wo, 1, 1))
-        picked = at(LAND + 8, "picked0", [P, PACK, M], F32)
-        pick_columns(0, 0, range(PACK), picked)
+        staged = round_weight(w2_raw[1], first[:, 4 * M : 6 * M].bitcast(BF16), True)
+        wo_raw.append(load_weight(2, "wo11", wo, 1, 1))
+        picked = first[:, 0 : 4 * M].rearrange("p (t c) -> p t c", t=PACK)
+        pick_all(0, 0, picked)
         diff = at(DIFF, "diff0", [P, M * PACK], BF16)
         subtract(b, picked, diff)
-        wo_raw.append(load_weight(1, "wo20", wo, 2, 0))
-        wo_raw.append(load_weight(4, "wo21", wo, 2, 1))
-        signed = split_signs("d0", diff[:], TURN + 8)
-        w2_q.append(quantise_weight("w2_1", 1, staged[0], DIFF))
+        wo_raw.append(load_weight(3, "wo20", wo, 2, 0))
+        signed = split_signs("d0", diff[:], ABOVE, BELOW, 2)
+        w2_q.append(quantise_weight("w2_1", 1, staged, DIFF))
         quantise_signed(0, 0, signed)
-        w2_q.append(quantise_weight("w2_2", 2, staged[1], DIFF + 1))
 
         b = [ledger_features(1, c, 4 + c) for c in range(4)]
-        wu_planes = at(TURN + 12, "wu_planes", [P, N], U8)
+        wu_planes = at(ABOVE + 1, "wu_planes", [P, N], U8)
         deal(nc.gpsimd, wu_planes[:], wu_raw_planes[:])
-        wu_codes = at(TURN, "wu_codes", [P, R_PASSES, N], I32)
-        for g in range(R_PASSES):
-            deal(nc.gpsimd, wu_codes[:, g, :], wu_raw[:, g, :])
-        picked = at(TURN + 13, "picked1", [P, PACK, M], F32)
-        pick_columns(1, 0, range(PACK), picked)
+        wu_first = at(ABOVE + 2, "wu_first", [P, N], I32)
+        deal(nc.gpsimd, wu_first[:], wu_raw[:, 0, :])
+        wu_codes = [wu_first[:]]
+        staged_w2 = round_weight(w2_raw[2], stage("w2_2", ABOVE - 3), True)
+        wo_raw.append(load_weight(4, "wo21", wo, 2, 1))
+        picked = at(BELOW, "picked1", [P, PACK, M], F32)
+        pick_all(1, 0, picked)
         diff = at(DIFF + 4, "diff1", [P, M * PACK], BF16)
         subtract(b, picked, diff)
-        staged = [round_weight("wo%d" % i, wo_raw[i], STAGE + 4 * (i % 4), False) for i in range(4)]
-        signed = split_signs("d1", diff[:], TURN + 13)
-        wo_q = [quantise_weight("wo0", 3, staged[0], DIFF + 4)]
+        staged = [round_weight(wo_raw[i], stage("wo%d" % i, STAGE + 4 * (i % 4)), False) for i in range(4)]
+        signed = split_signs("d1", diff[:], BELOW, BELOW + 4, 2)
+        wo_q = [quantise_weight("wo%d" % i, 3 + i, staged[i], DIFF + 4 + i / 2) for i in range(2)]
+        w2_q.append(quantise_weight("w2_2", 2, staged_w2, DIFF + 5))
         quantise_signed(1, 0, signed)
-        for i in range(1, 4):
-            wo_q.append(quantise_weight("wo%d" % i, 3 + i, staged[i], DIFF + 4 + i))
-        staged_last = [round_weight("wo%d" % i, wo_raw[i], STAGE + 4 * (i % 4), False) for i in (4, 5)]
+        for i in range(2, 4):
+            wo_q.append(quantise_weight("wo%d" % i, 3 + i, staged[i], DIFF + 4.5 + i / 2))
+        wu_last = at(STAGE + 7, "wu_last", [P, 2, N], I32)
+        for g in range(1, R_PASSES):
+            deal(nc.gpsimd, wu_last[:, g - 1, :], wu_raw[:, g, :])
+            wu_codes.append(wu_last[:, g - 1, :])
+        staged_last = [round_weight(wo_raw[i], stage("wo%d" % i, (STAGE, LAST + 8)[i - 4]), False) for i in (4, 5)]
 
         def add_pass(g, first, acc, n, first_slice, sides, closes):
             slices, width = acc.shape[1], acc.shape[2]
@@ -273,7 +296,7 @@ def tile_list_net_misstatement_scores_kernel(
                         codes = wo_q[2 * g + n][0][:, P * t : P * (t + 1)]
                         plane = wo_q[2 * g + n][1][:, P * t : P * (t + 1)]
                     else:
-                        codes = wu_codes[:, g, n * PASS + P * t : n * PASS + P * (t + 1)]
+                        codes = wu_codes[g][:, n * PASS + P * t : n * PASS + P * (t + 1)]
                         plane = wu_planes[4 * g : P, n * PASS + P * t : n * PASS + P * (t + 1)]
                     nc.tensor.matmul_mx(
                         out=acc[:, u, :],
@@ -281,8 +304,8 @@ def tile_list_net_misstatement_scores_kernel(
                         lhsT_scale=plane,
                         rhs=d_q[g][0][:, cols].bitcast(FP8X4),
                         rhs_scale=d_q[g][1][:, cols],
-                        start=(g == 0 and side == 0 and u == 0),
-                        stop=(closes and side == 1 and u == slices - 1),
+                        start=(g == 0 and side == 1 and u == 0),
+                        stop=(closes and side == sides[-1] and u == slices - 1),
                     )
 
         def scale_scores(n, first, sums, y):
@@ -308,17 +331,21 @@ def tile_list_net_misstatement_scores_kernel(
         banks0 = [bank(i, "y0_acc%d" % i, [P, 2, HALF]) for i in range(4)]
         banks2 = [bank(6 + n, "y2_acc%d" % n, [P, PACK, CHUNK]) for n in range(N_GROUPS)]
         for g in range(2):
-            for i, acc in enumerate(banks0):
-                add_pass(g, 0, acc, i // 2, 2 * (i % 2), (0, 1), False)
-            for n in range(N_GROUPS):
-                add_pass(g, HALF, banks2[n], n, 0, (0, 1), False)
-        picked = at(STAGE + 12, "picked2", [P, PACK, HALF], F32)
-        pick_columns(2, 0, range(PACK), picked)
+            for side in (1 - g, g):
+                for i, acc in enumerate(banks0):
+                    add_pass(g, 0, acc, i // 2, 2 * (i % 2), (side,), False)
+                for n in range(N_GROUPS):
+                    add_pass(g, HALF, banks2[n], n, 0, (side,), False)
+        picked = at(STAGE + 15, "picked2", [P, PACK, HALF], F32)
+        pick_all(2, 0, picked)
         diff = at(DIFF + 8, "diff2", [P, M * PACK], BF16)
         subtract(b, picked, diff)
-        b = [ledger_features(2, 2 + c, 4 + c) for c in range(2)]
+        b = ledger_features(2, 2, 4)
+        banks3 = [bank(5, "y3_acc0", [P, PACK, CHUNK])]
+        for g in range(2):
+            add_pass(g, HALF + CHUNK, banks3[0], 0, 0, (1, 0), False)
         wo_q.append(quantise_weight("wo4", 7, staged_last[0], W2_PLANE + 0.5))
-        signed = split_signs("d20", diff[:, 0 : 2 * BANK], LAST)
+        signed = split_signs("d20", diff[:, 0 : 2 * BANK], LAST, LAST + 2, 2)
         wo_q.append(quantise_weight("wo5", 8, staged_last[1], W2_PLANE + 1))
         quantise_signed(2, 0, signed)
         for i, acc in enumerate(banks0):
@@ -327,27 +354,28 @@ def tile_list_net_misstatement_scores_kernel(
         for n in range(N_GROUPS):
             scale_scores(n, 0, [banks0[2 * n + t // 2][:, t % 2, :] for t in range(PACK)], y0[n])
             store_scores(nc.sync, n, 0, y0[n])
+        banks3.append(bank(0, "y3_acc1", [P, PACK, CHUNK]))
+        for g in range(2):
+            add_pass(g, HALF + CHUNK, banks3[1], 1, 0, (1, 0), False)
+        rounded0 = [round_scores(nc.scalar.copy, at(H_ROWS + 16, "r00", [P, HALF * PACK], BF16)[:], y0[0])]
 
-        picked = at(STAGE + 4, "picked3", [P, 2, PACK, CHUNK], F32)
-        pick_columns(2, HALF, range(PACK), picked[:, 0])
-        pick_columns(2, HALF + CHUNK, range(1), picked[:, 1])
-        subtract(b[0:1], picked[:, 0], diff[:, 2 * BANK : 3 * BANK])
-        pick_columns(2, HALF + CHUNK, range(1, PACK), picked[:, 1])
-        signed = split_signs("d22", diff[:, 2 * BANK : 3 * BANK], LAST + 4)
-        subtract(b[1:2], picked[:, 1], diff[:, 3 * BANK : 4 * BANK])
+        picked = at(LAST + 8, "picked3", [P, PACK, CHUNK], F32)
+        pick_columns(2, HALF, range(PACK), picked)
+        subtract([b], picked, diff[:, 2 * BANK : 3 * BANK])
+        b = ledger_features(2, 3, 4)
+        signed = split_signs("d22", diff[:, 2 * BANK : 3 * BANK], LAST + 4, LAST + 5, 1)
         quantise_signed(2, HALF, signed)
-        banks3 = [bank(4 + n, "y3_acc%d" % n, [P, PACK, CHUNK]) for n in range(N_GROUPS)]
-        for g in range(2):
-            add_pass(g, HALF + CHUNK, banks3[0], 0, 0, (0, 1), False)
-        for n in range(N_GROUPS):
-            add_pass(2, HALF, banks2[n], n, 0, (0, 1), True)
-        for g in range(2):
-            add_pass(g, HALF + CHUNK, banks3[1], 1, 0, (0, 1), False)
-        signed = split_signs("d23", diff[:, 3 * BANK : 4 * BANK], LAST + 6)
-        quantise_signed(2, HALF + CHUNK, signed)
-        for side in range(2):
+        for side in (1, 0):
             for n in range(N_GROUPS):
-                add_pass(2, HALF + CHUNK, banks3[n], n, 0, (side,), True)
+                add_pass(2, HALF, banks2[n], n, 0, (side,), side == 0)
+        picked = at(LAST + 8, "picked4", [P, PACK, CHUNK], F32)
+        pick_columns(2, HALF + CHUNK, range(PACK), picked)
+        subtract([b], picked, diff[:, 3 * BANK : 4 * BANK])
+        signed = split_signs("d23", diff[:, 3 * BANK : 4 * BANK], LAST + 6, LAST + 7, 1)
+        quantise_signed(2, HALF + CHUNK, signed)
+        for side in (1, 0):
+            for n in range(N_GROUPS):
+                add_pass(2, HALF + CHUNK, banks3[n], n, 0, (side,), side == 0)
 
         y2 = [at(H_ROWS + 8 + 2 * n, "y2%d" % n, [P, PACK, CHUNK], F32) for n in range(N_GROUPS)]
         y3 = [at(H_ROWS + 12 + 2 * n, "y3%d" % n, [P, PACK, CHUNK], F32) for n in range(N_GROUPS)]
@@ -357,13 +385,12 @@ def tile_list_net_misstatement_scores_kernel(
         scale_scores(0, HALF + CHUNK, [banks3[0][:, t, :] for t in range(PACK)], y3[0])
         store_scores(nc.scalar, 0, HALF + CHUNK, y3[0])
 
-        y_codes = at(H_ROWS + 24, "y_codes", [P, N_GROUPS, M], U32)
+        y_codes = at(LAST + 3, "y_codes", [P, N_GROUPS, M], U32)
         y_plane = at(H_ROWS + 28, "y_plane", [P, N_GROUPS, M], U8)
         out_words = out_1.rearrange("g p m t -> p g (m t)").bitcast(I32)
-        both = at(LAST + 4, "r0", [P, N_GROUPS, HALF * PACK], BF16)
-        rounded = [round_scores(nc.vector.tensor_copy, both[:, n, :], y0[n]) for n in range(N_GROUPS)]
+        rounded0.append(round_scores(nc.vector.tensor_copy, at(LAST + 7, "r01", [P, HALF * PACK], BF16)[:], y0[1]))
         for n in range(N_GROUPS):
-            quantise_scores(n, 0, rounded[n])
+            quantise_scores(n, 0, rounded0[n])
         nc.sync.dma_start(out=out_words[:, :, 0:HALF], in_=y_codes[:, :, 0:HALF].bitcast(I32))
         nc.vector.tensor_tensor(
             out=y3[1][:], in0=banks3[1][:], in1=gains[:, 1, :].unsqueeze(2).to_broadcast([P, PACK, CHUNK]), op=MULT

@@ -35,15 +35,18 @@ LAND = 48
 WU_RAW = 96
 W1_RAW, W1_RAW_PLANE, W1_CODES, W1_PLANE = 108, 111, 113, 116
 TAB_PLANE, TAB2_PLANE, WU_RAW_PLANES = 118, 120, 122
-V_CODES, V_PLANE, V2_CODES, V2_PLANE = 123, 127, 128, 130
+V2_CODES, V2_PLANE = 123, 125
+D_PLANE = 126
 W_CODES = 131
 D_CODES = 149
 DIFF = 164
 STAGE = 176
-ABOVE = 197
-BELOW = 207
-LAST = 215
-W2_PLANE = 227
+ABOVE = 198
+BELOW = 204
+LAST = 212
+G_STAGE = 220
+W2_PLANE = 226
+EXTRA = 227
 
 
 def tile_list_net_misstatement_scores_kernel(
@@ -71,10 +74,10 @@ def tile_list_net_misstatement_scores_kernel(
                     out=plane[32 * q : 32 * q + 4, :].bitcast(I32), in_=rows[4 * q : 4 * q + 4, :].bitcast(I32)
                 )
 
-        def deal(engine, dealt, natural):
+        def deal(engine, dealt, natural, run):
             engine.tensor_copy(
-                out=dealt.rearrange("p (g t m) -> p g t m", t=PACK, m=P),
-                in_=natural.rearrange("p (g m t) -> p g t m", t=PACK, m=P),
+                out=dealt.rearrange("p (g t m i) -> p g m t i", t=PACK, m=P // run, i=run),
+                in_=natural.rearrange("p (g m i t) -> p g m t i", t=PACK, m=P // run, i=run),
             )
 
         def load_weight(place, name, w, g, group):
@@ -144,21 +147,21 @@ def tile_list_net_misstatement_scores_kernel(
         wu_raw = at(WU_RAW, "wu_raw", [P, R_PASSES, N], I32)
         nc.sync.dma_start(out=wu_raw[:], in_=wu_words.rearrange("a p c i -> p a (c i)").bitcast(I32))
 
-        w1_codes = [at(W1_CODES + g, "w1_codes%d" % g, [P, 2 * PASS], U8) for g in range(R_PASSES)]
+        w1_codes = [at(kb, "w1_codes", [P, 2 * PASS], U8) for kb in (W1_CODES, W1_CODES + 1, STAGE + 12)]
         w1_plane = [at(W1_PLANE + g / 2, "w1_plane%d" % g, [P, PASS], U8) for g in range(R_PASSES)]
-        deal(nc.vector, w1_codes[0][:].bitcast(U16), w1_raw[:, 0 : 2 * PASS].bitcast(U16))
+        deal(nc.vector, w1_codes[0][:].bitcast(U16), w1_raw[:, 0 : 2 * PASS].bitcast(U16), 8)
         for g in range(R_PASSES):
-            deal(nc.gpsimd, w1_plane[g][:], w1_raw_plane[:, g * PASS : (g + 1) * PASS])
+            deal(nc.gpsimd, w1_plane[g][:], w1_raw_plane[:, g * PASS : (g + 1) * PASS], 16)
         for g in range(1, R_PASSES):
             nc.gpsimd.tensor_copy(
-                out=w1_codes[g][:].rearrange("p (t m b) -> p t m b", t=PACK, b=2),
-                in_=w1_raw[:, 2 * PASS * g : 2 * PASS * (g + 1)].rearrange("p (m t b) -> p t m b", t=PACK, b=2),
+                out=w1_codes[g][:].rearrange("p (t m i b) -> p m t i b", t=PACK, i=8, b=2),
+                in_=w1_raw[:, 2 * PASS * g : 2 * PASS * (g + 1)].rearrange("p (m i t b) -> p m t i b", t=PACK, i=8, b=2),
             )
-        v_plane = at(V_PLANE, "v_plane", [P, S], U8)
+        v_plane = at(STAGE + 8, "v_plane", [P, S], U8)
         nc.vector.tensor_copy(out=v_plane[:], in_=tab_plane[:].indirect(idx[:]))
         v_codes = []
         for s in range(S // BANK):
-            codes = at(V_CODES + 2 * s, "v_codes%d" % s, [P, BANK], U32)
+            codes = at(STAGE + 4 * s, "v_codes%d" % s, [P, BANK], U32)
             offsets = idx[:, s * BANK // LIST : (s + 1) * BANK // LIST]
             nc.vector.tensor_copy(out=codes[:], in_=tab[:].bitcast(U32).indirect(offsets))
             v_codes.append(codes)
@@ -166,8 +169,7 @@ def tile_list_net_misstatement_scores_kernel(
         nc.vector.tensor_copy(out=v2_codes[:], in_=tab2[:].bitcast(U32).indirect(idx2[:]))
         v2_plane = at(V2_PLANE, "v2_plane", [P, M], U8)
         nc.vector.tensor_copy(out=v2_plane[:], in_=tab2_plane[:].indirect(idx2[:]))
-        first = at(LAST, "first", [P, 6 * M], F32)
-        staged = round_weight(w2_raw[0], first[:, 3 * M : 5 * M].bitcast(BF16), True)
+        staged = round_weight(w2_raw[0], stage("w2_0", G_STAGE), True)
         w2_q = [quantise_weight("w2_0", 0, staged, W2_PLANE)]
         wo_raw.append(load_weight(0, "wo01", wo, 0, 1))
         wo_raw.append(load_weight(1, "wo10", wo, 1, 0))
@@ -241,31 +243,34 @@ def tile_list_net_misstatement_scores_kernel(
                 cols = slice(side * M + first, side * M + first + words)
                 nc.vector.quantize_mx(out=d_q[g][0][:, cols].bitcast(FP8X4), scales=d_q[g][1][:, cols], in_=signed[side][:])
 
-        d_q = [
-            (at(D_CODES + 5 * g, "d%d_codes" % g, [P, 2 * M], U32), at(D_CODES + 5 * g + 4, "d%d_plane" % g, [P, 2 * M], U8))
-            for g in range(R_PASSES)
-        ]
-
         h = [summary_features(0)]
         h.append(summary_features(1))
         b = [ledger_features(0, c, c) for c in range(4)]
         h.append(summary_features(2))
-        staged = round_weight(w2_raw[1], first[:, 4 * M : 6 * M].bitcast(BF16), True)
+        staged = round_weight(w2_raw[1], stage("w2_1", G_STAGE + 2), True)
         wo_raw.append(load_weight(2, "wo11", wo, 1, 1))
-        picked = first[:, 0 : 4 * M].rearrange("p (t c) -> p t c", t=PACK)
-        pick_all(0, 0, picked)
+        early = at(LAST, "picked0", [P, PACK, M - CHUNK], F32)
+        pick_columns(0, 0, range(PACK), early)
+        late = at(G_STAGE, "picked0_late", [P, PACK, CHUNK], F32)
+        pick_columns(0, M - CHUNK, range(PACK), late)
         diff = at(DIFF, "diff0", [P, M * PACK], BF16)
-        subtract(b, picked, diff)
+        subtract(b[0:3], early, diff)
+        subtract(b[3:4], late, diff[:, 3 * BANK : 4 * BANK])
         wo_raw.append(load_weight(3, "wo20", wo, 2, 0))
+        w2_q.append(quantise_weight("w2_1", 1, staged, G_STAGE))
+        d_q = [
+            (at(D_CODES + 4 * g, "d_codes", [P, 2 * M], U32), at(kb, "d_plane", [P, 2 * M], U8))
+            for g, kb in enumerate((G_STAGE + 2, D_PLANE, D_PLANE + 1))
+        ]
+
         signed = split_signs("d0", diff[:], ABOVE, BELOW, 2)
-        w2_q.append(quantise_weight("w2_1", 1, staged, DIFF))
         quantise_signed(0, 0, signed)
 
         b = [ledger_features(1, c, 4 + c) for c in range(4)]
         wu_planes = at(ABOVE + 1, "wu_planes", [P, N], U8)
-        deal(nc.gpsimd, wu_planes[:], wu_raw_planes[:])
+        deal(nc.gpsimd, wu_planes[:], wu_raw_planes[:], 16)
         wu_first = at(ABOVE + 2, "wu_first", [P, N], I32)
-        deal(nc.gpsimd, wu_first[:], wu_raw[:, 0, :])
+        deal(nc.gpsimd, wu_first[:], wu_raw[:, 0, :], 4)
         wu_codes = [wu_first[:]]
         staged_w2 = round_weight(w2_raw[2], stage("w2_2", ABOVE - 3), True)
         wo_raw.append(load_weight(4, "wo21", wo, 2, 1))
@@ -274,17 +279,17 @@ def tile_list_net_misstatement_scores_kernel(
         diff = at(DIFF + 4, "diff1", [P, M * PACK], BF16)
         subtract(b, picked, diff)
         staged = [round_weight(wo_raw[i], stage("wo%d" % i, STAGE + 4 * (i % 4)), False) for i in range(4)]
-        signed = split_signs("d1", diff[:], BELOW, BELOW + 4, 2)
+        signed = split_signs("d1", diff[:], LAST, LAST + 4, 2)
         wo_q = [quantise_weight("wo%d" % i, 3 + i, staged[i], DIFF + 4 + i / 2) for i in range(2)]
         w2_q.append(quantise_weight("w2_2", 2, staged_w2, DIFF + 5))
         quantise_signed(1, 0, signed)
-        for i in range(2, 4):
-            wo_q.append(quantise_weight("wo%d" % i, 3 + i, staged[i], DIFF + 4.5 + i / 2))
+        wo_q.append(quantise_weight("wo2", 5, staged[2], DIFF + 5.5))
+        wo_q.append(quantise_weight("wo3", 6, staged[3], ABOVE))
         wu_last = at(STAGE + 7, "wu_last", [P, 2, N], I32)
         for g in range(1, R_PASSES):
-            deal(nc.gpsimd, wu_last[:, g - 1, :], wu_raw[:, g, :])
+            deal(nc.gpsimd, wu_last[:, g - 1, :], wu_raw[:, g, :], 4)
             wu_codes.append(wu_last[:, g - 1, :])
-        staged_last = [round_weight(wo_raw[i], stage("wo%d" % i, (STAGE, LAST + 8)[i - 4]), False) for i in (4, 5)]
+        staged_last = [round_weight(wo_raw[i], stage("wo%d" % i, (STAGE, EXTRA)[i - 4]), False) for i in (4, 5)]
 
         def add_pass(g, first, acc, n, first_slice, sides, closes):
             slices, width = acc.shape[1], acc.shape[2]
@@ -344,9 +349,9 @@ def tile_list_net_misstatement_scores_kernel(
         banks3 = [bank(5, "y3_acc0", [P, PACK, CHUNK])]
         for g in range(2):
             add_pass(g, HALF + CHUNK, banks3[0], 0, 0, (1, 0), False)
-        wo_q.append(quantise_weight("wo4", 7, staged_last[0], W2_PLANE + 0.5))
+        wo_q.append(quantise_weight("wo4", 7, staged_last[0], STAGE + 15))
         signed = split_signs("d20", diff[:, 0 : 2 * BANK], LAST, LAST + 2, 2)
-        wo_q.append(quantise_weight("wo5", 8, staged_last[1], W2_PLANE + 1))
+        wo_q.append(quantise_weight("wo5", 8, staged_last[1], STAGE + 15.5))
         quantise_signed(2, 0, signed)
         for i, acc in enumerate(banks0):
             add_pass(2, 0, acc, i // 2, 2 * (i % 2), (0, 1), True)
@@ -359,29 +364,28 @@ def tile_list_net_misstatement_scores_kernel(
             add_pass(g, HALF + CHUNK, banks3[1], 1, 0, (1, 0), False)
         rounded0 = [round_scores(nc.scalar.copy, at(H_ROWS + 16, "r00", [P, HALF * PACK], BF16)[:], y0[0])]
 
-        picked = at(LAST + 8, "picked3", [P, PACK, CHUNK], F32)
+        picked = at(EXTRA, "picked3", [P, PACK, CHUNK], F32)
         pick_columns(2, HALF, range(PACK), picked)
         subtract([b], picked, diff[:, 2 * BANK : 3 * BANK])
         b = ledger_features(2, 3, 4)
         signed = split_signs("d22", diff[:, 2 * BANK : 3 * BANK], LAST + 4, LAST + 5, 1)
         quantise_signed(2, HALF, signed)
-        for side in (1, 0):
-            for n in range(N_GROUPS):
-                add_pass(2, HALF, banks2[n], n, 0, (side,), side == 0)
-        picked = at(LAST + 8, "picked4", [P, PACK, CHUNK], F32)
+        for n in range(N_GROUPS):
+            add_pass(2, HALF, banks2[n], n, 0, (1, 0), True)
+        picked = at(EXTRA, "picked4", [P, PACK, CHUNK], F32)
         pick_columns(2, HALF + CHUNK, range(PACK), picked)
         subtract([b], picked, diff[:, 3 * BANK : 4 * BANK])
         signed = split_signs("d23", diff[:, 3 * BANK : 4 * BANK], LAST + 6, LAST + 7, 1)
         quantise_signed(2, HALF + CHUNK, signed)
-        for side in (1, 0):
-            for n in range(N_GROUPS):
-                add_pass(2, HALF + CHUNK, banks3[n], n, 0, (side,), side == 0)
+        for n in range(N_GROUPS):
+            add_pass(2, HALF + CHUNK, banks3[n], n, 0, (1, 0), True)
 
         y2 = [at(H_ROWS + 8 + 2 * n, "y2%d" % n, [P, PACK, CHUNK], F32) for n in range(N_GROUPS)]
         y3 = [at(H_ROWS + 12 + 2 * n, "y3%d" % n, [P, PACK, CHUNK], F32) for n in range(N_GROUPS)]
         for n in range(N_GROUPS):
             scale_scores(n, HALF, [banks2[n][:, t, :] for t in range(PACK)], y2[n])
             store_scores(nc.sync, n, HALF, y2[n])
+        rounded = [round_scores(nc.scalar.copy, at(H_ROWS + 20, "r2", [P, BANK], BF16)[:], y2[0])]
         scale_scores(0, HALF + CHUNK, [banks3[0][:, t, :] for t in range(PACK)], y3[0])
         store_scores(nc.scalar, 0, HALF + CHUNK, y3[0])
 
@@ -392,16 +396,18 @@ def tile_list_net_misstatement_scores_kernel(
         for n in range(N_GROUPS):
             quantise_scores(n, 0, rounded0[n])
         nc.sync.dma_start(out=out_words[:, :, 0:HALF], in_=y_codes[:, :, 0:HALF].bitcast(I32))
+        rounded.append(round_scores(nc.vector.tensor_copy, at(H_ROWS + 21, "r2", [P, BANK], BF16)[:], y2[1]))
         nc.vector.tensor_tensor(
             out=y3[1][:], in0=banks3[1][:], in1=gains[:, 1, :].unsqueeze(2).to_broadcast([P, PACK, CHUNK]), op=MULT
         )
         store_scores(nc.sync, 1, HALF + CHUNK, y3[1])
-        rounded = [
-            round_scores(nc.vector.tensor_copy, at(H_ROWS + 20 + i, "r%d" % (i + 2), [P, BANK], BF16)[:], y)
-            for i, y in enumerate(y2 + y3)
-        ]
-        for i in range(4):
-            quantise_scores(i % 2, HALF + CHUNK * (i // 2), rounded[i])
+        last = [at(H_ROWS + 22 + n, "r3", [P, BANK], BF16)[:] for n in range(N_GROUPS)]
+        round_scores(nc.vector.tensor_copy, last[0], y3[0])
+        quantise_scores(0, HALF, rounded[0])
+        round_scores(nc.vector.tensor_copy, last[1], y3[1])
+        quantise_scores(1, HALF, rounded[1])
+        for n in range(N_GROUPS):
+            quantise_scores(n, HALF + CHUNK, last[n])
         nc.scalar.dma_start(out=out_words[:, :, HALF:M], in_=y_codes[:, :, HALF:M].bitcast(I32))
         for q in range(QUADRANTS):
             queue = nc.scalar if q % 2 else nc.sync

@@ -134,18 +134,22 @@ def tile_list_net_misstatement_scores_kernel(
         load_words(tab2, tab2_words[0])
         load_plane(nc.sync, tab2_plane, tab2_scales[0])
         nc.sync.dma_start(pick[:], pos1)
-        w2_raw = [load_weight(2, "w2_0", w2, 0, 0)]
+        halves = [at(LAND + 16 + 4 * i, "w2_0_raw", [P, PACK, PASS // 2], F32) for i in range(2)]
+        for i in range(2):
+            rows = w2[:, i * PASS // 2 : (i + 1) * PASS // 2]
+            nc.sync.dma_start(out=halves[i][:], in_=rows.rearrange("(p j) c -> p j c", j=PACK))
+        w2_raw = [halves]
         w2_raw.append(load_weight(3, "w2_1", w2, 0, 1))
-        w2_raw.append(load_weight(4, "w2_2", w2, 0, 2))
-        wo_raw = [load_weight(5, "wo00", wo, 0, 0)]
         for q in range(QUADRANTS):
             nc.sync.dma_start(
                 out=wu_raw_planes[32 * q : 32 * q + 4 * R_PASSES, :].bitcast(I32),
                 in_=wu_scales[:, 4 * q : 4 * q + 4, :].bitcast(I32),
             )
+        wu_raw = at(WU_RAW, "wu_raw", [P, N], I32)
+        load_words(wu_raw, wu_words[0])
+        w2_raw.append(load_weight(4, "w2_2", w2, 0, 2))
+        wo_raw = [load_weight(5, "wo00", wo, 0, 0)]
         nc.sync.dma_start(out=gains[:], in_=gain.rearrange("(g p t) -> p g t", p=P, t=PACK))
-        wu_raw = at(WU_RAW, "wu_raw", [P, R_PASSES, N], I32)
-        nc.sync.dma_start(out=wu_raw[:], in_=wu_words.rearrange("a p c i -> p a (c i)").bitcast(I32))
 
         w1_codes = [at(kb, "w1_codes", [P, 2 * PASS], U8) for kb in (W1_CODES, W1_CODES + 1, STAGE + 12)]
         w1_plane = [at(W1_PLANE + g / 2, "w1_plane%d" % g, [P, PASS], U8) for g in range(R_PASSES)]
@@ -169,16 +173,25 @@ def tile_list_net_misstatement_scores_kernel(
         nc.vector.tensor_copy(out=v2_codes[:], in_=tab2[:].bitcast(U32).indirect(idx2[:]))
         v2_plane = at(V2_PLANE, "v2_plane", [P, M], U8)
         nc.vector.tensor_copy(out=v2_plane[:], in_=tab2_plane[:].indirect(idx2[:]))
-        staged = round_weight(w2_raw[0], stage("w2_0", G_STAGE), True)
+        staged = stage("w2_0", G_STAGE)
+        for i in range(2):
+            nc.gpsimd.tensor_scalar(
+                out=staged.rearrange("p (t h m j) -> p h m t j", t=PACK, h=2, j=PACK)[:, i],
+                in0=halves[i][:].rearrange("p j (m t) -> p m t j", t=PACK),
+                scalar1=1.0, scalar2=0.0, op0=MULT, op1=ADD,
+            )
         w2_q = [quantise_weight("w2_0", 0, staged, W2_PLANE)]
         wo_raw.append(load_weight(0, "wo01", wo, 0, 1))
         wo_raw.append(load_weight(1, "wo10", wo, 1, 0))
+        wo_raw.append(load_weight(6.5, "wo11", wo, 1, 1))
+        wu_rest = at(LAND + 16, "wu_rest", [P, 2, N], I32)
+        nc.sync.dma_start(out=wu_rest[:], in_=wu_words[1:3].rearrange("a p c i -> p a (c i)").bitcast(I32))
 
         def summary_features(g):
             rows = [at(H_ROWS + 4 * (PACK * g + t), "h%d%d" % (g, t), [P, S], F32) for t in range(PACK)]
             for t in range(PACK):
                 for s in range(S // BANK):
-                    acc = bank((2 * t + s) % 4 + (4 if g > 0 and t < 2 else 0), "h_acc", [P, BANK])
+                    acc = bank((2 * t + s) % 4 + (4 if g < 2 and t >= 2 else 0), "h_acc", [P, BANK])
                     nc.tensor.matmul_mx(
                         out=acc[:],
                         lhsT=w1_codes[g][:, 2 * P * t : 2 * P * (t + 1)].bitcast(FP4X4),
@@ -248,7 +261,6 @@ def tile_list_net_misstatement_scores_kernel(
         b = [ledger_features(0, c, c) for c in range(4)]
         h.append(summary_features(2))
         staged = round_weight(w2_raw[1], stage("w2_1", G_STAGE + 2), True)
-        wo_raw.append(load_weight(2, "wo11", wo, 1, 1))
         early = at(LAST, "picked0", [P, PACK, M - CHUNK], F32)
         pick_columns(0, 0, range(PACK), early)
         late = at(G_STAGE, "picked0_late", [P, PACK, CHUNK], F32)
@@ -270,7 +282,7 @@ def tile_list_net_misstatement_scores_kernel(
         wu_planes = at(ABOVE + 1, "wu_planes", [P, N], U8)
         deal(nc.gpsimd, wu_planes[:], wu_raw_planes[:], 16)
         wu_first = at(ABOVE + 2, "wu_first", [P, N], I32)
-        deal(nc.gpsimd, wu_first[:], wu_raw[:, 0, :], 4)
+        deal(nc.gpsimd, wu_first[:], wu_raw[:], 4)
         wu_codes = [wu_first[:]]
         staged_w2 = round_weight(w2_raw[2], stage("w2_2", ABOVE - 3), True)
         wo_raw.append(load_weight(4, "wo21", wo, 2, 1))
@@ -287,7 +299,7 @@ def tile_list_net_misstatement_scores_kernel(
         wo_q.append(quantise_weight("wo3", 6, staged[3], ABOVE))
         wu_last = at(STAGE + 7, "wu_last", [P, 2, N], I32)
         for g in range(1, R_PASSES):
-            deal(nc.gpsimd, wu_last[:, g - 1, :], wu_raw[:, g, :], 4)
+            deal(nc.gpsimd, wu_last[:, g - 1, :], wu_rest[:, g - 1, :], 4)
             wu_codes.append(wu_last[:, g - 1, :])
         staged_last = [round_weight(wo_raw[i], stage("wo%d" % i, (STAGE, EXTRA)[i - 4]), False) for i in (4, 5)]
 
@@ -359,15 +371,15 @@ def tile_list_net_misstatement_scores_kernel(
         for n in range(N_GROUPS):
             scale_scores(n, 0, [banks0[2 * n + t // 2][:, t % 2, :] for t in range(PACK)], y0[n])
             store_scores(nc.sync, n, 0, y0[n])
-        banks3.append(bank(0, "y3_acc1", [P, PACK, CHUNK]))
-        for g in range(2):
-            add_pass(g, HALF + CHUNK, banks3[1], 1, 0, (1, 0), False)
         rounded0 = [round_scores(nc.scalar.copy, at(H_ROWS + 16, "r00", [P, HALF * PACK], BF16)[:], y0[0])]
 
         picked = at(EXTRA, "picked3", [P, PACK, CHUNK], F32)
         pick_columns(2, HALF, range(PACK), picked)
         subtract([b], picked, diff[:, 2 * BANK : 3 * BANK])
         b = ledger_features(2, 3, 4)
+        banks3.append(bank(0, "y3_acc1", [P, PACK, CHUNK]))
+        for g in range(2):
+            add_pass(g, HALF + CHUNK, banks3[1], 1, 0, (1, 0), False)
         signed = split_signs("d22", diff[:, 2 * BANK : 3 * BANK], LAST + 4, LAST + 5, 1)
         quantise_signed(2, HALF, signed)
         for n in range(N_GROUPS):

@@ -86,6 +86,23 @@ def tile_list_net_misstatement_scores_kernel(
             nc.sync.dma_start(out=raw[:], in_=rows.rearrange("(p j) c -> p j c", j=PACK))
             return raw
 
+        def load_halves(place, group):
+            halves = [at(LAND + 8 * place + 4 * i, "w2_raw", [P, PACK, PASS // 2], F32) for i in range(2)]
+            for i in range(2):
+                first = group * PASS + i * PASS // 2
+                rows = w2[:, first : first + PASS // 2]
+                nc.sync.dma_start(out=halves[i][:], in_=rows.rearrange("(p j) c -> p j c", j=PACK))
+            return halves
+
+        def round_halves(halves, staged):
+            for i in range(2):
+                nc.gpsimd.tensor_scalar(
+                    out=staged.rearrange("p (t h m j) -> p h m t j", t=PACK, h=2, j=PACK)[:, i],
+                    in0=halves[i][:].rearrange("p j (m t) -> p m t j", t=PACK),
+                    scalar1=1.0, scalar2=0.0, op0=MULT, op1=ADD,
+                )
+            return staged
+
         def stage(name, kb):
             return at(kb, name + "_staged", [P, PASS * PACK], BF16)[:]
 
@@ -134,12 +151,8 @@ def tile_list_net_misstatement_scores_kernel(
         load_words(tab2, tab2_words[0])
         load_plane(nc.sync, tab2_plane, tab2_scales[0])
         nc.sync.dma_start(pick[:], pos1)
-        halves = [at(LAND + 16 + 4 * i, "w2_0_raw", [P, PACK, PASS // 2], F32) for i in range(2)]
-        for i in range(2):
-            rows = w2[:, i * PASS // 2 : (i + 1) * PASS // 2]
-            nc.sync.dma_start(out=halves[i][:], in_=rows.rearrange("(p j) c -> p j c", j=PACK))
-        w2_raw = [halves]
-        w2_raw.append(load_weight(3, "w2_1", w2, 0, 1))
+        w2_raw = [load_halves(2, 0)]
+        w2_raw.append(load_halves(3, 1))
         for q in range(QUADRANTS):
             nc.sync.dma_start(
                 out=wu_raw_planes[32 * q : 32 * q + 4 * R_PASSES, :].bitcast(I32),
@@ -173,19 +186,11 @@ def tile_list_net_misstatement_scores_kernel(
         nc.vector.tensor_copy(out=v2_codes[:], in_=tab2[:].bitcast(U32).indirect(idx2[:]))
         v2_plane = at(V2_PLANE, "v2_plane", [P, M], U8)
         nc.vector.tensor_copy(out=v2_plane[:], in_=tab2_plane[:].indirect(idx2[:]))
-        staged = stage("w2_0", G_STAGE)
-        for i in range(2):
-            nc.gpsimd.tensor_scalar(
-                out=staged.rearrange("p (t h m j) -> p h m t j", t=PACK, h=2, j=PACK)[:, i],
-                in0=halves[i][:].rearrange("p j (m t) -> p m t j", t=PACK),
-                scalar1=1.0, scalar2=0.0, op0=MULT, op1=ADD,
-            )
+        staged = round_halves(w2_raw[0], stage("w2_0", G_STAGE))
         w2_q = [quantise_weight("w2_0", 0, staged, W2_PLANE)]
         wo_raw.append(load_weight(0, "wo01", wo, 0, 1))
         wo_raw.append(load_weight(1, "wo10", wo, 1, 0))
         wo_raw.append(load_weight(6.5, "wo11", wo, 1, 1))
-        wu_rest = at(LAND + 16, "wu_rest", [P, 2, N], I32)
-        nc.sync.dma_start(out=wu_rest[:], in_=wu_words[1:3].rearrange("a p c i -> p a (c i)").bitcast(I32))
 
         def summary_features(g):
             rows = [at(H_ROWS + 4 * (PACK * g + t), "h%d%d" % (g, t), [P, S], F32) for t in range(PACK)]
@@ -260,16 +265,18 @@ def tile_list_net_misstatement_scores_kernel(
         h.append(summary_features(1))
         b = [ledger_features(0, c, c) for c in range(4)]
         h.append(summary_features(2))
-        staged = round_weight(w2_raw[1], stage("w2_1", G_STAGE + 2), True)
+        staged = round_halves(w2_raw[1], stage("w2_1", G_STAGE + 2))
         early = at(LAST, "picked0", [P, PACK, M - CHUNK], F32)
         pick_columns(0, 0, range(PACK), early)
-        late = at(G_STAGE, "picked0_late", [P, PACK, CHUNK], F32)
+        late = at(LAND + 20, "picked0_late", [P, PACK, CHUNK], F32)
         pick_columns(0, M - CHUNK, range(PACK), late)
         diff = at(DIFF, "diff0", [P, M * PACK], BF16)
         subtract(b[0:3], early, diff)
         subtract(b[3:4], late, diff[:, 3 * BANK : 4 * BANK])
+        wu_rest = at(LAND + 16, "wu_rest", [P, 2, N], I32)
+        nc.sync.dma_start(out=wu_rest[:], in_=wu_words[1:3].rearrange("a p c i -> p a (c i)").bitcast(I32))
         wo_raw.append(load_weight(3, "wo20", wo, 2, 0))
-        w2_q.append(quantise_weight("w2_1", 1, staged, G_STAGE))
+        w2_q.append(quantise_weight("w2_1", 1, staged, LAST + 5.5))
         d_q = [
             (at(D_CODES + 4 * g, "d_codes", [P, 2 * M], U32), at(kb, "d_plane", [P, 2 * M], U8))
             for g, kb in enumerate((G_STAGE + 2, D_PLANE, D_PLANE + 1))
@@ -284,23 +291,30 @@ def tile_list_net_misstatement_scores_kernel(
         wu_first = at(ABOVE + 2, "wu_first", [P, N], I32)
         deal(nc.gpsimd, wu_first[:], wu_raw[:], 4)
         wu_codes = [wu_first[:]]
-        staged_w2 = round_weight(w2_raw[2], stage("w2_2", ABOVE - 3), True)
+        staged = [round_weight(wo_raw[0], stage("wo0", STAGE), False)]
+        early = at(BELOW, "picked1", [P, PACK, M - CHUNK], F32)
+        pick_columns(1, 0, range(PACK), early)
+        wo_q = [quantise_weight("wo0", 3, staged[0], D_PLANE + 2)]
+        staged_w2 = round_weight(w2_raw[2], stage("w2_2", STAGE), True)
         wo_raw.append(load_weight(4, "wo21", wo, 2, 1))
-        picked = at(BELOW, "picked1", [P, PACK, M], F32)
-        pick_all(1, 0, picked)
-        diff = at(DIFF + 4, "diff1", [P, M * PACK], BF16)
-        subtract(b, picked, diff)
-        staged = [round_weight(wo_raw[i], stage("wo%d" % i, STAGE + 4 * (i % 4)), False) for i in range(4)]
-        signed = split_signs("d1", diff[:], LAST, LAST + 4, 2)
-        wo_q = [quantise_weight("wo%d" % i, 3 + i, staged[i], DIFF + 4 + i / 2) for i in range(2)]
-        w2_q.append(quantise_weight("w2_2", 2, staged_w2, DIFF + 5))
+        late = at(LAND + 40, "picked1_late", [P, PACK, CHUNK], F32)
+        pick_columns(1, M - CHUNK, range(PACK), late)
+        diff = at(LAND + 42, "diff1", [P, M * PACK], BF16)
+        subtract(b[0:3], early, diff)
+        subtract(b[3:4], late, diff[:, 3 * BANK : 4 * BANK])
+        staged += [round_weight(wo_raw[i], stage("wo%d" % i, STAGE + 4 * i), False) for i in range(1, 4)]
+        wo_q.append(quantise_weight("wo1", 4, staged[1], BELOW))
+        signed = split_signs("d1", diff[:], LAND, LAND + 4, 2)
+        w2_q.append(quantise_weight("w2_2", 2, staged_w2, LAND + 42))
         quantise_signed(1, 0, signed)
-        wo_q.append(quantise_weight("wo2", 5, staged[2], DIFF + 5.5))
-        wo_q.append(quantise_weight("wo3", 6, staged[3], ABOVE))
+        wo_q.append(quantise_weight("wo2", 5, staged[2], LAND + 42.5))
+        wo_q.append(quantise_weight("wo3", 6, staged[3], LAND + 43))
         wu_last = at(STAGE + 7, "wu_last", [P, 2, N], I32)
-        for g in range(1, R_PASSES):
-            deal(nc.gpsimd, wu_last[:, g - 1, :], wu_rest[:, g - 1, :], 4)
-            wu_codes.append(wu_last[:, g - 1, :])
+        for n in range(N_GROUPS):
+            cols = slice(n * PASS, (n + 1) * PASS)
+            deal(nc.gpsimd, wu_last[:, 0, cols], wu_rest[:, 0, cols], 4)
+        deal(nc.gpsimd, wu_last[:, 1, :], wu_rest[:, 1, :], 4)
+        wu_codes += [wu_last[:, 0, :], wu_last[:, 1, :]]
         staged_last = [round_weight(wo_raw[i], stage("wo%d" % i, (STAGE, EXTRA)[i - 4]), False) for i in (4, 5)]
 
         def add_pass(g, first, acc, n, first_slice, sides, closes):
@@ -353,41 +367,42 @@ def tile_list_net_misstatement_scores_kernel(
                     add_pass(g, 0, acc, i // 2, 2 * (i % 2), (side,), False)
                 for n in range(N_GROUPS):
                     add_pass(g, HALF, banks2[n], n, 0, (side,), False)
-        picked = at(STAGE + 15, "picked2", [P, PACK, HALF], F32)
+        picked = at(LAND + 52, "picked2", [P, PACK, HALF], F32)
         pick_all(2, 0, picked)
-        diff = at(DIFF + 8, "diff2", [P, M * PACK], BF16)
+        diff = at(DIFF + 8, "diff2", [P, HALF * PACK], BF16)
         subtract(b, picked, diff)
         b = ledger_features(2, 2, 4)
         banks3 = [bank(5, "y3_acc0", [P, PACK, CHUNK])]
         for g in range(2):
             add_pass(g, HALF + CHUNK, banks3[0], 0, 0, (1, 0), False)
-        wo_q.append(quantise_weight("wo4", 7, staged_last[0], STAGE + 15))
+        wo_q.append(quantise_weight("wo4", 7, staged_last[0], LAND + 52))
         signed = split_signs("d20", diff[:, 0 : 2 * BANK], LAST, LAST + 2, 2)
-        wo_q.append(quantise_weight("wo5", 8, staged_last[1], STAGE + 15.5))
+        wo_q.append(quantise_weight("wo5", 8, staged_last[1], LAND + 52.5))
         quantise_signed(2, 0, signed)
         for i, acc in enumerate(banks0):
-            add_pass(2, 0, acc, i // 2, 2 * (i % 2), (0, 1), True)
+            add_pass(2, 0, acc, i // 2, 2 * (i % 2), (1, 0), True)
         y0 = [at(H_ROWS + 4 * n, "y0%d" % n, [P, PACK, HALF], F32) for n in range(N_GROUPS)]
         for n in range(N_GROUPS):
             scale_scores(n, 0, [banks0[2 * n + t // 2][:, t % 2, :] for t in range(PACK)], y0[n])
             store_scores(nc.sync, n, 0, y0[n])
-        rounded0 = [round_scores(nc.scalar.copy, at(H_ROWS + 16, "r00", [P, HALF * PACK], BF16)[:], y0[0])]
+        rounded_late = round_scores(nc.scalar.copy, at(H_ROWS + 18, "r01", [P, HALF * PACK], BF16)[:], y0[1])
 
-        picked = at(EXTRA, "picked3", [P, PACK, CHUNK], F32)
+        picked = at(LAND + 24, "picked3", [P, PACK, CHUNK], F32)
         pick_columns(2, HALF, range(PACK), picked)
-        subtract([b], picked, diff[:, 2 * BANK : 3 * BANK])
+        diff = at(LAND + 32, "diff3", [P, 2 * BANK], BF16)
+        subtract([b], picked, diff[:, 0:BANK])
         b = ledger_features(2, 3, 4)
         banks3.append(bank(0, "y3_acc1", [P, PACK, CHUNK]))
         for g in range(2):
             add_pass(g, HALF + CHUNK, banks3[1], 1, 0, (1, 0), False)
-        signed = split_signs("d22", diff[:, 2 * BANK : 3 * BANK], LAST + 4, LAST + 5, 1)
+        signed = split_signs("d22", diff[:, 0:BANK], LAST + 4, LAST + 5, 1)
         quantise_signed(2, HALF, signed)
         for n in range(N_GROUPS):
             add_pass(2, HALF, banks2[n], n, 0, (1, 0), True)
-        picked = at(EXTRA, "picked4", [P, PACK, CHUNK], F32)
+        picked = at(LAND + 34, "picked4", [P, PACK, CHUNK], F32)
         pick_columns(2, HALF + CHUNK, range(PACK), picked)
-        subtract([b], picked, diff[:, 3 * BANK : 4 * BANK])
-        signed = split_signs("d23", diff[:, 3 * BANK : 4 * BANK], LAST + 6, LAST + 7, 1)
+        subtract([b], picked, diff[:, BANK : 2 * BANK])
+        signed = split_signs("d23", diff[:, BANK : 2 * BANK], LAST + 6, LAST + 7, 1)
         quantise_signed(2, HALF + CHUNK, signed)
         for n in range(N_GROUPS):
             add_pass(2, HALF + CHUNK, banks3[n], n, 0, (1, 0), True)
@@ -397,30 +412,28 @@ def tile_list_net_misstatement_scores_kernel(
         for n in range(N_GROUPS):
             scale_scores(n, HALF, [banks2[n][:, t, :] for t in range(PACK)], y2[n])
             store_scores(nc.sync, n, HALF, y2[n])
-        rounded = [round_scores(nc.scalar.copy, at(H_ROWS + 20, "r2", [P, BANK], BF16)[:], y2[0])]
-        scale_scores(0, HALF + CHUNK, [banks3[0][:, t, :] for t in range(PACK)], y3[0])
-        store_scores(nc.scalar, 0, HALF + CHUNK, y3[0])
+        for n in range(N_GROUPS):
+            scale_scores(n, HALF + CHUNK, [banks3[n][:, t, :] for t in range(PACK)], y3[n])
+            store_scores(nc.sync, n, HALF + CHUNK, y3[n])
 
         y_codes = at(LAST + 3, "y_codes", [P, N_GROUPS, M], U32)
         y_plane = at(H_ROWS + 28, "y_plane", [P, N_GROUPS, M], U8)
         out_words = out_1.rearrange("g p m t -> p g (m t)").bitcast(I32)
-        rounded0.append(round_scores(nc.vector.tensor_copy, at(LAST + 7, "r01", [P, HALF * PACK], BF16)[:], y0[1]))
+        rounded0 = [round_scores(nc.vector.tensor_copy, at(H_ROWS + 16, "r00", [P, HALF * PACK], BF16)[:], y0[0]), rounded_late]
         for n in range(N_GROUPS):
             quantise_scores(n, 0, rounded0[n])
-        nc.sync.dma_start(out=out_words[:, :, 0:HALF], in_=y_codes[:, :, 0:HALF].bitcast(I32))
-        rounded.append(round_scores(nc.vector.tensor_copy, at(H_ROWS + 21, "r2", [P, BANK], BF16)[:], y2[1]))
-        nc.vector.tensor_tensor(
-            out=y3[1][:], in0=banks3[1][:], in1=gains[:, 1, :].unsqueeze(2).to_broadcast([P, PACK, CHUNK]), op=MULT
-        )
-        store_scores(nc.sync, 1, HALF + CHUNK, y3[1])
-        last = [at(H_ROWS + 22 + n, "r3", [P, BANK], BF16)[:] for n in range(N_GROUPS)]
-        round_scores(nc.vector.tensor_copy, last[0], y3[0])
-        quantise_scores(0, HALF, rounded[0])
-        round_scores(nc.vector.tensor_copy, last[1], y3[1])
-        quantise_scores(1, HALF, rounded[1])
+        rounded = [at(H_ROWS + 20 + i, "r2", [P, BANK], BF16)[:] for i in range(4)]
         for n in range(N_GROUPS):
-            quantise_scores(n, HALF + CHUNK, last[n])
-        nc.scalar.dma_start(out=out_words[:, :, HALF:M], in_=y_codes[:, :, HALF:M].bitcast(I32))
+            round_scores(nc.vector.tensor_copy, rounded[n], y2[n])
+        quantise_scores(0, HALF, rounded[0])
+        round_scores(nc.vector.tensor_copy, rounded[2], y3[0])
+        quantise_scores(1, HALF, rounded[1])
+        done = M - CHUNK
+        nc.sync.dma_start(out=out_words[:, :, 0:done], in_=y_codes[:, :, 0:done].bitcast(I32))
+        round_scores(nc.vector.tensor_copy, rounded[3], y3[1])
+        for n in range(N_GROUPS):
+            quantise_scores(n, done, rounded[2 + n])
+        nc.scalar.dma_start(out=out_words[:, :, done:M], in_=y_codes[:, :, done:M].bitcast(I32))
         for q in range(QUADRANTS):
             queue = nc.scalar if q % 2 else nc.sync
             queue.dma_start(

@@ -84,7 +84,12 @@ def tile_list_net_misstatement_scores_kernel(
             raw = at(LAND + 8 * place, name + "_raw", [P, PACK, PASS], F32)
             rows = w[g * PASS : (g + 1) * PASS, group * PASS : (group + 1) * PASS]
             nc.sync.dma_start(out=raw[:], in_=rows.rearrange("(p j) c -> p j c", j=PACK))
-            return raw
+            return raw[:]
+
+        def load_pass(kb, g):
+            raw = at(kb, "wo_raw", [P, PACK, N], F32)
+            nc.sync.dma_start(out=raw[:], in_=wo[g * PASS : (g + 1) * PASS, :].rearrange("(p j) c -> p j c", j=PACK))
+            return [raw[:, :, n * PASS : (n + 1) * PASS] for n in range(N_GROUPS)]
 
         def load_halves(place, group):
             halves = [at(LAND + 8 * place + 4 * i, "w2_raw", [P, PACK, PASS // 2], F32) for i in range(2)]
@@ -110,13 +115,13 @@ def tile_list_net_misstatement_scores_kernel(
             if on_gpsimd:
                 nc.gpsimd.tensor_scalar(
                     out=staged.rearrange("p (t m j) -> p m t j", t=PACK, j=PACK),
-                    in0=raw[:].rearrange("p j (m t) -> p m t j", t=PACK),
+                    in0=raw.rearrange("p j (m t) -> p m t j", t=PACK),
                     scalar1=1.0, scalar2=0.0, op0=MULT, op1=ADD,
                 )
             else:
                 nc.scalar.copy(
                     out=staged.rearrange("p (t m j) -> p m j t", t=PACK, j=PACK),
-                    in_=raw[:].rearrange("p j (m t) -> p m j t", t=PACK),
+                    in_=raw.rearrange("p j (m t) -> p m j t", t=PACK),
                 )
             return staged
 
@@ -152,16 +157,16 @@ def tile_list_net_misstatement_scores_kernel(
         load_plane(nc.sync, tab2_plane, tab2_scales[0])
         nc.sync.dma_start(pick[:], pos1)
         w2_raw = [load_halves(2, 0)]
-        w2_raw.append(load_halves(3, 1))
+        w2_raw.append(load_weight(3, "w2_1", w2, 0, 1))
         for q in range(QUADRANTS):
             nc.sync.dma_start(
                 out=wu_raw_planes[32 * q : 32 * q + 4 * R_PASSES, :].bitcast(I32),
                 in_=wu_scales[:, 4 * q : 4 * q + 4, :].bitcast(I32),
             )
-        wu_raw = at(WU_RAW, "wu_raw", [P, N], I32)
+        wu_raw = at(LAND + 56, "wu_raw", [P, N], I32)
         load_words(wu_raw, wu_words[0])
+        wo_raw = load_pass(LAND + 40, 0)
         w2_raw.append(load_weight(4, "w2_2", w2, 0, 2))
-        wo_raw = [load_weight(5, "wo00", wo, 0, 0)]
         nc.sync.dma_start(out=gains[:], in_=gain.rearrange("(g p t) -> p g t", p=P, t=PACK))
 
         w1_codes = [at(kb, "w1_codes", [P, 2 * PASS], U8) for kb in (W1_CODES, W1_CODES + 1, STAGE + 12)]
@@ -188,9 +193,8 @@ def tile_list_net_misstatement_scores_kernel(
         nc.vector.tensor_copy(out=v2_plane[:], in_=tab2_plane[:].indirect(idx2[:]))
         staged = round_halves(w2_raw[0], stage("w2_0", G_STAGE))
         w2_q = [quantise_weight("w2_0", 0, staged, W2_PLANE)]
-        wo_raw.append(load_weight(0, "wo01", wo, 0, 1))
-        wo_raw.append(load_weight(1, "wo10", wo, 1, 0))
-        wo_raw.append(load_weight(6.5, "wo11", wo, 1, 1))
+        wo_raw.append(load_weight(0, "wo10", wo, 1, 0))
+        wo_raw.append(load_weight(1, "wo11", wo, 1, 1))
 
         def summary_features(g):
             rows = [at(H_ROWS + 4 * (PACK * g + t), "h%d%d" % (g, t), [P, S], F32) for t in range(PACK)]
@@ -265,7 +269,7 @@ def tile_list_net_misstatement_scores_kernel(
         h.append(summary_features(1))
         b = [ledger_features(0, c, c) for c in range(4)]
         h.append(summary_features(2))
-        staged = round_halves(w2_raw[1], stage("w2_1", G_STAGE + 2))
+        staged = round_weight(w2_raw[1], stage("w2_1", G_STAGE + 2), True)
         early = at(LAST, "picked0", [P, PACK, M - CHUNK], F32)
         pick_columns(0, 0, range(PACK), early)
         late = at(LAND + 20, "picked0_late", [P, PACK, CHUNK], F32)
@@ -291,24 +295,19 @@ def tile_list_net_misstatement_scores_kernel(
         wu_first = at(ABOVE + 2, "wu_first", [P, N], I32)
         deal(nc.gpsimd, wu_first[:], wu_raw[:], 4)
         wu_codes = [wu_first[:]]
-        staged = [round_weight(wo_raw[0], stage("wo0", STAGE), False)]
-        early = at(BELOW, "picked1", [P, PACK, M - CHUNK], F32)
-        pick_columns(1, 0, range(PACK), early)
-        wo_q = [quantise_weight("wo0", 3, staged[0], D_PLANE + 2)]
-        staged_w2 = round_weight(w2_raw[2], stage("w2_2", STAGE), True)
+        staged_w2 = round_weight(w2_raw[2], stage("w2_2", ABOVE - 3), True)
         wo_raw.append(load_weight(4, "wo21", wo, 2, 1))
-        late = at(LAND + 40, "picked1_late", [P, PACK, CHUNK], F32)
-        pick_columns(1, M - CHUNK, range(PACK), late)
-        diff = at(LAND + 42, "diff1", [P, M * PACK], BF16)
-        subtract(b[0:3], early, diff)
-        subtract(b[3:4], late, diff[:, 3 * BANK : 4 * BANK])
-        staged += [round_weight(wo_raw[i], stage("wo%d" % i, STAGE + 4 * i), False) for i in range(1, 4)]
-        wo_q.append(quantise_weight("wo1", 4, staged[1], BELOW))
-        signed = split_signs("d1", diff[:], LAND, LAND + 4, 2)
-        w2_q.append(quantise_weight("w2_2", 2, staged_w2, LAND + 42))
+        picked = at(BELOW, "picked1", [P, PACK, M], F32)
+        pick_all(1, 0, picked)
+        diff = at(DIFF + 4, "diff1", [P, M * PACK], BF16)
+        subtract(b, picked, diff)
+        staged = [round_weight(wo_raw[i], stage("wo%d" % i, STAGE + 4 * (i % 4)), False) for i in range(4)]
+        signed = split_signs("d1", diff[:], LAST, LAST + 4, 2)
+        wo_q = [quantise_weight("wo%d" % i, 3 + i, staged[i], DIFF + 4 + i / 2) for i in range(2)]
+        w2_q.append(quantise_weight("w2_2", 2, staged_w2, DIFF + 5))
         quantise_signed(1, 0, signed)
-        wo_q.append(quantise_weight("wo2", 5, staged[2], LAND + 42.5))
-        wo_q.append(quantise_weight("wo3", 6, staged[3], LAND + 43))
+        wo_q.append(quantise_weight("wo2", 5, staged[2], DIFF + 5.5))
+        wo_q.append(quantise_weight("wo3", 6, staged[3], ABOVE))
         wu_last = at(STAGE + 7, "wu_last", [P, 2, N], I32)
         for n in range(N_GROUPS):
             cols = slice(n * PASS, (n + 1) * PASS)
@@ -367,7 +366,7 @@ def tile_list_net_misstatement_scores_kernel(
                     add_pass(g, 0, acc, i // 2, 2 * (i % 2), (side,), False)
                 for n in range(N_GROUPS):
                     add_pass(g, HALF, banks2[n], n, 0, (side,), False)
-        picked = at(LAND + 52, "picked2", [P, PACK, HALF], F32)
+        picked = at(LAND + 8, "picked2", [P, PACK, HALF], F32)
         pick_all(2, 0, picked)
         diff = at(DIFF + 8, "diff2", [P, HALF * PACK], BF16)
         subtract(b, picked, diff)
@@ -375,9 +374,9 @@ def tile_list_net_misstatement_scores_kernel(
         banks3 = [bank(5, "y3_acc0", [P, PACK, CHUNK])]
         for g in range(2):
             add_pass(g, HALF + CHUNK, banks3[0], 0, 0, (1, 0), False)
-        wo_q.append(quantise_weight("wo4", 7, staged_last[0], LAND + 52))
+        wo_q.append(quantise_weight("wo4", 7, staged_last[0], LAND + 8))
         signed = split_signs("d20", diff[:, 0 : 2 * BANK], LAST, LAST + 2, 2)
-        wo_q.append(quantise_weight("wo5", 8, staged_last[1], LAND + 52.5))
+        wo_q.append(quantise_weight("wo5", 8, staged_last[1], LAND + 8.5))
         quantise_signed(2, 0, signed)
         for i, acc in enumerate(banks0):
             add_pass(2, 0, acc, i // 2, 2 * (i % 2), (1, 0), True)
@@ -435,8 +434,7 @@ def tile_list_net_misstatement_scores_kernel(
             quantise_scores(n, done, rounded[2 + n])
         nc.scalar.dma_start(out=out_words[:, :, done:M], in_=y_codes[:, :, done:M].bitcast(I32))
         for q in range(QUADRANTS):
-            queue = nc.scalar if q % 2 else nc.sync
-            queue.dma_start(
+            nc.scalar.dma_start(
                 out=out_2[:, 4 * q : 4 * q + 4, :].rearrange("g r m -> r g m").bitcast(I32),
                 in_=y_plane[32 * q : 32 * q + 4, :, :].bitcast(I32),
             )

@@ -91,11 +91,11 @@ def tile_list_net_misstatement_scores_kernel(
             nc.sync.dma_start(out=raw[:], in_=wo[g * PASS : (g + 1) * PASS, :].rearrange("(p j) c -> p j c", j=PACK))
             return [raw[:, :, n * PASS : (n + 1) * PASS] for n in range(N_GROUPS)]
 
-        def load_halves(place, group):
-            halves = [at(LAND + 8 * place + 4 * i, "w2_raw", [P, PACK, PASS // 2], F32) for i in range(2)]
+        def load_halves(place, w, g, group):
+            halves = [at(LAND + 8 * place + 4 * i, "half_raw", [P, PACK, PASS // 2], F32) for i in range(2)]
             for i in range(2):
                 first = group * PASS + i * PASS // 2
-                rows = w2[:, first : first + PASS // 2]
+                rows = w[g * PASS : (g + 1) * PASS, first : first + PASS // 2]
                 nc.sync.dma_start(out=halves[i][:], in_=rows.rearrange("(p j) c -> p j c", j=PACK))
             return halves
 
@@ -156,7 +156,7 @@ def tile_list_net_misstatement_scores_kernel(
         load_words(tab2, tab2_words[0])
         load_plane(nc.sync, tab2_plane, tab2_scales[0])
         nc.sync.dma_start(pick[:], pos1)
-        w2_raw = [load_halves(2, 0)]
+        w2_raw = [load_halves(2, w2, 0, 0)]
         w2_raw.append(load_weight(3, "w2_1", w2, 0, 1))
         for q in range(QUADRANTS):
             nc.sync.dma_start(
@@ -296,27 +296,30 @@ def tile_list_net_misstatement_scores_kernel(
         deal(nc.gpsimd, wu_first[:], wu_raw[:], 4)
         wu_codes = [wu_first[:]]
         staged_w2 = round_weight(w2_raw[2], stage("w2_2", ABOVE - 3), True)
-        wo_raw.append(load_weight(4, "wo21", wo, 2, 1))
+        wo_raw.append(load_halves(4, wo, 2, 1))
         picked = at(BELOW, "picked1", [P, PACK, M], F32)
         pick_all(1, 0, picked)
         diff = at(DIFF + 4, "diff1", [P, M * PACK], BF16)
         subtract(b, picked, diff)
         staged = [round_weight(wo_raw[i], stage("wo%d" % i, STAGE + 4 * (i % 4)), False) for i in range(4)]
-        signed = split_signs("d1", diff[:], LAST, LAST + 4, 2)
-        wo_q = [quantise_weight("wo%d" % i, 3 + i, staged[i], DIFF + 4 + i / 2) for i in range(2)]
+        wo_q = [quantise_weight("wo%d" % i, 3 + i, staged[i], D_PLANE + 2 + i / 2) for i in range(2)]
+        signed = split_signs("d1", diff[:], LAND + 40, LAND + 44, 2)
         w2_q.append(quantise_weight("w2_2", 2, staged_w2, DIFF + 5))
         quantise_signed(1, 0, signed)
         wo_q.append(quantise_weight("wo2", 5, staged[2], DIFF + 5.5))
         wo_q.append(quantise_weight("wo3", 6, staged[3], ABOVE))
         wu_last = at(STAGE + 7, "wu_last", [P, 2, N], I32)
-        for n in range(N_GROUPS):
-            cols = slice(n * PASS, (n + 1) * PASS)
-            deal(nc.gpsimd, wu_last[:, 0, cols], wu_rest[:, 0, cols], 4)
-        deal(nc.gpsimd, wu_last[:, 1, :], wu_rest[:, 1, :], 4)
+        for g in range(2):
+            deal(nc.gpsimd, wu_last[:, g, :], wu_rest[:, g, :], 4)
         wu_codes += [wu_last[:, 0, :], wu_last[:, 1, :]]
-        staged_last = [round_weight(wo_raw[i], stage("wo%d" % i, (STAGE, EXTRA)[i - 4]), False) for i in (4, 5)]
+        staged_last = [round_weight(wo_raw[4], stage("wo4", STAGE), False), stage("wo5", EXTRA)]
+        for i in range(2):
+            nc.scalar.copy(
+                out=staged_last[1].rearrange("p (t h m j) -> p h m j t", t=PACK, h=2, j=PACK)[:, i],
+                in_=wo_raw[5][i][:].rearrange("p j (m t) -> p m j t", t=PACK),
+            )
 
-        def add_pass(g, first, acc, n, first_slice, sides, closes):
+        def add_pass(g, first, acc, n, first_slice, sides, closes, opening=0):
             slices, width = acc.shape[1], acc.shape[2]
             for side in sides:
                 cols = slice(side * M + first, side * M + first + width)
@@ -334,7 +337,7 @@ def tile_list_net_misstatement_scores_kernel(
                         lhsT_scale=plane,
                         rhs=d_q[g][0][:, cols].bitcast(FP8X4),
                         rhs_scale=d_q[g][1][:, cols],
-                        start=(g == 0 and side == 1 and u == 0),
+                        start=(g == opening and side == 1 and u == 0),
                         stop=(closes and side == sides[-1] and u == slices - 1),
                     )
 
@@ -370,10 +373,10 @@ def tile_list_net_misstatement_scores_kernel(
         pick_all(2, 0, picked)
         diff = at(DIFF + 8, "diff2", [P, HALF * PACK], BF16)
         subtract(b, picked, diff)
-        b = ledger_features(2, 2, 4)
-        banks3 = [bank(5, "y3_acc0", [P, PACK, CHUNK])]
-        for g in range(2):
-            add_pass(g, HALF + CHUNK, banks3[0], 0, 0, (1, 0), False)
+        b = ledger_features(2, 2, 5)
+        banks3 = [bank(4, "y3_acc0", [P, PACK, CHUNK])]
+        for g in (1, 0):
+            add_pass(g, HALF + CHUNK, banks3[0], 0, 0, (1, 0), False, 1)
         wo_q.append(quantise_weight("wo4", 7, staged_last[0], LAND + 8))
         signed = split_signs("d20", diff[:, 0 : 2 * BANK], LAST, LAST + 2, 2)
         wo_q.append(quantise_weight("wo5", 8, staged_last[1], LAND + 8.5))
@@ -388,9 +391,9 @@ def tile_list_net_misstatement_scores_kernel(
 
         picked = at(LAND + 24, "picked3", [P, PACK, CHUNK], F32)
         pick_columns(2, HALF, range(PACK), picked)
-        diff = at(LAND + 32, "diff3", [P, 2 * BANK], BF16)
+        diff = at(LAND + 36, "diff3", [P, 2 * BANK], BF16)
         subtract([b], picked, diff[:, 0:BANK])
-        b = ledger_features(2, 3, 4)
+        b = ledger_features(2, 3, 5)
         banks3.append(bank(0, "y3_acc1", [P, PACK, CHUNK]))
         for g in range(2):
             add_pass(g, HALF + CHUNK, banks3[1], 1, 0, (1, 0), False)
@@ -398,7 +401,7 @@ def tile_list_net_misstatement_scores_kernel(
         quantise_signed(2, HALF, signed)
         for n in range(N_GROUPS):
             add_pass(2, HALF, banks2[n], n, 0, (1, 0), True)
-        picked = at(LAND + 34, "picked4", [P, PACK, CHUNK], F32)
+        picked = at(LAND + 38, "picked4", [P, PACK, CHUNK], F32)
         pick_columns(2, HALF + CHUNK, range(PACK), picked)
         subtract([b], picked, diff[:, BANK : 2 * BANK])
         signed = split_signs("d23", diff[:, BANK : 2 * BANK], LAST + 6, LAST + 7, 1)

@@ -13,6 +13,7 @@ U16 = mybir.dt.uint16
 U8 = mybir.dt.uint8
 FP8X4 = mybir.dt.float8_e4m3fn_x4
 FP4X4 = mybir.dt.float4_e2m1fn_x4
+RELU = mybir.ActivationFunctionType.Relu
 COPY = mybir.ActivationFunctionType.Copy
 ADD = mybir.AluOpType.add
 MULT = mybir.AluOpType.mult
@@ -249,14 +250,17 @@ def tile_list_net_misstatement_scores_kernel(
                     op=SUBTRACT,
                 )
 
-        def split_signs(name, diff, kb, below_kb, parts):
+        def split_signs(name, diff, kb, below_kb, parts, scalar_max=False):
             width = diff.shape[1]
             above = at(kb, name + "_above", [P, width], BF16)
             below = at(below_kb, name + "_below", [P, width], BF16)
             for c in range(0, width, width // parts):
                 cols = slice(c, c + width // parts)
                 nc.vector.tensor_scalar_min(out=below[:, cols], in0=diff[:, cols], scalar1=0.0)
-                nc.vector.tensor_scalar_max(out=above[:, cols], in0=diff[:, cols], scalar1=0.0)
+                if scalar_max:
+                    nc.scalar.activation(out=above[:, cols], in_=diff[:, cols], func=RELU)
+                else:
+                    nc.vector.tensor_scalar_max(out=above[:, cols], in0=diff[:, cols], scalar1=0.0)
             return above, below
 
         def quantise_signed(g, first, signed):
@@ -301,14 +305,14 @@ def tile_list_net_misstatement_scores_kernel(
         pick_all(1, 0, picked)
         diff = at(DIFF + 4, "diff1", [P, M * PACK], BF16)
         subtract(b, picked, diff)
-        staged = [round_weight(wo_raw[i], stage("wo%d" % i, STAGE + 4 * (i % 4)), False) for i in range(4)]
+        staged = [round_weight(wo_raw[i], stage("wo%d" % i, STAGE + 4 * i), False) for i in range(3)]
         wo_q = [quantise_weight("wo%d" % i, 3 + i, staged[i], D_PLANE + 2 + i / 2) for i in range(2)]
-        signed = split_signs("d1", diff[:], LAND + 40, LAND + 44, 2)
-        w2_q.append(quantise_weight("w2_2", 2, staged_w2, DIFF + 5))
+        signed = split_signs("d1", diff[:], LAND, LAND + 44, 2, True)
+        staged.append(round_weight(wo_raw[3], stage("wo3", STAGE + 12), False))
+        w2_q.append(quantise_weight("w2_2", 2, staged_w2, BELOW))
+        wo_q.append(quantise_weight("wo2", 5, staged[2], BELOW + 0.5))
         quantise_signed(1, 0, signed)
-        wo_q.append(quantise_weight("wo2", 5, staged[2], DIFF + 5.5))
-        wo_q.append(quantise_weight("wo3", 6, staged[3], ABOVE))
-        wu_last = at(STAGE + 7, "wu_last", [P, 2, N], I32)
+        wu_last = at(LAND, "wu_last", [P, 2, N], I32)
         for g in range(2):
             deal(nc.gpsimd, wu_last[:, g, :], wu_rest[:, g, :], 4)
         wu_codes += [wu_last[:, 0, :], wu_last[:, 1, :]]
@@ -363,23 +367,31 @@ def tile_list_net_misstatement_scores_kernel(
         b = [ledger_features(2, c, 4 + c) for c in range(2)]
         banks0 = [bank(i, "y0_acc%d" % i, [P, 2, HALF]) for i in range(4)]
         banks2 = [bank(6 + n, "y2_acc%d" % n, [P, PACK, CHUNK]) for n in range(N_GROUPS)]
-        for g in range(2):
-            for side in (1 - g, g):
-                for i, acc in enumerate(banks0):
-                    add_pass(g, 0, acc, i // 2, 2 * (i % 2), (side,), False)
-                for n in range(N_GROUPS):
-                    add_pass(g, HALF, banks2[n], n, 0, (side,), False)
-        picked = at(LAND + 8, "picked2", [P, PACK, HALF], F32)
+
+        def early_pass(g, side, groups):
+            for n in groups:
+                for i in (2 * n, 2 * n + 1):
+                    add_pass(g, 0, banks0[i], n, 2 * (i % 2), (side,), False)
+            for n in groups:
+                add_pass(g, HALF, banks2[n], n, 0, (side,), False)
+
+        early_pass(0, 1, range(N_GROUPS))
+        early_pass(0, 0, range(N_GROUPS))
+        early_pass(1, 0, [0])
+        early_pass(1, 1, range(N_GROUPS))
+        picked = at(DIFF + 4, "picked2", [P, PACK, HALF], F32)
         pick_all(2, 0, picked)
         diff = at(DIFF + 8, "diff2", [P, HALF * PACK], BF16)
         subtract(b, picked, diff)
+        wo_q.append(quantise_weight("wo3", 6, staged[3], DIFF + 4))
+        early_pass(1, 0, [1])
         b = ledger_features(2, 2, 5)
         banks3 = [bank(4, "y3_acc0", [P, PACK, CHUNK])]
         for g in (1, 0):
             add_pass(g, HALF + CHUNK, banks3[0], 0, 0, (1, 0), False, 1)
-        wo_q.append(quantise_weight("wo4", 7, staged_last[0], LAND + 8))
+        wo_q.append(quantise_weight("wo4", 7, staged_last[0], DIFF + 4.5))
         signed = split_signs("d20", diff[:, 0 : 2 * BANK], LAST, LAST + 2, 2)
-        wo_q.append(quantise_weight("wo5", 8, staged_last[1], LAND + 8.5))
+        wo_q.append(quantise_weight("wo5", 8, staged_last[1], DIFF + 5))
         quantise_signed(2, 0, signed)
         for i, acc in enumerate(banks0):
             add_pass(2, 0, acc, i // 2, 2 * (i % 2), (1, 0), True)

@@ -47,7 +47,7 @@ BELOW = 204
 LAST = 212
 G_STAGE = 220
 W2_PLANE = 226
-EXTRA = 227
+EXTRA = 230
 
 
 def tile_list_net_misstatement_scores_kernel(
@@ -92,8 +92,8 @@ def tile_list_net_misstatement_scores_kernel(
             nc.sync.dma_start(out=raw[:], in_=wo[g * PASS : (g + 1) * PASS, :].rearrange("(p j) c -> p j c", j=PACK))
             return [raw[:, :, n * PASS : (n + 1) * PASS] for n in range(N_GROUPS)]
 
-        def load_halves(place, w, g, group):
-            halves = [at(LAND + 8 * place + 4 * i, "half_raw", [P, PACK, PASS // 2], F32) for i in range(2)]
+        def load_halves(places, w, g, group):
+            halves = [at(kb, "half_raw", [P, PACK, PASS // 2], F32) for kb in places]
             for i in range(2):
                 first = group * PASS + i * PASS // 2
                 rows = w[g * PASS : (g + 1) * PASS, first : first + PASS // 2]
@@ -135,7 +135,6 @@ def tile_list_net_misstatement_scores_kernel(
         idx = keep.tile([P, S // LIST], U16, name="idx")
         idx2 = keep.tile([P, M // LIST], U16, name="idx2")
         pick = keep.tile([P, M // LIST], U16, name="pick")
-        gains = keep.tile([P, N_GROUPS, PACK], F32, name="gains")
         tab_plane = at(TAB_PLANE, "tab_plane", [P, T], U8)
         w1_raw_plane = at(W1_RAW_PLANE, "w1_raw_plane", [P, H], U8)
         tab2_plane = at(TAB2_PLANE, "tab2_plane", [P, T], U8)
@@ -157,7 +156,7 @@ def tile_list_net_misstatement_scores_kernel(
         load_words(tab2, tab2_words[0])
         load_plane(nc.sync, tab2_plane, tab2_scales[0])
         nc.sync.dma_start(pick[:], pos1)
-        w2_raw = [load_halves(2, w2, 0, 0)]
+        w2_raw = [load_halves((LAND + 16, LAND + 20), w2, 0, 0)]
         w2_raw.append(load_weight(3, "w2_1", w2, 0, 1))
         for q in range(QUADRANTS):
             nc.sync.dma_start(
@@ -168,7 +167,6 @@ def tile_list_net_misstatement_scores_kernel(
         load_words(wu_raw, wu_words[0])
         wo_raw = load_pass(LAND + 40, 0)
         w2_raw.append(load_weight(4, "w2_2", w2, 0, 2))
-        nc.sync.dma_start(out=gains[:], in_=gain.rearrange("(g p t) -> p g t", p=P, t=PACK))
 
         w1_codes = [at(kb, "w1_codes", [P, 2 * PASS], U8) for kb in (W1_CODES, W1_CODES + 1, STAGE + 12)]
         w1_plane = [at(W1_PLANE + g / 2, "w1_plane%d" % g, [P, PASS], U8) for g in range(R_PASSES)]
@@ -287,11 +285,12 @@ def tile_list_net_misstatement_scores_kernel(
         w2_q.append(quantise_weight("w2_1", 1, staged, LAST + 5.5))
         d_q = [
             (at(D_CODES + 4 * g, "d_codes", [P, 2 * M], U32), at(kb, "d_plane", [P, 2 * M], U8))
-            for g, kb in enumerate((G_STAGE + 2, D_PLANE, D_PLANE + 1))
+            for g, kb in enumerate((G_STAGE + 5, D_PLANE, D_PLANE + 1))
         ]
 
         signed = split_signs("d0", diff[:], ABOVE, BELOW, 2)
         quantise_signed(0, 0, signed)
+        wo_raw.append(load_halves((G_STAGE + 1, W2_PLANE), wo, 2, 1))
 
         b = [ledger_features(1, c, 4 + c) for c in range(4)]
         wu_planes = at(ABOVE + 1, "wu_planes", [P, N], U8)
@@ -299,8 +298,9 @@ def tile_list_net_misstatement_scores_kernel(
         wu_first = at(ABOVE + 2, "wu_first", [P, N], I32)
         deal(nc.gpsimd, wu_first[:], wu_raw[:], 4)
         wu_codes = [wu_first[:]]
+        gains = at(LAND + 56, "gains", [P, N_GROUPS, PACK], F32)
+        nc.sync.dma_start(out=gains[:], in_=gain.rearrange("(g p t) -> p g t", p=P, t=PACK))
         staged_w2 = round_weight(w2_raw[2], stage("w2_2", ABOVE - 3), True)
-        wo_raw.append(load_halves(4, wo, 2, 1))
         picked = at(BELOW, "picked1", [P, PACK, M], F32)
         pick_all(1, 0, picked)
         diff = at(DIFF + 4, "diff1", [P, M * PACK], BF16)
@@ -403,7 +403,7 @@ def tile_list_net_misstatement_scores_kernel(
 
         picked = at(LAND + 24, "picked3", [P, PACK, CHUNK], F32)
         pick_columns(2, HALF, range(PACK), picked)
-        diff = at(LAND + 36, "diff3", [P, 2 * BANK], BF16)
+        diff = at(W2_PLANE, "diff3", [P, 2 * BANK], BF16)
         subtract([b], picked, diff[:, 0:BANK])
         b = ledger_features(2, 3, 5)
         banks3.append(bank(0, "y3_acc1", [P, PACK, CHUNK]))
@@ -413,7 +413,7 @@ def tile_list_net_misstatement_scores_kernel(
         quantise_signed(2, HALF, signed)
         for n in range(N_GROUPS):
             add_pass(2, HALF, banks2[n], n, 0, (1, 0), True)
-        picked = at(LAND + 38, "picked4", [P, PACK, CHUNK], F32)
+        picked = at(W2_PLANE + 2, "picked4", [P, PACK, CHUNK], F32)
         pick_columns(2, HALF + CHUNK, range(PACK), picked)
         subtract([b], picked, diff[:, BANK : 2 * BANK])
         signed = split_signs("d23", diff[:, BANK : 2 * BANK], LAST + 6, LAST + 7, 1)

@@ -69,10 +69,11 @@ def tile_list_net_misstatement_scores_kernel(
         def load_words(words, source):
             nc.sync.dma_start(out=words[:], in_=source.rearrange("p c i -> p (c i)").bitcast(I32))
 
-        def load_plane(queue, plane, rows):
+        def load_plane(queue, plane, rows, first=0):
             for q in range(QUADRANTS):
                 queue.dma_start(
-                    out=plane[32 * q : 32 * q + 4, :].bitcast(I32), in_=rows[4 * q : 4 * q + 4, :].bitcast(I32)
+                    out=plane[32 * q + first : 32 * q + first + 4, :].bitcast(I32),
+                    in_=rows[4 * q : 4 * q + 4, :].bitcast(I32),
                 )
 
         def deal(engine, dealt, natural, run):
@@ -154,13 +155,13 @@ def tile_list_net_misstatement_scores_kernel(
         load_plane(nc.sync, w1_raw_plane, w1_scales[0])
         tab2 = at(LAND + 8, "tab2", [P, T], I32)
         load_words(tab2, tab2_words[0])
-        load_plane(nc.sync, tab2_plane, tab2_scales[0])
+        load_plane(nc.sync, tab2_plane, tab2_scales[0], 4)
         nc.sync.dma_start(pick[:], pos1)
         w2_raw = [load_halves((LAND + 16, LAND + 20), w2, 0, 0)]
         w2_raw.append(load_weight(3, "w2_1", w2, 0, 1))
         for q in range(QUADRANTS):
             nc.sync.dma_start(
-                out=wu_raw_planes[32 * q : 32 * q + 4 * R_PASSES, :].bitcast(I32),
+                out=wu_raw_planes[32 * q + 4 : 32 * q + 4 + 4 * R_PASSES, :].bitcast(I32),
                 in_=wu_scales[:, 4 * q : 4 * q + 4, :].bitcast(I32),
             )
         wu_raw = at(LAND + 56, "wu_raw", [P, N], I32)
@@ -222,7 +223,7 @@ def tile_list_net_misstatement_scores_kernel(
                     lhsT=codes[:, P * t : P * (t + 1)].bitcast(FP8X4),
                     lhsT_scale=plane[:, P * t : P * (t + 1)],
                     rhs=v2_codes[:, cols].bitcast(FP8X4),
-                    rhs_scale=v2_plane[:, cols],
+                    rhs_scale=v2_plane[4:P, cols],
                     start=True,
                     stop=True,
                 )
@@ -334,7 +335,7 @@ def tile_list_net_misstatement_scores_kernel(
                         plane = wo_q[2 * g + n][1][:, P * t : P * (t + 1)]
                     else:
                         codes = wu_codes[g][:, n * PASS + P * t : n * PASS + P * (t + 1)]
-                        plane = wu_planes[4 * g : P, n * PASS + P * t : n * PASS + P * (t + 1)]
+                        plane = wu_planes[4 + 4 * g : P, n * PASS + P * t : n * PASS + P * (t + 1)]
                     nc.tensor.matmul_mx(
                         out=acc[:, u, :],
                         lhsT=codes.bitcast(FP8X4),

@@ -122,8 +122,8 @@ def tile_list_net_misstatement_scores_kernel(
                 )
             else:
                 nc.scalar.copy(
-                    out=staged.rearrange("p (t m j) -> p m j t", t=PACK, j=PACK),
-                    in_=raw.rearrange("p j (m t) -> p m j t", t=PACK),
+                    out=staged.rearrange("p (t m h l) -> p m h t l", t=PACK, h=2, l=2),
+                    in_=raw.rearrange("p (h l) (m t) -> p m h t l", t=PACK, l=2),
                 )
             return staged
 
@@ -320,8 +320,8 @@ def tile_list_net_misstatement_scores_kernel(
         staged_last = [round_weight(wo_raw[4], stage("wo4", STAGE), False), stage("wo5", EXTRA)]
         for i in range(2):
             nc.scalar.copy(
-                out=staged_last[1].rearrange("p (t h m j) -> p h m j t", t=PACK, h=2, j=PACK)[:, i],
-                in_=wo_raw[5][i][:].rearrange("p j (m t) -> p m j t", t=PACK),
+                out=staged_last[1].rearrange("p (t u m h l) -> p u m h t l", t=PACK, u=2, h=2, l=2)[:, i],
+                in_=wo_raw[5][i][:].rearrange("p (h l) (m t) -> p m h t l", t=PACK, l=2),
             )
 
         def add_pass(g, first, acc, n, first_slice, sides, closes, opening=0):

from contextlib import ExitStack

import concourse.mybir as mybir

K, H, N, T, S, M = 512, 1536, 1024, 2048, 1024, 512
FLOPS = 2 * K * H * S + 2 * K * H * M + 4 * H * N * M

F32 = mybir.dt.float32
BF16 = mybir.dt.bfloat16
I32 = mybir.dt.int32
U32 = mybir.dt.uint32
U16 = mybir.dt.uint16
U8 = mybir.dt.uint8
FP8X4 = mybir.dt.float8_e4m3fn_x4
FP4X4 = mybir.dt.float4_e2m1fn_x4
RELU = mybir.ActivationFunctionType.Relu
COPY = mybir.ActivationFunctionType.Copy
ADD = mybir.AluOpType.add
MULT = mybir.AluOpType.mult
SUBTRACT = mybir.AluOpType.subtract

P = 128
PACK = 4
PASS = P * PACK
BANK = 512
LIST = 16
QUADRANTS = 4
R_PASSES = H // PASS
N_GROUPS = N // PASS
HALF = M // 2
CHUNK = BANK // PACK
KB = 1024

H_ROWS = 0
LAND = 48
WU_RAW = 96
W1_RAW, W1_RAW_PLANE, W1_CODES, W1_PLANE = 108, 111, 113, 116
TAB_PLANE, TAB2_PLANE, WU_RAW_PLANES = 118, 120, 122
V2_CODES, V2_PLANE = 123, 125
D_PLANE = 126
W_CODES = 131
D_CODES = 149
DIFF = 164
STAGE = 176
ABOVE = 198
BELOW = 204
LAST = 212
G_STAGE = 220
W2_PLANE = 226
EXTRA = 230


def tile_list_net_misstatement_scores_kernel(
    tc, tab_words, tab_scales, offs, pos1, tab2_words, tab2_scales, offs2,
    w1_words, w1_scales, w2, wo, wu_words, wu_scales, gain, out_0, out_1, out_2,
):
    nc = tc.nc
    with ExitStack() as ctx:
        keep = ctx.enter_context(tc.tile_pool(name="keep", bufs=1))
        sbuf = ctx.enter_context(tc.tile_pool(name="sbuf", bufs=1))
        psum = ctx.enter_context(tc.psum_pool(name="psum", bufs=1))

        def at(kb, name, shape, dtype):
            return sbuf.tile(shape, dtype, name=name, offset=int(kb * KB), align_bytes=64)

        def bank(number, name, shape):
            return psum.tile(shape, F32, name=name, tag="bank%d" % number)

        def load_words(words, source):
            nc.sync.dma_start(out=words[:], in_=source.rearrange("p c i -> p (c i)").bitcast(I32))

        def load_plane(queue, plane, rows, first=0):
            for q in range(QUADRANTS):
                queue.dma_start(
                    out=plane[32 * q + first : 32 * q + first + 4, :].bitcast(I32),
                    in_=rows[4 * q : 4 * q + 4, :].bitcast(I32),
                )

        def deal(engine, dealt, natural, run):
            engine.tensor_copy(
                out=dealt.rearrange("p (g t m i) -> p g m t i", t=PACK, m=P // run, i=run),
                in_=natural.rearrange("p (g m i t) -> p g m t i", t=PACK, m=P // run, i=run),
            )

        def load_weight(place, name, w, g, group):
            raw = at(LAND + 8 * place, name + "_raw", [P, PACK, PASS], F32)
            rows = w[g * PASS : (g + 1) * PASS, group * PASS : (group + 1) * PASS]
            nc.sync.dma_start(out=raw[:], in_=rows.rearrange("(p j) c -> p j c", j=PACK))
            return raw[:]

        def load_pass(kb, g):
            raw = at(kb, "wo_raw", [P, PACK, N], F32)
            nc.sync.dma_start(out=raw[:], in_=wo[g * PASS : (g + 1) * PASS, :].rearrange("(p j) c -> p j c", j=PACK))
            return [raw[:, :, n * PASS : (n + 1) * PASS] for n in range(N_GROUPS)]

        def load_halves(places, w, g, group):
            halves = [at(kb, "half_raw", [P, PACK, PASS // 2], F32) for kb in places]
            for i in range(2):
                first = group * PASS + i * PASS // 2
                rows = w[g * PASS : (g + 1) * PASS, first : first + PASS // 2]
                nc.sync.dma_start(out=halves[i][:], in_=rows.rearrange("(p j) c -> p j c", j=PACK))
            return halves

        def round_halves(halves, staged):
            for i in range(2):
                nc.gpsimd.tensor_scalar(
                    out=staged.rearrange("p (t h m j) -> p h m t j", t=PACK, h=2, j=PACK)[:, i],
                    in0=halves[i][:].rearrange("p j (m t) -> p m t j", t=PACK),
                    scalar1=1.0, scalar2=0.0, op0=MULT, op1=ADD,
                )
            return staged

        def stage(name, kb):
            return at(kb, name + "_staged", [P, PASS * PACK], BF16)[:]

        def round_weight(raw, staged, on_gpsimd):
            if on_gpsimd:
                nc.gpsimd.tensor_scalar(
                    out=staged.rearrange("p (t m j) -> p m t j", t=PACK, j=PACK),
                    in0=raw.rearrange("p j (m t) -> p m t j", t=PACK),
                    scalar1=1.0, scalar2=0.0, op0=MULT, op1=ADD,
                )
            else:
                nc.scalar.copy(
                    out=staged.rearrange("p (t m h l) -> p m h t l", t=PACK, h=2, l=2),
                    in_=raw.rearrange("p (h l) (m t) -> p m h t l", t=PACK, l=2),
                )
            return staged

        def quantise_weight(name, number, staged, plane_kb):
            codes = at(W_CODES + 2 * number, name + "_codes", [P, PASS], U32)
            plane = at(plane_kb, name + "_plane", [P, PASS], U8)
            nc.vector.quantize_mx(out=codes[:].bitcast(FP8X4), scales=plane[:], in_=staged)
            return codes, plane

        idx = keep.tile([P, S // LIST], U16, name="idx")
        idx2 = keep.tile([P, M // LIST], U16, name="idx2")
        pick = keep.tile([P, M // LIST], U16, name="pick")
        tab_plane = at(TAB_PLANE, "tab_plane", [P, T], U8)
        w1_raw_plane = at(W1_RAW_PLANE, "w1_raw_plane", [P, H], U8)
        tab2_plane = at(TAB2_PLANE, "tab2_plane", [P, T], U8)
        wu_raw_planes = at(WU_RAW_PLANES, "wu_raw_planes", [P, N], U8)
        for engine, plane in (
            (nc.gpsimd, tab_plane), (nc.vector, w1_raw_plane), (nc.vector, tab2_plane), (nc.gpsimd, wu_raw_planes)
        ):
            engine.memset(plane[:].bitcast(I32), 0)

        nc.sync.dma_start(idx[:], offs)
        w1_raw = at(W1_RAW, "w1_raw", [P, 2 * H], U8)
        nc.sync.dma_start(out=w1_raw[:].bitcast(I32), in_=w1_words[0].bitcast(I32))
        load_plane(nc.sync, tab_plane, tab_scales[0])
        tab = at(LAND, "tab", [P, T], I32)
        load_words(tab, tab_words[0])
        nc.sync.dma_start(idx2[:], offs2)
        load_plane(nc.sync, w1_raw_plane, w1_scales[0])
        tab2 = at(LAND + 8, "tab2", [P, T], I32)
        load_words(tab2, tab2_words[0])
        load_plane(nc.sync, tab2_plane, tab2_scales[0], 4)
        nc.sync.dma_start(pick[:], pos1)
        w2_raw = [load_halves((LAND + 16, LAND + 20), w2, 0, 0)]
        w2_raw.append(load_weight(3, "w2_1", w2, 0, 1))
        for q in range(QUADRANTS):
            nc.sync.dma_start(
                out=wu_raw_planes[32 * q + 4 : 32 * q + 4 + 4 * R_PASSES, :].bitcast(I32),
                in_=wu_scales[:, 4 * q : 4 * q + 4, :].bitcast(I32),
            )
        wu_raw = at(LAND + 56, "wu_raw", [P, N], I32)
        load_words(wu_raw, wu_words[0])
        wo_raw = load_pass(LAND + 40, 0)
        w2_raw.append(load_weight(4, "w2_2", w2, 0, 2))

        w1_codes = [at(kb, "w1_codes", [P, 2 * PASS], U8) for kb in (W1_CODES, W1_CODES + 1, STAGE + 12)]
        w1_plane = [at(W1_PLANE + g / 2, "w1_plane%d" % g, [P, PASS], U8) for g in range(R_PASSES)]
        deal(nc.vector, w1_codes[0][:].bitcast(U16), w1_raw[:, 0 : 2 * PASS].bitcast(U16), 8)
        for g in range(R_PASSES):
            deal(nc.gpsimd, w1_plane[g][:], w1_raw_plane[:, g * PASS : (g + 1) * PASS], 16)
        for g in range(1, R_PASSES):
            nc.gpsimd.tensor_copy(
                out=w1_codes[g][:].rearrange("p (t m i b) -> p m t i b", t=PACK, i=8, b=2),
                in_=w1_raw[:, 2 * PASS * g : 2 * PASS * (g + 1)].rearrange("p (m i t b) -> p m t i b", t=PACK, i=8, b=2),
            )
        v_plane = at(STAGE + 8, "v_plane", [P, S], U8)
        nc.vector.tensor_copy(out=v_plane[:], in_=tab_plane[:].indirect(idx[:]))
        v_codes = []
        for s in range(S // BANK):
            codes = at(STAGE + 4 * s, "v_codes%d" % s, [P, BANK], U32)
            offsets = idx[:, s * BANK // LIST : (s + 1) * BANK // LIST]
            nc.vector.tensor_copy(out=codes[:], in_=tab[:].bitcast(U32).indirect(offsets))
            v_codes.append(codes)
        v2_codes = at(V2_CODES, "v2_codes", [P, M], U32)
        nc.vector.tensor_copy(out=v2_codes[:], in_=tab2[:].bitcast(U32).indirect(idx2[:]))
        v2_plane = at(V2_PLANE, "v2_plane", [P, M], U8)
        nc.vector.tensor_copy(out=v2_plane[:], in_=tab2_plane[:].indirect(idx2[:]))
        staged = round_halves(w2_raw[0], stage("w2_0", G_STAGE))
        w2_q = [quantise_weight("w2_0", 0, staged, W2_PLANE)]
        wo_raw.append(load_weight(0, "wo10", wo, 1, 0))
        wo_raw.append(load_weight(1, "wo11", wo, 1, 1))

        def summary_features(g):
            rows = [at(H_ROWS + 4 * (PACK * g + t), "h%d%d" % (g, t), [P, S], F32) for t in range(PACK)]
            for t in range(PACK):
                for s in range(S // BANK):
                    acc = bank((2 * t + s) % 4 + (4 if g < 2 and t >= 2 else 0), "h_acc", [P, BANK])
                    nc.tensor.matmul_mx(
                        out=acc[:],
                        lhsT=w1_codes[g][:, 2 * P * t : 2 * P * (t + 1)].bitcast(FP4X4),
                        lhsT_scale=w1_plane[g][:, P * t : P * (t + 1)],
                        rhs=v_codes[s][:].bitcast(FP8X4),
                        rhs_scale=v_plane[:, s * BANK : (s + 1) * BANK],
                        start=True,
                        stop=True,
                    )
                    nc.scalar.copy(out=rows[t][:, s * BANK : (s + 1) * BANK], in_=acc[:])
            return rows

        def ledger_features(g, c, number):
            codes, plane = w2_q[g]
            cols = slice(c * CHUNK, (c + 1) * CHUNK)
            acc = bank(number, "b_acc%d%d" % (g, c), [P, PACK, CHUNK])
            for t in range(PACK):
                nc.tensor.matmul_mx(
                    out=acc[:, t, :],
                    lhsT=codes[:, P * t : P * (t + 1)].bitcast(FP8X4),
                    lhsT_scale=plane[:, P * t : P * (t + 1)],
                    rhs=v2_codes[:, cols].bitcast(FP8X4),
                    rhs_scale=v2_plane[4:P, cols],
                    start=True,
                    stop=True,
                )
            return acc

        def pick_columns(g, first, slices, picked):
            offsets = pick[:, first // LIST : (first + picked.shape[2]) // LIST]
            for t in slices:
                nc.vector.tensor_copy(out=picked[:, t, :], in_=h[g][t][:].indirect(offsets))

        def pick_all(g, first, picked):
            half = picked.shape[2] // 2
            pick_columns(g, first, range(PACK - 1), picked)
            for part in range(2):
                pick_columns(g, first + part * half, [PACK - 1], picked[:, :, part * half : (part + 1) * half])

        def subtract(banks, picked, diff):
            for c, acc in enumerate(banks):
                nc.vector.tensor_tensor(
                    out=diff[:, c * BANK : (c + 1) * BANK].rearrange("p (c i t) -> p c t i", i=2, t=PACK),
                    in0=acc[:].rearrange("p t (c i) -> p c t i", i=2),
                    in1=picked[:, :, c * CHUNK : (c + 1) * CHUNK].rearrange("p t (c i) -> p c t i", i=2),
                    op=SUBTRACT,
                )

        def split_signs(name, diff, kb, below_kb, parts, scalar_max=False):
            width = diff.shape[1]
            above = at(kb, name + "_above", [P, width], BF16)
            below = at(below_kb, name + "_below", [P, width], BF16)
            for c in range(0, width, width // parts):
                cols = slice(c, c + width // parts)
                nc.vector.tensor_scalar_min(out=below[:, cols], in0=diff[:, cols], scalar1=0.0)
                if scalar_max:
                    nc.scalar.activation(out=above[:, cols], in_=diff[:, cols], func=RELU)
                else:
                    nc.vector.tensor_scalar_max(out=above[:, cols], in0=diff[:, cols], scalar1=0.0)
            return above, below

        def quantise_signed(g, first, signed):
            for side in (1, 0):
                words = signed[side].shape[1] // PACK
                cols = slice(side * M + first, side * M + first + words)
                nc.vector.quantize_mx(out=d_q[g][0][:, cols].bitcast(FP8X4), scales=d_q[g][1][:, cols], in_=signed[side][:])

        h = [summary_features(0)]
        h.append(summary_features(1))
        b = [ledger_features(0, c, c) for c in range(4)]
        h.append(summary_features(2))
        staged = round_weight(w2_raw[1], stage("w2_1", G_STAGE + 2), True)
        early = at(LAST, "picked0", [P, PACK, M - CHUNK], F32)
        pick_columns(0, 0, range(PACK), early)
        late = at(LAND + 20, "picked0_late", [P, PACK, CHUNK], F32)
        pick_columns(0, M - CHUNK, range(PACK), late)
        diff = at(DIFF, "diff0", [P, M * PACK], BF16)
        subtract(b[0:3], early, diff)
        subtract(b[3:4], late, diff[:, 3 * BANK : 4 * BANK])
        wu_rest = at(LAND + 16, "wu_rest", [P, 2, N], I32)
        nc.sync.dma_start(out=wu_rest[:], in_=wu_words[1:3].rearrange("a p c i -> p a (c i)").bitcast(I32))
        wo_raw.append(load_weight(3, "wo20", wo, 2, 0))
        w2_q.append(quantise_weight("w2_1", 1, staged, LAST + 5.5))
        d_q = [
            (at(D_CODES + 4 * g, "d_codes", [P, 2 * M], U32), at(kb, "d_plane", [P, 2 * M], U8))
            for g, kb in enumerate((G_STAGE + 5, D_PLANE, D_PLANE + 1))
        ]

        signed = split_signs("d0", diff[:], ABOVE, BELOW, 2)
        quantise_signed(0, 0, signed)
        wo_raw.append(load_halves((G_STAGE + 1, W2_PLANE), wo, 2, 1))

        b = [ledger_features(1, c, 4 + c) for c in range(4)]
        wu_planes = at(ABOVE + 1, "wu_planes", [P, N], U8)
        deal(nc.gpsimd, wu_planes[:], wu_raw_planes[:], 16)
        wu_first = at(ABOVE + 2, "wu_first", [P, N], I32)
        deal(nc.gpsimd, wu_first[:], wu_raw[:], 4)
        wu_codes = [wu_first[:]]
        gains = at(LAND + 56, "gains", [P, N_GROUPS, PACK], F32)
        nc.sync.dma_start(out=gains[:], in_=gain.rearrange("(g p t) -> p g t", p=P, t=PACK))
        staged_w2 = round_weight(w2_raw[2], stage("w2_2", ABOVE - 3), True)
        picked = at(BELOW, "picked1", [P, PACK, M], F32)
        pick_all(1, 0, picked)
        diff = at(DIFF + 4, "diff1", [P, M * PACK], BF16)
        subtract(b, picked, diff)
        staged = [round_weight(wo_raw[i], stage("wo%d" % i, STAGE + 4 * i), False) for i in range(3)]
        wo_q = [quantise_weight("wo%d" % i, 3 + i, staged[i], D_PLANE + 2 + i / 2) for i in range(2)]
        signed = split_signs("d1", diff[:], LAND, LAND + 44, 2, True)
        staged.append(round_weight(wo_raw[3], stage("wo3", STAGE + 12), False))
        w2_q.append(quantise_weight("w2_2", 2, staged_w2, BELOW))
        wo_q.append(quantise_weight("wo2", 5, staged[2], BELOW + 0.5))
        quantise_signed(1, 0, signed)
        wu_last = at(LAND, "wu_last", [P, 2, N], I32)
        for g in range(2):
            deal(nc.gpsimd, wu_last[:, g, :], wu_rest[:, g, :], 4)
        wu_codes += [wu_last[:, 0, :], wu_last[:, 1, :]]
        staged_last = [round_weight(wo_raw[4], stage("wo4", STAGE), False), stage("wo5", EXTRA)]
        for i in range(2):
            nc.scalar.copy(
                out=staged_last[1].rearrange("p (t u m h l) -> p u m h t l", t=PACK, u=2, h=2, l=2)[:, i],
                in_=wo_raw[5][i][:].rearrange("p (h l) (m t) -> p m h t l", t=PACK, l=2),
            )

        def add_pass(g, first, acc, n, first_slice, sides, closes, opening=0):
            slices, width = acc.shape[1], acc.shape[2]
            for side in sides:
                cols = slice(side * M + first, side * M + first + width)
                for u in range(slices):
                    t = first_slice + u
                    if side == 0:
                        codes = wo_q[2 * g + n][0][:, P * t : P * (t + 1)]
                        plane = wo_q[2 * g + n][1][:, P * t : P * (t + 1)]
                    else:
                        codes = wu_codes[g][:, n * PASS + P * t : n * PASS + P * (t + 1)]
                        plane = wu_planes[4 + 4 * g : P, n * PASS + P * t : n * PASS + P * (t + 1)]
                    nc.tensor.matmul_mx(
                        out=acc[:, u, :],
                        lhsT=codes.bitcast(FP8X4),
                        lhsT_scale=plane,
                        rhs=d_q[g][0][:, cols].bitcast(FP8X4),
                        rhs_scale=d_q[g][1][:, cols],
                        start=(g == opening and side == 1 and u == 0),
                        stop=(closes and side == sides[-1] and u == slices - 1),
                    )

        def scale_scores(n, first, sums, y):
            for t in range(PACK):
                nc.scalar.activation(out=y[:, t, :], in_=sums[t], func=COPY, scale=gains[:, n, t : t + 1])

        def store_scores(queue, n, first, y):
            rows = out_0[n * PASS : (n + 1) * PASS, first : first + y.shape[2]]
            queue.dma_start(out=rows.rearrange("(p t) m -> p t m", t=PACK), in_=y[:])

        def round_scores(copy, rounded, y):
            copy(
                out=rounded.rearrange("p (c i t) -> p c t i", i=4, t=PACK),
                in_=y[:].rearrange("p t (c i) -> p c t i", i=4),
            )
            return rounded

        def quantise_scores(n, first, rounded):
            cols = slice(first, first + rounded.shape[1] // PACK)
            nc.vector.quantize_mx(out=y_codes[:, n, cols].bitcast(FP8X4), scales=y_plane[:, n, cols], in_=rounded)

        b = [ledger_features(2, c, 4 + c) for c in range(2)]
        banks0 = [bank(i, "y0_acc%d" % i, [P, 2, HALF]) for i in range(4)]
        banks2 = [bank(6 + n, "y2_acc%d" % n, [P, PACK, CHUNK]) for n in range(N_GROUPS)]

        def early_pass(g, side, groups):
            for n in groups:
                for i in (2 * n, 2 * n + 1):
                    add_pass(g, 0, banks0[i], n, 2 * (i % 2), (side,), False)
            for n in groups:
                add_pass(g, HALF, banks2[n], n, 0, (side,), False)

        early_pass(0, 1, range(N_GROUPS))
        early_pass(0, 0, range(N_GROUPS))
        early_pass(1, 0, [0])
        early_pass(1, 1, range(N_GROUPS))
        picked = at(DIFF + 4, "picked2", [P, PACK, HALF], F32)
        pick_all(2, 0, picked)
        diff = at(DIFF + 8, "diff2", [P, HALF * PACK], BF16)
        subtract(b, picked, diff)
        wo_q.append(quantise_weight("wo3", 6, staged[3], DIFF + 4))
        early_pass(1, 0, [1])
        b = ledger_features(2, 2, 5)
        banks3 = [bank(4, "y3_acc0", [P, PACK, CHUNK])]
        for g in (1, 0):
            add_pass(g, HALF + CHUNK, banks3[0], 0, 0, (1, 0), False, 1)
        wo_q.append(quantise_weight("wo4", 7, staged_last[0], DIFF + 4.5))
        signed = split_signs("d20", diff[:, 0 : 2 * BANK], LAST, LAST + 2, 2)
        wo_q.append(quantise_weight("wo5", 8, staged_last[1], DIFF + 5))
        quantise_signed(2, 0, signed)
        for i, acc in enumerate(banks0):
            add_pass(2, 0, acc, i // 2, 2 * (i % 2), (1, 0), True)
        y0 = [at(H_ROWS + 4 * n, "y0%d" % n, [P, PACK, HALF], F32) for n in range(N_GROUPS)]
        for n in range(N_GROUPS):
            scale_scores(n, 0, [banks0[2 * n + t // 2][:, t % 2, :] for t in range(PACK)], y0[n])
            store_scores(nc.sync, n, 0, y0[n])
        rounded_late = round_scores(nc.scalar.copy, at(H_ROWS + 18, "r01", [P, HALF * PACK], BF16)[:], y0[1])

        picked = at(LAND + 24, "picked3", [P, PACK, CHUNK], F32)
        pick_columns(2, HALF, range(PACK), picked)
        diff = at(W2_PLANE, "diff3", [P, 2 * BANK], BF16)
        subtract([b], picked, diff[:, 0:BANK])
        b = ledger_features(2, 3, 5)
        banks3.append(bank(0, "y3_acc1", [P, PACK, CHUNK]))
        for g in range(2):
            add_pass(g, HALF + CHUNK, banks3[1], 1, 0, (1, 0), False)
        signed = split_signs("d22", diff[:, 0:BANK], LAST + 4, LAST + 5, 1)
        quantise_signed(2, HALF, signed)
        for n in range(N_GROUPS):
            add_pass(2, HALF, banks2[n], n, 0, (1, 0), True)
        picked = at(W2_PLANE + 2, "picked4", [P, PACK, CHUNK], F32)
        pick_columns(2, HALF + CHUNK, range(PACK), picked)
        subtract([b], picked, diff[:, BANK : 2 * BANK])
        signed = split_signs("d23", diff[:, BANK : 2 * BANK], LAST + 6, LAST + 7, 1)
        quantise_signed(2, HALF + CHUNK, signed)
        for n in range(N_GROUPS):
            add_pass(2, HALF + CHUNK, banks3[n], n, 0, (1, 0), True)

        y2 = [at(H_ROWS + 8 + 2 * n, "y2%d" % n, [P, PACK, CHUNK], F32) for n in range(N_GROUPS)]
        y3 = [at(H_ROWS + 12 + 2 * n, "y3%d" % n, [P, PACK, CHUNK], F32) for n in range(N_GROUPS)]
        for n in range(N_GROUPS):
            scale_scores(n, HALF, [banks2[n][:, t, :] for t in range(PACK)], y2[n])
            store_scores(nc.sync, n, HALF, y2[n])
        for n in range(N_GROUPS):
            scale_scores(n, HALF + CHUNK, [banks3[n][:, t, :] for t in range(PACK)], y3[n])
            store_scores(nc.sync, n, HALF + CHUNK, y3[n])

        y_codes = at(LAST + 3, "y_codes", [P, N_GROUPS, M], U32)
        y_plane = at(H_ROWS + 28, "y_plane", [P, N_GROUPS, M], U8)
        out_words = out_1.rearrange("g p m t -> p g (m t)").bitcast(I32)
        rounded0 = [round_scores(nc.vector.tensor_copy, at(H_ROWS + 16, "r00", [P, HALF * PACK], BF16)[:], y0[0]), rounded_late]
        for n in range(N_GROUPS):
            quantise_scores(n, 0, rounded0[n])
        rounded = [at(H_ROWS + 20 + i, "r2", [P, BANK], BF16)[:] for i in range(4)]
        for n in range(N_GROUPS):
            round_scores(nc.vector.tensor_copy, rounded[n], y2[n])
        quantise_scores(0, HALF, rounded[0])
        round_scores(nc.vector.tensor_copy, rounded[2], y3[0])
        quantise_scores(1, HALF, rounded[1])
        done = M - CHUNK
        nc.sync.dma_start(out=out_words[:, :, 0:done], in_=y_codes[:, :, 0:done].bitcast(I32))
        round_scores(nc.vector.tensor_copy, rounded[3], y3[1])
        for n in range(N_GROUPS):
            quantise_scores(n, done, rounded[2 + n])
        nc.scalar.dma_start(out=out_words[:, :, done:M], in_=y_codes[:, :, done:M].bitcast(I32))
        for q in range(QUADRANTS):
            nc.scalar.dma_start(
                out=out_2[:, 4 * q : 4 * q + 4, :].rearrange("g r m -> r g m").bitcast(I32),
                in_=y_plane[32 * q : 32 * q + 4, :, :].bitcast(I32),
            )
